import numpy as np, ml_dtypes
CORES = [40,41,42,43,44,45,46,47]
N = 8
import mx_ref
BF = ml_dtypes.bfloat16
def entries(a):
    return np.ascontiguousarray(a.T).reshape(-1)
def table(e):
    return np.ascontiguousarray(np.reshape(e, (-1, 16)).T).astype(np.int32)
def gentries(a):
    return np.ascontiguousarray(a.reshape(8, 16, -1).transpose(0, 2, 1)).reshape(8, -1)
def gtable(e):
    e = np.asarray(e); return np.ascontiguousarray(e.reshape(8, -1, 16).transpose(0, 2, 1)).reshape(128, -1).astype(np.int32)
def gcols(t, e):
    v = np.concatenate([t.reshape(8, 16, -1, 4), np.zeros((8, 16, 1, 4), BF)], axis=2)
    return np.ascontiguousarray(np.stack([v[g][:, e[g]] for g in range(8)])).reshape(128, -1)
def tile(rs):
    return np.stack(rs, axis=2).reshape(128, -1).astype(BF)
def cut(t, i, w=512):
    return t[:, w * i:w * i + w]
def pick(q, e):
    c = np.concatenate([q[0].reshape(128, -1, 4), np.zeros((128, 1, 4), np.uint8)], axis=1); s = np.concatenate([q[1], np.ones((16, 1), np.uint8)], axis=1)
    return (np.ascontiguousarray(c[:, e].reshape(128, -1)), np.ascontiguousarray(s[:, e]))
def join(*qs):
    return (np.concatenate([q[0] for q in qs], axis=1), np.concatenate([q[1] for q in qs], axis=1))
def put(q, e, v):
    c, s = q[0].reshape(128, -1, 4).copy(), q[1].copy(); c[:, e] = v[0].reshape(128, -1, 4); s[:, e] = v[1]
    return (c.reshape(128, -1), s)
def pk(c, s):
    return (np.ascontiguousarray(c), mx_ref.live(s))
def emit(q):
    return q[0], q[1]
def packed(v, rng):
    q = [mx_ref.quantize(np.ascontiguousarray(v[r])) for r in range(N)]
    return np.stack([a for a, b in q]), np.stack([mx_ref.plane(b, rng) for a, b in q])
def values_of_codes():
    e, c = np.zeros((128, 128, 4), np.float32), np.zeros((128, 2, 4), np.uint8)
    e[np.arange(128), np.arange(128), 0] = 1
    c[:127, :, 0] = np.arange(256).reshape(2, 128).T[:127]
    return mx_ref.matmul(mx_ref.quantize(e.reshape(128, 512).astype(BF)), (c.reshape(128, 8), np.full((16, 2), 127, np.uint8))).T.reshape(-1).astype(np.float64)
CODE_VALUE, SCALE_VALUE = values_of_codes(), 2.0 ** (np.arange(256) - 127.0)
def decode(q):
    return (CODE_VALUE[q[0]].reshape(16, 8, -1, 4) * SCALE_VALUE[q[1]][:, None, :, None] + 0.0).reshape(128, -1).astype(np.float32)
def f(rng, *shape):
    return mx_ref.flush((rng.standard_normal(shape, dtype=np.float32) * np.exp2(rng.integers(-2, 3, shape[:-1] + (1,)))).astype(BF))
def wide(rng, *shape, cols=0):
    v = rng.standard_normal(shape, dtype=np.float32) * np.exp2(rng.integers(-12, 13, shape)).astype(np.float32)
    if cols: v *= np.repeat(np.exp2(rng.integers(-cols, cols + 1, shape[:-2] + (1, shape[-1] // 4))) * (rng.random(shape[:-2] + (1, shape[-1] // 4)) > 0.0625), 4, axis=-1).astype(np.float32)
    return mx_ref.flush(v.astype(BF))
H, A, C, L, M, R = 6, 64, 384, 288, 32, 3
WAY = [(-1, -1), (-1, 0), (-1, 1), (0, -1), (0, 1), (1, -1), (1, 0), (1, 1)]
ROW, COL = np.arange(C) // A, np.arange(C) % A
def seen(place, life):
    e = np.full((N, 8, C), -1)
    for g in range(8):
        k = place[:, g]
        lives = np.take_along_axis(life, k, axis=1)
        b = [np.where(lives, k + C * i, -1).reshape(N, H, A) for i in range(3)]
        field = np.concatenate([np.roll(b[0], 1, axis=0), b[1], np.roll(b[2], -1, axis=0)], axis=1)
        near = np.full((N, C), -1)
        for n in range(A + 2 * H, 0, -1):
            i, j = H + ROW + n * WAY[g][0], COL + n * WAY[g][1]
            ok = (i >= 0) & (i < 3 * H) & (j >= 0) & (j < A)
            z = field[:, np.where(ok, i, 0), np.where(ok, j, 0)]
            near = np.where(ok & (z >= 0), z, near)
        np.put_along_axis(e[:, g], k, near, axis=1)
    return e
def big(v):
    v = v.astype(np.float32)
    v[np.abs(v) < np.float32(2.0 ** -16)] = 0
    return v.astype(BF)
def numbers_of(rng):
    return {"x": big(f(rng, N, 128, 4 * C)), "u": np.array(f(rng, N, 128, 512)), "v": np.array(f(rng, N, 128, 512))}
def layers(rng, still=[]):
    w = np.array(f(rng, N, 128, 2048)).reshape(N, 8, 16, 4, 8, 16, 4)
    for i in still:
        w[:, :, i] = 0
        w[:, :, :, :, :, i] = 0
    return w
def weights(rng, w):
    c, p = packed(np.ascontiguousarray(w).reshape(N, 128, 2048), rng)
    return {"wc": c, "ws": p}
def signs(rng):
    return np.stack([rng.permutation(8) % 2 * 2.0 - 1.0 for r in range(N)])
def lives_of(rng):
    return np.stack([rng.permutation(C) < L for r in range(N)])
def seats_of(rng):
    return np.argsort(rng.random((N, 8, C)), axis=2)
def lists_of(place, life):
    return {"seat": np.stack([gtable(place[r]) for r in range(N)]), "alive": np.stack([table(life[r].astype(int)) for r in range(N)])}
def sit(e, squares, cells):
    others = e[~np.isin(e, cells)]
    e[squares] = cells
    e[np.setdiff1d(np.arange(C), squares)] = others
def marks(d, a, m):
    x, u = d["x"].reshape(N, 8, 16, C, 4), d["u"].reshape(N, 128, 128, 4)
    x[:, :, 0] = 0
    x[:, :, 0, :, 0] = a.astype(np.float32).astype(BF)
    x[:, 3, 8] = 0
    x[:, 3, 8, :, 0] = m.astype(np.float32).astype(BF)
    u[:, :, ::16] = 0
    u[:, :, 1] = 0
    for i in range(0, 128, 16): u[:, i, i, 0] = 1
    u[:, 56, 1, 0] = 1
def setup_inputs(rng):
    return {**numbers_of(rng), **weights(rng, layers(rng)), **lists_of(seats_of(rng), lives_of(rng))}
def setup_inputs_ties(rng):
    d = numbers_of(rng)
    k = np.array([1.5, 0.0, -1.25])
    a, m = k[rng.integers(0, 3, (N, 8, C))], k[rng.integers(0, 3, (N, C))]
    e = rng.permutation(N)
    a[e[0]], m[e[0]] = 1.5, 1.5
    marks(d, a, m)
    d["x"][e[1]] = 0
    return {**d, **weights(rng, layers(rng, [0, 8])), **lists_of(seats_of(rng), lives_of(rng))}
def setup_inputs_near(rng):
    d = numbers_of(rng)
    life, place = lives_of(rng), seats_of(rng)
    x = np.zeros((N, 8, 16, C, 4), np.float32)
    u = d["u"].reshape(N, 128, 128, 4)
    u[:, :, ::16] = 0
    u[:, :, 1] = 0
    w = layers(rng, [0, 8, 9, 10, 11, 12, 13, 14, 15])
    o, c = rng.permutation(N) % 4, signs(rng)
    j = np.arange(C)
    for r in range(N):
        place[r, 3] = j
        s = j // 2
        size = 1.0 if o[r] < 2 else 2.0 ** -4
        if o[r] < 2:
            x[r, :, 1:8] = d["x"][r].astype(np.float32).reshape(8, 16, C, 4)[:, 1:8]
            x[r, :, 0, :, 0] = c[r][:, None]
            for i in rng.permutation(8)[:4]: x[r, i, 0, rng.choice(np.flatnonzero(life[r])), 0] *= np.float32(2.0 ** 30)
        else: w[r] = 0
        if o[r] == 3:
            h = rng.permutation(C // 2) < L // 2
            life[r] = np.concatenate([h, h])
            s = j % (C // 2)
            x[r, :, 0, :, 0] = (8 + j // (C // 2)) * 2.0 ** -33
            n = np.flatnonzero(life[r])
            x[r, 3, 0, n[0], 0] = 2.0 ** -18
            who, left = n[1:], n[:-1]
            low = who[(who // A == left // A) & (who < C // 2)][-(M // 2):]
            fight = np.concatenate([n[1:2], low, low + C // 2])
            behind = rng.permutation(np.setdiff1d(n, np.concatenate([fight, left[np.isin(who, fight)]])))[:3 * M + 3]
            sit(place[r, 6], (np.arange(4)[:, None] * A + np.arange(M + 1)).reshape(-1), np.concatenate([fight, behind]))
            x[r, 6, 0, behind, 0] = -2.0 ** -18
        z = ((s[:, None] >> np.arange(8)) & 1) * np.exp2(np.arange(8) - 23.0) * size
        x[r, :, 8] = z[:, :4]
        x[r, :, 9] = z[:, 4:]
        x[r, :, 10:] = rng.integers(4, 8, (8, 6, C, 4)) * rng.choice([-1.0, 1.0], (8, 6, C, 4)) * 2.0 ** -20 * size
        k = 1.0 if o[r] == 0 else 2.0 ** -30
        for h in range(0, 128, 16):
            u[r, h, h, 0] = k
            u[r, h + 8:h + 10, h] = k
        u[r, 48, 1, 0] = k
        u[r, 56:58, 1] = k
    d["x"] = x.reshape(N, 128, 4 * C).astype(BF)
    return {**d, **weights(rng, w), **lists_of(place, life)}
def setup_inputs_huge(rng):
    d = numbers_of(rng)
    life, place = lives_of(rng), seats_of(rng)
    x = 2.0 ** 30 * (0.75 + 0.15 * rng.random((N, 128, C, 4)))
    a = 2.0 ** 30 * (1 - 0.1 * rng.random((N, 8, 16, 9, 4)))
    a[:, :, :, 8] *= -1
    a[:, [1, 6], :, 8] = 0
    c = signs(rng)
    for r in rng.permutation(N)[:N // 2]:
        x[r] *= (rng.permutation(C) % 2 * 2.0 - 1.0)[:, None]
        for g in range(8):
            a[r, np.arange(8) != g, :, g] = 0
            a[r, :, :, g] *= c[r, g]
        a[r, np.arange(8) != 3, :, 8] = 0
    u = d["u"].reshape(N, 128, 128, 4)
    a = a.reshape(N, 128, 9, 4).astype(np.float32).astype(BF)
    u[:, :, ::16] = a[:, :, :8]
    u[:, :, 1] = a[:, :, 8]
    corner = [0, 0, A - 1, 0, A - 1, C - A, C - A, C - 1]
    for g in range(8):
        k, way = rng.permutation(A), WAY[g][0] * WAY[g][1]
        q = rng.integers(H)
        for r in range(N):
            z = (ROW == q) & (COL > 0) & (COL < A - 1)
            if WAY[g][0]:
                n = k[(COL - way * (ROW + H * r)) % A]
                kept = (n + r) % 4
                z = (n < (C - L) // H) & ~((ROW == 0) & (kept % 2 == 1)) & ~((ROW == H - 1) & (kept >= 2))
            z[corner[g]] = False
            free = rng.permutation(np.flatnonzero(~z & (np.arange(C) != corner[g])))
            z[free[:C - L - int(np.sum(z))]] = True
            e = place[r, g]
            e[z] = rng.permutation(np.flatnonzero(~life[r]))
            e[~z] = rng.permutation(np.flatnonzero(life[r]))
            lone = np.flatnonzero(life[r])[0]
            e[np.flatnonzero(e == lone)[0]] = e[corner[g]]
            e[corner[g]] = lone
    w = np.zeros((N, 128, 4, 128, 4), np.float32)
    i = np.arange(128)
    for b in range(4): w[:, i, b, i, b] = -1
    d["x"] = x.astype(np.float32).reshape(N, 128, 4 * C).astype(BF)
    return {**d, **weights(rng, w.astype(BF)), **lists_of(place, life)}
def setup_inputs_deaths(rng):
    d = numbers_of(rng)
    life, place = lives_of(rng), seats_of(rng)
    a, m = rng.integers(8, 16, (N, 8, C)) * 0.125, np.zeros((N, C))
    o = rng.permutation(N) % 2
    for r in range(N):
        life[r] = np.roll(life[r], -int(np.flatnonzero(life[r])[0]))
        k = rng.permutation(np.flatnonzero(life[r])[1:])
        fight, behind = k[:M], k[M + 1:4 * M + 1]
        n = M - 1 - int(o[r])
        m[r, k[M]] = 1
        m[r, fight[:n]] = rng.integers(8, 16, n) * 0.125
        if o[r]:
            lone = fight[-1]
            sit(place[r, 0], [1, C - A], [lone, 0])
            for g, s in ((1, 0), (2, A - 1), (5, C - A), (6, C - A), (7, C - 1)): sit(place[r, g], [s], [lone])
            sit(place[r, 3], np.append(np.arange(M), A), np.concatenate([k[M:M + 1], fight]))
            sit(place[r, 4], np.arange(A - M, A), fight)
            for g in (3, 4): a[r, g, fight] *= -1
            a[r, 4, lone] = -4
        else:
            sit(place[r, 0], [C - A], [0])
            sit(place[r, 3], np.arange(M + 1), np.concatenate([k[M:M + 1], fight]))
            sit(place[r, 6], (np.arange(4)[:, None] * A + np.arange(M)).reshape(-1), np.concatenate([fight, behind]))
            a[r, 6, behind] *= -1
    marks(d, a, m)
    x, u = d["x"].reshape(N, 8, 16, C, 4), d["u"].reshape(N, 128, 128, 4)
    x[:, 0, 8] = 0
    x[:, 0, 8, 0, 0] = np.roll(o, -1).astype(np.float32).astype(BF)
    u[:, 8, 1, 0] = 1
    return {**d, **weights(rng, layers(rng, [0, 8])), **lists_of(place, life)}
def setup_inputs_spread(rng):
    d = setup_inputs(rng)
    d["x"] = big(wide(rng, N, 128, 4 * C, cols=6))
    return d
def check_inputs(d):
    b = []
    for k in ("x", "u", "v"):
        a = np.abs(d[k].astype(np.float32))
        if not (np.isfinite(a).all() and ((a == 0) | (a >= 2.0 ** -30) & (a <= 2.0 ** 30)).all()): b.append("a value of " + k)
    if ((d["wc"] & 0x7F) == 0x7F).any(): b.append("a code of wc that is no number")
    z = np.zeros((128, 4, 4), np.float32)
    z[:, 1] = 2.0 ** -30
    z[:, 2] = 2.0 ** 30
    c, s = emit(mx_ref.quantize(z.reshape(128, 16).astype(BF)))
    for r in range(N):
        p = mx_ref.live(d["ws"][r])
        if not ((p == s[0, 0]) | (p >= s[0, 1]) & (p <= s[0, 2])).all(): b.append("a scale of ws")
        if not (np.sort(gentries(d["seat"][r]), axis=1) == np.arange(C)).all(): b.append("seat: a permutation for every group")
        e = entries(d["alive"][r])
        if not ((e == 0) | (e == 1)).all(): b.append("alive: zeros and ones")
        if int(np.sum(e == 1)) != L: b.append("alive: the number of ones")
    return b
def reference(x, u, v, wc, ws, seat, alive):
    qu = [mx_ref.quantize(u[r]) for r in range(N)]
    lay = [pk(wc[r], ws[r]) for r in range(N)]
    place = np.stack([gentries(seat[r]) for r in range(N)])
    life = np.stack([entries(alive[r]) == 1 for r in range(N)])
    now = [x[r] for r in range(N)]
    for t in range(R):
        came = decode(join(*[mx_ref.quantize(now[r]) for r in range(N)])).astype(BF)
        e, after, now = seen(place, life), life.copy(), []
        for r in range(N):
            above, own, below = [cut(came, (r + i) % N, 4 * C) for i in (-1, 0, 1)]
            q = mx_ref.quantize(gcols(np.concatenate([above, own, below], axis=1), e[r]))
            p = mx_ref.matmul(qu[r], q) + np.float32(0.0)
            made = tile([mx_ref.matmul(pick(lay[r], np.arange(128 * b, 128 * b + 128)), q) * np.float32(0.015625) + own[:, b::4].astype(np.float32) for b in range(4)])
            now.append(np.where(np.repeat(life[r], 4), made, own))
            c = np.argsort(-np.where(life[r], p[1], -np.inf), kind="stable")[:M]
            k = e[r][:, c]
            mine = (k >= C) & (k < 2 * C)
            g = np.argmin(np.where(mine, p[::16][:, c], np.inf), axis=0)
            named = k[g, np.arange(M)][mine.any(axis=0)] - C
            after[r, named[~np.isin(named, c)]] = False
        life = after
    y, ol = np.zeros((N, 128, C), np.float32), np.zeros((N, 1, C), np.float32)
    oc, osc = np.zeros((N, 128, 4 * C), np.uint8), np.zeros((N, 16, C), np.uint8)
    for r in range(N):
        q = mx_ref.quantize(now[r])
        y[r] = mx_ref.matmul(mx_ref.quantize(v[r]), q)
        ol[r, 0] = life[r]
        oc[r], osc[r] = emit(q)
    return {"y": y, "ol": ol, "oc": oc, "osc": osc}

@@ -1,0 +1,432 @@
+from concourse.bass import DstId, RemoteDMATransfer
+from concourse.mybir import dt, AluOpType, ActivationFunctionType
+
+H, A, C, M, R = 6, 64, 384, 32, 3
+WAY = [(-1, -1), (-1, 0), (-1, 1), (0, -1), (0, 1), (1, -1), (1, 0), (1, 1)]
+UP, DOWN, OWN, W = 16, 80, 144, 528
+LL = 496
+K, BIG = 1024.0, 1e29
+X4, U8 = "float8_e4m3fn_x4", "uint8"
+
+
+def _sb(n, d):
+    return ("sbuf", [128, n], d)
+
+
+SCRATCH = {
+    "ps": ("psum", [128, 4096], "float32"),
+    "cnt": _sb(W, "float32"), "pint": _sb(8, "int32"), "pf": _sb(32, "float32"), "four": _sb(64, "float32"),
+    "tmp": _sb(256, "float32"), "blk": _sb(16, "float32"), "m16": _sb(LL, "float32"), "m4": _sb(64, "float32"),
+    "q16u": _sb(32, "uint16"), "posi": _sb(24, "int32"), "posu": _sb(24, "uint16"), "posf": _sb(C, "float32"),
+    "tri": _sb(128, "float32"), "strip": _sb(528, "bfloat16"), "wts": _sb(1032, "bfloat16"),
+    "eq": _sb(512, X4), "es": _sb(512, U8), "kq": _sb(384, X4), "ks": _sb(384, U8),
+    "lin": _sb(48, "int32"), "linu": _sb(48, "uint16"), "seatf": _sb(C, "float32"), "idl": _sb(LL, "float32"),
+    "ext": _sb(LL, "float32"), "lu": _sb(32, "uint16"), "pc": _sb(C, "float32"), "pu": _sb(24, "uint16"),
+    "life": _sb(W, "float32"), "la": _sb(LL, "float32"), "lb": _sb(LL, "float32"),
+    "fw": _sb(512, "float32"), "bw": _sb(512, "float32"), "c64": _sb(64, "float32"), "cu": _sb(16, "uint16"),
+    "sees": _sb(C, "float32"), "su": _sb(24, "uint16"), "back": _sb(C, "float32"), "bu": _sb(24, "uint16"),
+    "ext2": _sb(C, "float32"), "far": _sb(C, "float32"), "pen": _sb(C, "float32"), "lt": _sb(4, "float32"),
+    "pt": _sb(4, "float32"), "sc": _sb(4, "float32"), "dl": _sb(4, "float32"), "thr": _sb(C, "float32"),
+    "xs": _sb(C, "float32"),
+    "xb": _sb(4 * W, "bfloat16"), "xq": _sb(C, X4), "xp": _sb(C, U8), "tp": _sb(4 * W, "bfloat16"),
+    "comp": _sb(512, "bfloat16"), "z": _sb(4 * C, "bfloat16"), "zq": _sb(C, X4), "zp": _sb(C, U8),
+    "cm": _sb(4 * C, "bfloat16"), "cmq": _sb(C, X4), "cmp": _sb(C, U8),
+    "win": _sb(W, "bfloat16"), "kt": _sb(2 * C, "bfloat16"), "ktq": _sb(C // 2, X4), "ktp": _sb(C // 2, U8),
+    "ub": _sb(512, "bfloat16"), "uq": _sb(128, X4), "up": _sb(128, U8), "uu": _sb(24, "uint16"),
+    "uq2": _sb(C, X4), "up2": _sb(C, U8), "vb": _sb(512, "bfloat16"), "vq": _sb(128, X4), "vp": _sb(128, U8),
+    "wq": _sb(512, X4), "wp": _sb(512, U8), "yb": _sb(C, "float32"),
+}
+for _t in range(R):
+    SCRATCH["sq%d" % _t] = _sb(128, X4)
+    SCRATCH["sp%d" % _t] = _sb(128, U8)
+    SCRATCH["lq%d" % _t] = _sb(128, X4)
+    SCRATCH["lp%d" % _t] = _sb(128, U8)
+
+SEMAPHORES = ["v", "s", "t", "g", "sent", "arr0", "arr1", "arr2"] + ["d%d" % i for i in range(16)]
+
+Op, Fn = AluOpType, ActivationFunctionType
+
+
+def rank_program(g, core, T, topo):
+    rank = T.rank_of(core)
+    if rank is None:
+        return
+    n = len(T.cores)
+    above, below = T.cores[(rank - 1) % n], T.cores[(rank + 1) % n]
+    V, S, PE = g.vector, g.scalar, g.tensor
+    queue = {"v": V, "s": S, "t": PE, "g": g, "y": g.sync}
+    count = {}
+    known = {q: {} for q in queue}
+    writer, readers = {}, {}
+
+    def need(q, tok):
+        sem, val, seen = tok[0], tok[1], tok[2]
+        if known[q].get(sem, 0) >= val:
+            return
+        queue[q].wait_ge(T.sem[sem], val)
+        known[q][sem] = val
+        for k in seen:
+            known[q][k] = max(known[q].get(k, 0), seen[k])
+
+    def order(q, r, w, add):
+        toks = []
+        for k in r:
+            toks += writer.get(k, [])
+            if k[0] == "P":
+                toks += [t for t in readers.get(k, []) if t[3] != q]
+        for k in w:
+            if k not in add:
+                toks += writer.get(k, [])
+            toks += readers.get(k, [])
+        for tok in sorted(toks, key=lambda t: -t[1]):
+            need(q, tok)
+
+    def note(tok, r, w):
+        for k in r:
+            readers.setdefault(k, []).append(tok)
+        for k in w:
+            writer[k] = [tok]
+            readers[k] = []
+
+    def op(q, call, r, w, add=()):
+        order(q, r, w, add)
+        count[q] = count.get(q, 0) + 1
+        call().then_inc(T.sem[q], 1)
+        note((q, count[q], dict(known[q]), q), r, w)
+
+    def dma(parts, r, w):
+        sem = "d%d" % len([k for k in count if k[0] == "d"])
+        for q, out, src in parts:
+            order(q, r, w, ())
+        for q, out, src in parts:
+            queue[q].dma_start(out, src).then_inc(T.sem[sem], 16)
+        count[sem] = 16 * len(parts)
+        note((sem, count[sem], dict(known[parts[0][0]]), "dma"), r, w)
+
+    def ts(out, a, s1, s2, o1, o2, r, w):
+        if o2 is None:
+            op("v", lambda: V.tensor_scalar(out, a, s1, None, o1), r, w)
+        else:
+            op("v", lambda: V.tensor_scalar(out, a, s1, s2, o1, o2), r, w)
+
+    def tt(out, a, b, o, r, w):
+        op("v", lambda: V.tensor_tensor(out, a, b, o), r, w)
+
+    def cp(out, a, r, w):
+        op("v", lambda: V.tensor_copy(out, a), r, w)
+
+    def fill(out, c, w):
+        op("v", lambda: V.memset(out, c), [], w)
+
+    def scan(out, a, b, o0, o1, r, w):
+        op("v", lambda: V.tensor_tensor_scan(out, a, b, 0.0, o0, o1), r, w)
+
+    def quant(q, p, a, r, w):
+        op("v", lambda: V.quantize_mx(q, p, a), r, w)
+
+    def act(out, a, f, r, w, bias=None, scale=None):
+        more = {k: x for k, x in (("bias", bias), ("scale", scale)) if x is not None}
+        op("s", lambda: S.activation(out, a, f, **more), r, w)
+
+    def iota(out, pattern, base, cm, r, w, small=False):
+        if small:
+            op("g", lambda: g.iota(out, pattern, base, cm, allow_small_or_imprecise_dtypes=True), r, w)
+        else:
+            op("g", lambda: g.iota(out, pattern, base, cm), r, w)
+
+    def bank(b, lo, hi):
+        return T.ps[:, 512 * b + lo:512 * b + hi]
+
+    def mm(b, cols, lq, lp, rq, rp, r, start=True, stop=True):
+        k = "P%d" % b
+        op("t", lambda: PE.matmul_mx(bank(b, 0, cols), lq, lp, rq, rp, start, stop), r, [k], add=() if start else (k,))
+
+    def part(q, p, b):
+        return q[:, 128 * b:128 * b + 128], p[:, 128 * b:128 * b + 128]
+
+    names = ["p", "q16", "q12", "q3", "q7", "offk", "c4a", "c4", "z0", "zp", "thv", "g16", "ca", "cb", "cc", "c3", "eb",
+             "sg", "sg32", "pens", "w0", "w1"]
+
+    def col(name):
+        i = names.index(name)
+        return T.pf[:, i:i + 1]
+
+    def small(name, src, f, bias, scale):
+        r = [k if k not in names[:5] else "pf" for k in (src, bias, scale) if isinstance(k, str)]
+        act(col(name), col(src), f, r, [name], bias=col(bias) if isinstance(bias, str) else bias,
+            scale=col(scale) if isinstance(scale, str) else scale)
+
+    def hold(buf, src, cols, r, key):
+        scan(buf[:, 0:cols], T.m16[:, 0:cols], src, Op.add, Op.max, r + ["m16"], [key])
+
+    def take(out, buf, cols, key, w):
+        ts(out, buf[:, 15:cols:16], col("offk"), None, Op.subtract, None, [key, "offk"], w)
+
+    u32 = dt.uint32
+    xall = ["x0", "x1", "x2", "x3"]
+    dma([("y", T.lin[:, 0:24], T.seat[:])], [], ["seat"])
+    dma([("y" if i < 4 else "s", T.lin[16 * i:16 * i + 16, 24:48], T.alive[:]) for i in range(8)], [], ["alive"])
+    dma([("y", T.xb[:, 4 * OWN:4 * W], T.x[:])], [], xall)
+    dma([("y", T.ub[:], T.u[:])], [], ["ub"])
+    dma([("y", T.wq[:].bitcast(dt.uint8), T.wc[:]), ("y", T.wp[:], T.ws[:])], [], ["w"])
+    dma([("y", T.vb[:], T.v[:])], [], ["vb"])
+
+    iota(T.pint[:, 0:1], [[0, 1]], 0, 1, [], ["pi"])
+    iota(T.cnt[:, 0:OWN], [[1, OWN]], 0, 0, [], ["cnt0"], True)
+    for odd in (1, 0):
+        for a in range(4):
+            di, dj = WAY[2 * a + odd]
+            if di == 0:
+                al, be, ga = -dj, 65, (1 if dj < 0 else 64)
+            else:
+                al = -7 if dj > 0 else 7
+                bi, ga = (1, 1) if dj == 0 else (-6, 36 + (7 * 63 if dj > 0 else 0))
+                be, ga = (bi, ga) if di < 0 else (-bi, ga + 5 * bi)
+            iota(T.posi[32 * a:32 * a + 16 + 16 * odd, :], [[be, 6], [16 * al, 4]], ga - 16 * al * odd, al, ["pi", "cnt0"],
+                 ["posi%d" % a])
+    posi_all = ["posi0", "posi1", "posi2", "posi3"]
+    iota(T.four[:], [[0, 16], [4, 4]], 0, 0, posi_all, ["four"], True)
+    iota(T.life[:, 0:OWN], [[0, OWN]], 1, 0, [], ["life0"], True)
+    iota(T.xb[:, 0:4 * OWN], [[0, 4 * OWN]], 0, 0, [], ["xz"], True)
+    iota(T.comp[:, 256:512], [[0, 256]], 0, 0, [], ["compz"], True)
+    op("g", lambda: g.affine_select(T.tri[:], T.life[:, 0:128], [[1, 128]], Op.is_gt, 0.0, 0, -1), ["life0"], ["tri"])
+    for b in range(4):
+        iota(T.tp[:, W * b:W * b + UP], [[0, UP]], 0, 0, [], ["tz%d" % b], True)
+    iota(T.win[:, 0:OWN], [[0, OWN]], 0, 0, [], ["winz"], True)
+
+    fill(T.strip[:], 0.0, ["strip"])
+    for i, m in enumerate((15, 12, 3, 7)):
+        ts(T.pint[:, 1 + i:2 + i], T.pint[:, 0:1], m, None, Op.bitwise_and, None, ["pi"], ["pi%d" % i])
+    eb = names.index("eb")
+    fill(T.pf[0:64, eb:eb + 1], float(UP), ["eb0"])
+    cp(T.pf[:, 0:5], T.pint[:, 0:5], ["pi", "pi0", "pi1", "pi2", "pi3"], ["pf"])
+    fill(T.pf[64:128, eb:eb + 1], float(DOWN), ["eb1"])
+    for i in range(3):
+        act(T.cnt[:, OWN + 128 * i:OWN + 128 * i + 128], T.cnt[:, 0:128], Fn.Identity, ["cnt0"], ["cnt%d" % (i + 1)],
+            bias=float(OWN + 128 * i))
+    cnt_all = ["cnt0", "cnt1", "cnt2", "cnt3"]
+    small("g16", "q16", Fn.Identity, "p", -1.0)
+    small("ca", "g16", Fn.Abs, -56.0, 1.0)
+    small("cb", "ca", Fn.Square, -2.5, 0.0625)
+    small("cc", "cb", Fn.Square, 0.0, 1.0)
+    act(T.idl[:], T.cnt[:, 0:LL], Fn.Copy, cnt_all, ["idl"], scale=0.0)
+    ts(T.strip[:, 3:515:4], T.cnt[:, 0:128], col("p"), 64.0, Op.is_equal, Op.mult, ["cnt0", "pf"], ["strip"])
+    ts(T.q16u[:], T.cnt[:, 0:32], 0.0, col("q16"), Op.mult, Op.add, ["cnt0", "pf"], ["q16u"])
+    ts(T.blk[:], T.cnt[:, 0:16], col("q16"), -BIG, Op.is_equal, Op.mult, ["cnt0", "pf"], ["blk"])
+    for b in range(4):
+        quant(*part(T.eq, T.es, b), T.strip[:, 3 - b:515 - b], ["strip"], ["e%d" % b])
+    ts(col("c3"), col("cc"), 6.0, None, Op.mult, None, ["cc"], ["c3"])
+    cp(T.linu[:, 0:24], T.lin[:, 0:24], ["seat"], ["seatu"])
+    seatu, aliveu = T.linu[:, 0:24], T.linu[:, 24:48]
+    act(T.seatf[:], T.cnt[:, OWN:W].indirect(seatu), Fn.Copy, cnt_all + ["seatu"], ["seatf"])
+    ts(T.tmp[:, 0:69], T.cnt[:, 0:69], col("c3"), None, Op.subtract, None, ["cnt0", "c3"], ["tmp0"])
+    cp(T.posu[:], T.posi[:], posi_all, ["posu"])
+    ts(T.tmp[:, 72:141], T.tmp[:, 0:69], 0.0, None, Op.is_ge, None, ["tmp0"], ["tmp1"])
+    ts(T.tmp[:, 144:213], T.tmp[:, 0:69], col("eb"), float(OWN - 1), Op.add, Op.min, ["tmp0", "eb0", "eb1"], ["tmp2"])
+    cp(T.linu[:, 24:48], T.lin[:, 24:48], ["alive"], ["aliveu"])
+    tt(T.idl[:, 0:483:7], T.tmp[:, 72:141], T.tmp[:, 144:213], Op.mult, ["tmp1", "tmp2"], ["idl"])
+    ts(T.tmp[:, 0:64], T.four[:], col("q12"), -BIG, Op.is_equal, Op.mult, ["four", "pf"], ["tmp0"])
+    act(T.m16[:], T.blk[:].indirect(T.q16u[:, 0:31]), Fn.Identity, ["blk", "q16u"], ["m16"], bias=K)
+    small("offk", "q16", Fn.Identity, 15 * K, -K)
+    act(T.life[:, OWN:W], T.cnt[:, 0:8].indirect(aliveu), Fn.Copy, ["cnt0", "aliveu"], ["life"])
+    act(T.m4[:], T.tmp[:, 0:64], Fn.Identity, ["tmp0"], ["m4"], bias=K)
+    small("c4a", "q3", Fn.Identity, -12 * K, 1.0)
+    small("z0", "q16", Fn.Relu, 1.0, -1.0)
+    small("c4", "q12", Fn.Identity, "c4a", K)
+    cp(T.idl[:].indirect(T.posu[:]), T.seatf[:], ["seatf", "posu"], ["idl"])
+    hold(T.ext, T.idl[:], LL, ["idl"], "ext")
+    take(T.lu[:, 0:31], T.ext, LL, "ext", ["lu"])
+    lines = T.lu[:, 0:31]
+
+    def quant_x():
+        quant(T.xq[:], T.xp[:], T.xb[:, 4 * OWN:4 * W], xall, ["xq"])
+
+    def unpack_own(stop):
+        for b in range(4):
+            mm(b, C, *part(T.eq, T.es, b), T.xq[:], T.xp[:], ["e%d" % b, "xq"], True, stop)
+
+    def later_constants():
+        act(T.posf[:], T.cnt[:].indirect(T.posu[:]), Fn.Copy, cnt_all + ["posu"], ["posf"])
+        small("sg", "q16", Fn.Sign, "p", -17.0)
+        small("w0", "z0", Fn.Identity, 0.0, 0.0625)
+        small("w1", "z0", Fn.Identity, 0.0078125, -0.0078125)
+        small("zp", "p", Fn.Identity, 0.0, "z0")
+        small("sg32", "sg", Fn.Identity, 0.0, 32.0)
+        small("pens", "sg", Fn.Identity, 0.0, BIG / 256)
+        small("thv", "zp", Fn.Identity, 31.5, -2.0)
+        act(T.fw[:, 0:1], T.cnt[:, 0:1], Fn.Copy, ["cnt0"], ["fwz"])
+        for b in range(4):
+            act(T.wts[:, b:512:4], T.cnt[:, 0:128], Fn.Identity, ["cnt0"], ["wv%d" % b], bias=1.0 if b < 3 else 0.0, scale=0.0)
+
+    def backward():
+        scan(T.bw[:, LL + 6:6:-1], T.la[:, LL - 1::-1], T.lb[:, LL - 1::-1], Op.mult, Op.add, ["la", "lb"], ["bw"])
+
+    def seen_by():
+        act(T.back[:], T.bw[:, 8:LL + 7].indirect(T.pu[:]), Fn.Copy, ["bw", "pu"], ["back"])
+
+    def arrived(b, q):
+        out = T.tp[:, W * b + UP:W * b + OWN]
+        if q == "v":
+            ts(out, bank(4 + b, 0, 128), 0.015625, None, Op.mult, None, ["P%d" % (4 + b)], ["ta%d" % b])
+        else:
+            act(out, bank(4 + b, 0, 128), Fn.Copy, ["P%d" % (4 + b)], ["ta%d" % b], scale=0.015625)
+
+    def gather_z(b, q, lo, hi):
+        src = T.tp[:, W * b:W * b + W].indirect(T.su[:, lo // 16:hi // 16])
+        r, w = ["tz%d" % b, "ta%d" % b, "to%d" % b, "su"], ["z%d%d" % (b, h) for h in range(lo // 192, hi // 192)]
+        if q == "v":
+            cp(T.z[:, 4 * lo + b:4 * hi:4], src, r, w)
+        else:
+            act(T.z[:, 4 * lo + b:4 * hi:4], src, Fn.Copy, r, w)
+
+    for t in range(R):
+        first, last = t == 0, t == R - 1
+        tt(T.lb[:], T.life[:].indirect(lines), T.idl[:], Op.mult, ["life0", "life", "lu", "idl"], ["lb"])
+        act(T.la[:], T.life[:].indirect(lines), Fn.Identity, ["life0", "life", "lu"], ["la"], bias=1.0, scale=-1.0)
+        if first:
+            later_constants()
+        dma([("y", T.lt[:, k:k + 1], T.life[0:1, OWN + 128 * k:OWN + 128 * k + 128]) for k in range(3)], ["life"], ["lt"])
+        scan(T.fw[:, 1:LL + 1], T.la[:], T.lb[:], Op.mult, Op.add, ["la", "lb"], ["fw"])
+        scan(T.c64[:], T.m4[:], T.fw[:, 7:455:7], Op.add, Op.max, ["fw", "m4"], ["c64"])
+        ts(T.cu[:], T.c64[:, 3:64:4], 4.0, col("c4"), Op.mult, Op.add, ["c64", "c4"], ["cu"])
+        cp(T.comp[:, 0:256], T.xb[:].indirect(T.cu[:]), ["cu", "xz"] + xall, ["comp"])
+        sq, sp, lq, lp = T["sq%d" % t], T["sp%d" % t], T["lq%d" % t], T["lp%d" % t]
+        quant(sq[:], sp[:], T.comp[:], ["comp", "compz"], ["sq%d" % t])
+        order("g", ["sq%d" % t], [], ())
+        for src, dst, codes in ((sq, lq, True), (sp, lp, False)):
+            moves = []
+            for i, to in enumerate((below, above)):
+                eng = topo.engines(core, to)
+                half = eng[i * len(eng) // 2:(i + 1) * len(eng) // 2]
+                rid, pid = topo.addr(to)[:2]
+                a, b = src[:, 0:64], dst[:, 64 * i:64 * i + 64]
+                if codes:
+                    a, b = a.bitcast(dt.uint8), b.bitcast(dt.uint8)
+                moves.append(RemoteDMATransfer(dst_ids=[DstId(rid=rid, pnc=pid)], dma_engine_mask=sum(1 << e for e in half),
+                                               remote_sem=T.sem["arr%d" % t], src=a, dst=b))
+                count["sent"] = count.get("sent", 0) + len(half)
+            g.remote_dma_fused(moves, local_sem=T.sem.sent)
+        landed = len(topo.engines(above, core)) + len(topo.engines(below, core))
+        writer["land"] = [("arr%d" % t, landed, {}, "far")]
+        readers["land"] = []
+
+        if first:
+            quant_x()
+            unpack_own(True)
+        for b in range(4):
+            act(T.tp[:, W * b + OWN:W * b + W], bank(b, 0, C), Fn.Copy, ["P%d" % b], ["to%d" % b], scale=0.015625)
+        for b in range(4):
+            mm(4 + b, 128, *part(T.eq, T.es, b), lq[:], lp[:], ["e%d" % b, "land"])
+        unpack_own(False)
+        if first:
+            cp(T.pc[:].indirect(seatu), T.posf[:], ["posf", "seatu"], ["pc"])
+            hold(T.ext, T.pc[:], C, ["pc"], "ext")
+            quant(T.uq[:], T.up[:], T.ub[:], ["ub"], ["uq"])
+            take(T.pu[:], T.ext, C, "ext", ["pu"])
+            ts(T.uu[:, 8:16], T.cnt[:, 0:8], col("q7"), 16.0, Op.max, Op.mult, ["cnt0", "pf"], ["uu1"])
+            ts(T.uu[:, 16:24], T.cnt[:, 0:8], col("q7"), 16.0, Op.min, Op.mult, ["cnt0", "pf"], ["uu2"])
+            fill(T.uu[:, 0:8], 1, ["uu0"])
+            act(T.up2[:], T.up[:].indirect(T.uu[:]), Fn.Copy, ["uq", "uu0", "uu1", "uu2"], ["u2b"])
+        if last:
+            backward()
+            seen_by()
+        tt(T.sees[:], T.fw[:, 0:LL + 1].indirect(T.pu[:]), T.life[:, OWN:W], Op.mult, ["fw", "fwz", "pu", "life"], ["sees"])
+        if t == 1:
+            backward()
+        hold(T.ext, T.sees[:], C, ["sees"], "ext")
+        if t == 1:
+            quant(T.vq[:], T.vp[:], T.vb[:], ["vb"], ["vq"])
+        if last:
+            hold(T.ext2, T.back[:], C, ["back"], "ext2")
+        take(T.su[:], T.ext, C, "ext", ["su"])
+        if first:
+            cp(T.uq2[:].bitcast(u32), T.uq[:].bitcast(u32).indirect(T.uu[:]), ["uq", "uu0", "uu1", "uu2"], ["u2a"])
+            for b in range(4):
+                arrived(b, "s")
+            for b, q, lo, hi in ((1, "s", 0, C), (0, "v", 0, C), (3, "s", 0, C), (2, "v", 0, C // 2), (2, "s", C // 2, C)):
+                gather_z(b, q, lo, hi)
+            act(T.pt[:, 0:3], T.lt[:, 0:3], Fn.Identity, ["lt"], ["pt"], bias=-BIG, scale=BIG)
+            act(T.far[:], T.sees[:], Fn.Relu, ["sees"], ["far"], bias=float(OWN), scale=-1.0)
+        else:
+            act(T.pt[:, 0:3], T.lt[:, 0:3], Fn.Identity, ["lt"], ["pt"], bias=-BIG, scale=BIG)
+            for b in range(4):
+                arrived(b, "vs"[b % 2])
+            for b in range(4):
+                gather_z(b, "vs"[b % 2], 0, C)
+            if not last:
+                seen_by()
+        quant(T.zq[:], T.zp[:], T.z[:], ["z%d%d" % (b, h) for b in range(4) for h in range(2)], ["zq"])
+        if first:
+            backward()
+        else:
+            ts(T.pen[:], T.sees[:], OWN - 0.5, col("pens"), Op.is_lt, Op.mult, ["sees", "pens"], ["pen"])
+        uk = ["u2a", "u2b", "zq"]
+        for k in range(3):
+            mm(4 + k, 128, *part(T.zq, T.zp, k), *part(T.uq2, T.up2, 0), uk)
+        mm(7, C, *part(T.uq2, T.up2, 0), T.zq[:], T.zp[:], uk)
+        tt(T.sc[:, 0:3], T.ps[:, 2048:3584:512], T.pt[:, 0:3], Op.add, ["P4", "P5", "P6", "pt"], ["sc"])
+
+        def layer(b):
+            mm(b, C, *part(T.wq, T.wp, b), T.zq[:], T.zp[:], ["w", "zq"], False, True)
+
+        layer(0)
+        mm(4, C, *part(T.uq2, T.up2, 1), T.zq[:], T.zp[:], uk)
+        mm(5, C, *part(T.uq2, T.up2, 2), T.zq[:], T.zp[:], uk)
+        for b in (1, 2, 3):
+            layer(b)
+        if first:
+            act(T.pen[:], T.far[:], Fn.Identity, ["far", "pens"], ["pen"], scale=col("pens"))
+        act(T.dl[:, 0:3], T.sc[:, 0:3], Fn.Abs, ["sc"], ["dl"], bias=2.0 ** -122, scale=1.25 * 2.0 ** -24)
+        for k in range(3):
+            act(T.thr[:, 128 * k:128 * k + 128], T.tri[:], Fn.Identity, ["tri", "sc", "dl"], ["thr%d" % k],
+                bias=T.sc[:, k:k + 1], scale=T.dl[:, k:k + 1])
+        if first:
+            seen_by()
+            for b in range(4):
+                act(T.wts[:, 512 + b:1026:4], T.cnt[:, 0:129 if b < 2 else 128], Fn.Identity, ["cnt0", "w0", "w1"],
+                    ["wk%d" % b], bias=col("w%d" % (b - 2)) if b >= 2 else 0.0, scale=0.0)
+        for k, lo, hi, slot, o in ((0, 128, 384, 0, Op.is_le), (2, 0, 256, 1, Op.is_lt), (1, 0, 128, 0, Op.is_lt),
+                                   (1, 256, 384, 1, Op.is_le)):
+            ts(T.cm[:, 4 * lo + slot:4 * hi:4], bank(7, lo, hi), T.sc[:, k:k + 1], None, o, None, ["P7", "sc"],
+               ["cm%d%d" % (k, slot)])
+        tt(T.xs[:], bank(4, 0, C), T.pen[:], Op.add, ["P4", "pen"], ["xs"])
+        tt(T.cm[:, 2:4 * C:4], bank(7, 0, C), T.thr[:], Op.is_lt, ["P7", "thr0", "thr1", "thr2"], ["cmd"])
+        tt(T.cm[:, 3:4 * C:4], bank(5, 0, C), T.xs[:], Op.is_gt, ["P5", "xs"], ["cma"])
+        if first:
+            ts(T.wts[:, 3:512:64], T.cnt[:, 0:8], col("q16"), col("sg32"), Op.is_equal, Op.mult, ["cnt0", "pf", "sg32"], ["wv3"])
+            quant(*part(T.kq, T.ks, 0), T.wts[:, 0:512], ["wv0", "wv1", "wv2", "wv3"], ["kq"])
+        quant(T.cmq[:], T.cmp[:], T.cm[:], ["cm00", "cm21", "cm10", "cm11", "cmd", "cma"], ["cmq"])
+        mm(6, C, *part(T.kq, T.ks, 0), T.cmq[:], T.cmp[:], ["kq", "cmq"])
+        if not last:
+            hold(T.ext2, T.back[:], C, ["back"], "ext2")
+        for b in range(4):
+            act(T.xb[:, 4 * OWN + b:4 * W:4], bank(b, 0, C), Fn.Copy, ["P%d" % b], ["x%d" % b], scale=0.015625)
+        if last:
+            quant_x()
+            mm(0, C, T.vq[:], T.vp[:], T.xq[:], T.xp[:], ["vq", "xq"])
+            dma([("y", T.oc[:], T.xq[:].bitcast(dt.uint8))]
+                + [("y", T.osc[4 * k:4 * k + 4, :], T.xp[32 * k:32 * k + 4, :]) for k in range(4)], ["xq"], [])
+        ts(T.win[:, OWN:W], bank(6, 0, C), col("thv"), None, Op.is_lt, None, ["P6", "thv"], ["win"])
+        take(T.bu[:], T.ext2, C, "ext2", ["bu"])
+        if last:
+            act(T.yb[:], bank(0, 0, C), Fn.Copy, ["P0"], ["yb"])
+            dma([("y", T.y[:], T.yb[:])], ["yb"], [])
+        act(T.kt[:, 1:2 * C:2], T.win[:, OWN:W], Fn.Identity, ["win"], ["kt1"], bias=1.0, scale=-1.0)
+        cp(T.kt[:, 0:2 * C:2], T.win[:].indirect(T.bu[:]), ["win", "winz", "bu"], ["kt0"])
+        if first:
+            for h in range(2):
+                quant(*part(T.kq, T.ks, 1 + h), T.wts[:, 514 - 2 * h:1026 - 2 * h], ["wk0", "wk1", "wk2", "wk3"], ["kq%d" % h])
+        quant(T.ktq[:], T.ktp[:], T.kt[:], ["kt0", "kt1"], ["ktq"])
+        for h in range(2):
+            mm(7 - h, C // 2, *part(T.kq, T.ks, 1 + h), T.ktq[:], T.ktp[:], ["kq%d" % h, "ktq"])
+        if not last:
+            quant_x()
+            unpack_own(True)
+        order("v", ["life"], ["life"], ())
+        for h in range(2):
+            tt(T.life[:, OWN + h:W:2], bank(7 - h, 0, C // 2), T.life[:, OWN + h:W:2], Op.is_lt, ["P%d" % (7 - h)], ["lh%d" % h])
+        writer["life"] = writer["lh0"] + writer["lh1"]
+        readers["life"] = []
+    dma([("y", T.ol[:], T.life[0:1, OWN:W])], ["life"], [])
+    for sem in count:
+        need("g", (sem, count[sem], {}))

@@ -3,9 +3,10 @@ from concourse.mybir import dt, AluOpType, ActivationFunctionType
 
 H, A, C, M, R = 6, 64, 384, 32, 3
 WAY = [(-1, -1), (-1, 0), (-1, 1), (0, -1), (0, 1), (1, -1), (1, 0), (1, 1)]
-UP, DOWN, OWN, W = 16, 80, 144, 528
-LL = 496
-K, BIG = 1024.0, 1e29
+UP, DOWN, GAP, OWN, W = 16, 80, 144, 160, 544
+XO = 4
+LL, LS = 496, 484
+K, BIG, EPS = 1024.0, 1e29, 2.0 ** -36
 X4, U8 = "float8_e4m3fn_x4", "uint8"
 
 
@@ -15,23 +16,26 @@ def _sb(n, d):
 
 SCRATCH = {
     "ps": ("psum", [128, 4096], "float32"),
-    "cnt": _sb(W, "float32"), "pint": _sb(8, "int32"), "pf": _sb(32, "float32"), "four": _sb(64, "float32"),
-    "tmp": _sb(256, "float32"), "blk": _sb(16, "float32"), "m16": _sb(LL, "float32"), "m4": _sb(64, "float32"),
-    "q16u": _sb(32, "uint16"), "posi": _sb(24, "int32"), "posu": _sb(24, "uint16"), "posf": _sb(C, "float32"),
+    "cnt": _sb(W, "float32"), "pint": _sb(8, "int32"), "pf": _sb(32, "float32"), "ones": _sb(LL, "float32"),
+    "two": _sb(8, "float32"),
+    "tmp": _sb(256, "float32"), "blk": _sb(32, "float32"), "m16": _sb(C, "float32"), "m4": _sb(C, "float32"),
+    "q16u": _sb(24, "uint16"), "posi": _sb(48, "float32"), "posu": _sb(24, "uint16"), "posf": _sb(C, "float32"),
     "tri": _sb(128, "float32"), "strip": _sb(528, "bfloat16"), "wts": _sb(1032, "bfloat16"),
     "eq": _sb(512, X4), "es": _sb(512, U8), "kq": _sb(384, X4), "ks": _sb(384, U8),
-    "lin": _sb(48, "int32"), "linu": _sb(48, "uint16"), "seatf": _sb(C, "float32"), "idl": _sb(LL, "float32"),
-    "ext": _sb(LL, "float32"), "lu": _sb(32, "uint16"), "pc": _sb(C, "float32"), "pu": _sb(24, "uint16"),
-    "life": _sb(W, "float32"), "la": _sb(LL, "float32"), "lb": _sb(LL, "float32"),
+    "lin": _sb(48, "int32"), "seatu": _sb(24, "uint16"), "aliveu": _sb(24, "uint16"), "jw": _sb(24, "float32"),
+    "ni": _sb(C, "float32"), "nis": _sb(C, "float32"),
+    "d0": _sb(LL, "float32"), "d1": _sb(LL, "float32"), "idl": _sb(LL, "float32"),
+    "ext": _sb(C, "float32"), "ext3": _sb(LL, "float32"), "lu": _sb(32, "uint16"), "pc": _sb(C, "float32"), "pu": _sb(24, "uint16"),
+    "dead": _sb(W, "float32"), "life": _sb(C, "float32"),
     "fw": _sb(512, "float32"), "bw": _sb(512, "float32"), "c64": _sb(64, "float32"), "cu": _sb(16, "uint16"),
-    "sees": _sb(C, "float32"), "su": _sb(24, "uint16"), "back": _sb(C, "float32"), "bu": _sb(24, "uint16"),
+    "sees": _sb(C, "float32"), "su": _sb(96, "uint16"), "back": _sb(C, "float32"), "bu": _sb(24, "uint16"),
     "ext2": _sb(C, "float32"), "far": _sb(C, "float32"), "pen": _sb(C, "float32"), "lt": _sb(4, "float32"),
     "pt": _sb(4, "float32"), "sc": _sb(4, "float32"), "dl": _sb(4, "float32"), "thr": _sb(C, "float32"),
     "xs": _sb(C, "float32"),
-    "xb": _sb(4 * W, "bfloat16"), "xq": _sb(C, X4), "xp": _sb(C, U8), "tp": _sb(4 * W, "bfloat16"),
+    "xb": _sb(4 * (XO + C), "bfloat16"), "xq": _sb(C, X4), "xp": _sb(C, U8), "tp": _sb(4 * W, "bfloat16"),
     "comp": _sb(512, "bfloat16"), "z": _sb(4 * C, "bfloat16"), "zq": _sb(C, X4), "zp": _sb(C, U8),
     "cm": _sb(4 * C, "bfloat16"), "cmq": _sb(C, X4), "cmp": _sb(C, U8),
-    "win": _sb(W, "bfloat16"), "kt": _sb(2 * C, "bfloat16"), "ktq": _sb(C // 2, X4), "ktp": _sb(C // 2, U8),
+    "win": _sb(16 + C, "bfloat16"), "kt": _sb(2 * C, "bfloat16"), "ktq": _sb(C // 2, X4), "ktp": _sb(C // 2, U8),
     "ub": _sb(512, "bfloat16"), "uq": _sb(128, X4), "up": _sb(128, U8), "uu": _sb(24, "uint16"),
     "uq2": _sb(C, X4), "up2": _sb(C, U8), "vb": _sb(512, "bfloat16"), "vq": _sb(128, X4), "vp": _sb(128, U8),
     "wq": _sb(512, X4), "wp": _sb(512, U8), "yb": _sb(C, "float32"),
@@ -128,11 +132,20 @@ def rank_program(g, core, T, topo):
         more = {k: x for k, x in (("bias", bias), ("scale", scale)) if x is not None}
         op("s", lambda: S.activation(out, a, f, **more), r, w)
 
+    def move(q, out, a, r, w):
+        if q == "v":
+            cp(out, a, r, w)
+        else:
+            act(out, a, Fn.Copy, r, w)
+
     def iota(out, pattern, base, cm, r, w, small=False):
         if small:
             op("g", lambda: g.iota(out, pattern, base, cm, allow_small_or_imprecise_dtypes=True), r, w)
         else:
             op("g", lambda: g.iota(out, pattern, base, cm), r, w)
+
+    def whole(out, cols, value, r, w):
+        iota(out, [[0, cols]], value, 0, r, w, True)
 
     def bank(b, lo, hi):
         return T.ps[:, 512 * b + lo:512 * b + hi]
@@ -144,8 +157,8 @@ def rank_program(g, core, T, topo):
     def part(q, p, b):
         return q[:, 128 * b:128 * b + 128], p[:, 128 * b:128 * b + 128]
 
-    names = ["p", "q16", "q12", "q3", "q7", "offk", "c4a", "c4", "z0", "zp", "thv", "g16", "ca", "cb", "cc", "c3", "eb",
-             "sg", "sg32", "pens", "w0", "w1"]
+    names = ["p", "q16", "q12", "q3", "q7", "offk", "offb", "c4a", "c4s", "c4c", "z0", "zp", "thv", "g16", "ca", "cb", "cc",
+             "c3", "eb", "sg", "sg32", "pens", "w0", "w1"]
 
     def col(name):
         i = names.index(name)
@@ -156,20 +169,45 @@ def rank_program(g, core, T, topo):
         act(col(name), col(src), f, r, [name], bias=col(bias) if isinstance(bias, str) else bias,
             scale=col(scale) if isinstance(scale, str) else scale)
 
-    def hold(buf, src, cols, r, key):
-        scan(buf[:, 0:cols], T.m16[:, 0:cols], src, Op.add, Op.max, r + ["m16"], [key])
+    def const(out, cols, value, r, w):
+        act(out, T.cnt[:, 0:cols], Fn.Identity, ["cnt0"] + r, w, bias=value, scale=0.0)
 
-    def take(out, buf, cols, key, w):
-        ts(out, buf[:, 15:cols:16], col("offk"), None, Op.subtract, None, [key, "offk"], w)
+    def hold(out, src, cols, r, key):
+        scan(out, T.m16[:, 0:cols], src, Op.add, Op.max, r + ["m16"], [key])
+
+    def hold4(buf, src, cols, r, key):
+        scan(buf[:, 0:cols], T.m4[:, 0:cols], src, Op.add, Op.max, r + ["m40", "m41", "m42", "m43"], [key])
 
     u32 = dt.uint32
     xall = ["x0", "x1", "x2", "x3"]
-    dma([("y", T.lin[:, 0:24], T.seat[:])], [], ["seat"])
-    dma([("y" if i < 4 else "s", T.lin[16 * i:16 * i + 16, 24:48], T.alive[:]) for i in range(8)], [], ["alive"])
-    dma([("y", T.xb[:, 4 * OWN:4 * W], T.x[:])], [], xall)
+    X = T.xb[:, 4 * XO:4 * (XO + C)]
+
+    def quant_x():
+        quant(T.xq[:], T.xp[:], X, xall, ["xq"])
+
+    def unpack_own(stop):
+        for b in range(4):
+            mm(b, C, *part(T.eq, T.es, b), T.xq[:], T.xp[:], ["e%d" % b, "xq"], True, stop)
+
+    def copy_t(b):
+        act(T.tp[:, 4 * OWN + b:4 * W:4], bank(b, 0, C), Fn.Copy, ["P%d" % b], ["to%d" % b], scale=0.015625)
+
+    def copy_out(q, out, b, cols, key):
+        if q == "v":
+            ts(out, bank(b, 0, cols), 0.015625, None, Op.mult, None, ["P%d" % b], [key])
+        else:
+            act(out, bank(b, 0, cols), Fn.Copy, ["P%d" % b], [key], scale=0.015625)
+
+    def copy_x(b, q="s"):
+        copy_out(q, T.xb[:, 4 * XO + b:4 * (XO + C):4], b, C, "x%d" % b)
+
+    dma([("s", T.lin[:, 0:24], T.seat[:])], [], ["seat"])
+    dma([("y" if i < 5 else "s", T.lin[16 * i:16 * i + 16, 24:48], T.alive[:]) for i in range(8)], [], ["alive"])
+    dma([("y", X, T.x[:])], [], xall)
     dma([("y", T.ub[:], T.u[:])], [], ["ub"])
     dma([("y", T.wq[:].bitcast(dt.uint8), T.wc[:]), ("y", T.wp[:], T.ws[:])], [], ["w"])
     dma([("y", T.vb[:], T.v[:])], [], ["vb"])
+    alive = T.lin[:, 24:48]
 
     iota(T.pint[:, 0:1], [[0, 1]], 0, 1, [], ["pi"])
     iota(T.cnt[:, 0:OWN], [[1, OWN]], 0, 0, [], ["cnt0"], True)
@@ -182,122 +220,146 @@ def rank_program(g, core, T, topo):
                 al = -7 if dj > 0 else 7
                 bi, ga = (1, 1) if dj == 0 else (-6, 36 + (7 * 63 if dj > 0 else 0))
                 be, ga = (bi, ga) if di < 0 else (-bi, ga + 5 * bi)
-            iota(T.posi[32 * a:32 * a + 16 + 16 * odd, :], [[be, 6], [16 * al, 4]], ga - 16 * al * odd, al, ["pi", "cnt0"],
-                 ["posi%d" % a])
+            entry = -1000 if di == 0 else (UP if di < 0 else DOWN) - (6 if dj else 0)
+            iota(T.posi[32 * a:32 * a + 16 + 16 * odd, :], [[entry, 2], [be, 6], [16 * al, 4]], ga - 16 * al * odd, al,
+                 ["pi", "cnt0"], ["posi%d" % a], True)
     posi_all = ["posi0", "posi1", "posi2", "posi3"]
-    iota(T.four[:], [[0, 16], [4, 4]], 0, 0, posi_all, ["four"], True)
-    iota(T.life[:, 0:OWN], [[0, OWN]], 1, 0, [], ["life0"], True)
-    iota(T.xb[:, 0:4 * OWN], [[0, 4 * OWN]], 0, 0, [], ["xz"], True)
-    iota(T.comp[:, 256:512], [[0, 256]], 0, 0, [], ["compz"], True)
-    op("g", lambda: g.affine_select(T.tri[:], T.life[:, 0:128], [[1, 128]], Op.is_gt, 0.0, 0, -1), ["life0"], ["tri"])
-    for b in range(4):
-        iota(T.tp[:, W * b:W * b + UP], [[0, UP]], 0, 0, [], ["tz%d" % b], True)
-    iota(T.win[:, 0:OWN], [[0, OWN]], 0, 0, [], ["winz"], True)
+    whole(T.strip[:], 528, 0, posi_all, ["strip"])
+    diagonal = T.strip[:, 3:515:4]
+    op("g", lambda: g.affine_select(diagonal, diagonal, [[1, 128]], Op.not_equal, 64.0, 0, -1), ["strip"], ["strip"])
+    whole(T.xb[:, 0:4 * XO], 4 * XO, 0, [], ["xz"])
+    whole(T.comp[:, 256:512], 256, 0, [], ["compz"])
+    whole(T.dead[:, 0:OWN], OWN, 0, [], ["dead0"])
 
-    fill(T.strip[:], 0.0, ["strip"])
+    fill(T.ones[:], 1.0, ["ones"])
     for i, m in enumerate((15, 12, 3, 7)):
         ts(T.pint[:, 1 + i:2 + i], T.pint[:, 0:1], m, None, Op.bitwise_and, None, ["pi"], ["pi%d" % i])
-    eb = names.index("eb")
-    fill(T.pf[0:64, eb:eb + 1], float(UP), ["eb0"])
+    op("v", lambda: V.tensor_tensor_scan(T.cnt[:, OWN:W], T.ones[:, 0:C], T.ones[:, 0:C], OWN - 1.0, Op.mult, Op.add),
+       ["ones"], ["cnt1"])
+    act(T.two[:, 0:1], T.ones[:, 0:1], Fn.Copy, ["ones"], ["two0"], scale=-1 / EPS)
+    act(T.two[:, 1:2], T.ones[:, 0:1], Fn.Copy, ["ones"], ["two1"], scale=BIG)
+    act(T.d0[:], T.ones[:], Fn.Copy, ["ones"], ["d0"], scale=-EPS)
+    cp(T.aliveu[:], alive, ["alive"], ["aliveu"])
     cp(T.pf[:, 0:5], T.pint[:, 0:5], ["pi", "pi0", "pi1", "pi2", "pi3"], ["pf"])
-    fill(T.pf[64:128, eb:eb + 1], float(DOWN), ["eb1"])
-    for i in range(3):
-        act(T.cnt[:, OWN + 128 * i:OWN + 128 * i + 128], T.cnt[:, 0:128], Fn.Identity, ["cnt0"], ["cnt%d" % (i + 1)],
-            bias=float(OWN + 128 * i))
-    cnt_all = ["cnt0", "cnt1", "cnt2", "cnt3"]
-    small("g16", "q16", Fn.Identity, "p", -1.0)
-    small("ca", "g16", Fn.Abs, -56.0, 1.0)
-    small("cb", "ca", Fn.Square, -2.5, 0.0625)
-    small("cc", "cb", Fn.Square, 0.0, 1.0)
-    act(T.idl[:], T.cnt[:, 0:LL], Fn.Copy, cnt_all, ["idl"], scale=0.0)
-    ts(T.strip[:, 3:515:4], T.cnt[:, 0:128], col("p"), 64.0, Op.is_equal, Op.mult, ["cnt0", "pf"], ["strip"])
-    ts(T.q16u[:], T.cnt[:, 0:32], 0.0, col("q16"), Op.mult, Op.add, ["cnt0", "pf"], ["q16u"])
-    ts(T.blk[:], T.cnt[:, 0:16], col("q16"), -BIG, Op.is_equal, Op.mult, ["cnt0", "pf"], ["blk"])
-    for b in range(4):
-        quant(*part(T.eq, T.es, b), T.strip[:, 3 - b:515 - b], ["strip"], ["e%d" % b])
-    ts(col("c3"), col("cc"), 6.0, None, Op.mult, None, ["cc"], ["c3"])
-    cp(T.linu[:, 0:24], T.lin[:, 0:24], ["seat"], ["seatu"])
-    seatu, aliveu = T.linu[:, 0:24], T.linu[:, 24:48]
-    act(T.seatf[:], T.cnt[:, OWN:W].indirect(seatu), Fn.Copy, cnt_all + ["seatu"], ["seatf"])
-    ts(T.tmp[:, 0:69], T.cnt[:, 0:69], col("c3"), None, Op.subtract, None, ["cnt0", "c3"], ["tmp0"])
-    cp(T.posu[:], T.posi[:], posi_all, ["posu"])
-    ts(T.tmp[:, 72:141], T.tmp[:, 0:69], 0.0, None, Op.is_ge, None, ["tmp0"], ["tmp1"])
-    ts(T.tmp[:, 144:213], T.tmp[:, 0:69], col("eb"), float(OWN - 1), Op.add, Op.min, ["tmp0", "eb0", "eb1"], ["tmp2"])
-    cp(T.linu[:, 24:48], T.lin[:, 24:48], ["alive"], ["aliveu"])
-    tt(T.idl[:, 0:483:7], T.tmp[:, 72:141], T.tmp[:, 144:213], Op.mult, ["tmp1", "tmp2"], ["idl"])
-    ts(T.tmp[:, 0:64], T.four[:], col("q12"), -BIG, Op.is_equal, Op.mult, ["four", "pf"], ["tmp0"])
-    act(T.m16[:], T.blk[:].indirect(T.q16u[:, 0:31]), Fn.Identity, ["blk", "q16u"], ["m16"], bias=K)
+    tt(T.ni[:], T.two[:, 0:2].indirect(T.aliveu[:]), T.cnt[:, OWN:W], Op.min, ["two0", "two1", "aliveu", "cnt1"], ["ni"])
+    cp(T.seatu[:], T.lin[:, 0:24], ["seat"], ["seatu"])
+    small("c4a", "q3", Fn.Identity, 12 * K, 1.0)
     small("offk", "q16", Fn.Identity, 15 * K, -K)
-    act(T.life[:, OWN:W], T.cnt[:, 0:8].indirect(aliveu), Fn.Copy, ["cnt0", "aliveu"], ["life"])
-    act(T.m4[:], T.tmp[:, 0:64], Fn.Identity, ["tmp0"], ["m4"], bias=K)
-    small("c4a", "q3", Fn.Identity, -12 * K, 1.0)
-    small("z0", "q16", Fn.Relu, 1.0, -1.0)
-    small("c4", "q12", Fn.Identity, "c4a", K)
-    cp(T.idl[:].indirect(T.posu[:]), T.seatf[:], ["seatf", "posu"], ["idl"])
-    hold(T.ext, T.idl[:], LL, ["idl"], "ext")
-    take(T.lu[:, 0:31], T.ext, LL, "ext", ["lu"])
-    lines = T.lu[:, 0:31]
+    small("c4s", "q12", Fn.Identity, "c4a", -K)
+    small("sg", "q16", Fn.Sign, "p", -17.0)
+    ts(T.blk[:, 16:32], T.cnt[:, 0:16], col("q12"), -BIG, Op.is_equal, Op.mult, ["cnt0", "pf"], ["blk4"])
+    act(T.nis[:, 0:224], T.ni[:].indirect(T.seatu[:, 0:14]), Fn.Copy, ["ni", "seatu"], ["nis0"], scale=-EPS)
+    ts(T.nis[:, 224:C], T.ni[:].indirect(T.seatu[:, 14:24]), -EPS, None, Op.mult, None, ["ni", "seatu"], ["nis1"])
+    cp(T.posu[:], T.posi[:, 0:24], posi_all, ["posu"])
+    ts(T.tmp[:, 0:69], T.cnt[:, 0:69], T.posi[:, 24:25], T.posi[:, 0:1], Op.add, Op.subtract, ["cnt0"] + posi_all, ["tmp0"])
+    cp(T.d0[:].indirect(T.posu[:]), T.nis[:], ["nis0", "nis1", "posu"], ["d0"])
+    cnt_all = ["cnt0", "cnt1"]
+    act(T.blk[:, 16:32], T.blk[:, 16:32], Fn.Identity, ["blk4"], ["blk4"], bias=K * EPS)
+    act(T.tmp[:, 72:141], T.tmp[:, 0:69], Fn.Copy, ["tmp0"], ["tmp1"], scale=-EPS)
+    for h, least in enumerate((1, DOWN)):
+        act(T.tmp[64 * h:64 * h + 64, 144:213], T.tmp[64 * h:64 * h + 64, 0:69], Fn.Relu, ["tmp0"], ["tmp2%d" % h],
+            bias=least - 0.5, scale=-1.0)
+    for b in range(4):
+        const(T.m4[:, b:C:4], C // 4, T.blk[:, 16 + 4 * b:17 + 4 * b], ["blk4"], ["m4%d" % b])
+    small("c4c", "c4s", Fn.Identity, -4.0 * (OWN - XO), 1.0)
+    act(T.posf[:], T.cnt[:, 0:W].indirect(T.posu[:]), Fn.Copy, cnt_all + ["posu"], ["posf"])
+    tt(T.tmp[:, 72:141], T.tmp[:, 72:141], T.tmp[:, 144:213], Op.add, ["tmp1", "tmp20", "tmp21"], ["tmp1"])
+    ts(T.q16u[:], T.cnt[:, 0:24], 0.0, col("q16"), Op.mult, Op.add, ["cnt0", "pf"], ["q16u"])
+    tt(T.d0[:, 0:483:7], T.d0[:, 0:483:7], T.tmp[:, 72:141], Op.min, ["tmp1", "d0"], ["d0"])
+    ts(T.blk[:, 0:16], T.cnt[:, 0:16], col("q16"), -BIG, Op.is_equal, Op.mult, ["cnt0", "pf"], ["blk"])
+    dead_all = ["dead0", "deadA", "deadB"]
 
-    def quant_x():
-        quant(T.xq[:], T.xp[:], T.xb[:, 4 * OWN:4 * W], xall, ["xq"])
-
-    def unpack_own(stop):
-        for b in range(4):
-            mm(b, C, *part(T.eq, T.es, b), T.xq[:], T.xp[:], ["e%d" % b, "xq"], True, stop)
-
-    def later_constants():
-        act(T.posf[:], T.cnt[:].indirect(T.posu[:]), Fn.Copy, cnt_all + ["posu"], ["posf"])
-        small("sg", "q16", Fn.Sign, "p", -17.0)
-        small("w0", "z0", Fn.Identity, 0.0, 0.0625)
-        small("w1", "z0", Fn.Identity, 0.0078125, -0.0078125)
-        small("zp", "p", Fn.Identity, 0.0, "z0")
-        small("sg32", "sg", Fn.Identity, 0.0, 32.0)
-        small("pens", "sg", Fn.Identity, 0.0, BIG / 256)
-        small("thv", "zp", Fn.Identity, 31.5, -2.0)
-        act(T.fw[:, 0:1], T.cnt[:, 0:1], Fn.Copy, ["cnt0"], ["fwz"])
-        for b in range(4):
-            act(T.wts[:, b:512:4], T.cnt[:, 0:128], Fn.Identity, ["cnt0"], ["wv%d" % b], bias=1.0 if b < 3 else 0.0, scale=0.0)
-
-    def backward():
-        scan(T.bw[:, LL + 6:6:-1], T.la[:, LL - 1::-1], T.lb[:, LL - 1::-1], Op.mult, Op.add, ["la", "lb"], ["bw"])
-
-    def seen_by():
-        act(T.back[:], T.bw[:, 8:LL + 7].indirect(T.pu[:]), Fn.Copy, ["bw", "pu"], ["back"])
+    def unpacker(b):
+        quant(*part(T.eq, T.es, b), T.strip[:, 3 - b:515 - b], ["strip"], ["e%d" % b])
 
     def arrived(b, q):
-        out = T.tp[:, W * b + UP:W * b + OWN]
-        if q == "v":
-            ts(out, bank(4 + b, 0, 128), 0.015625, None, Op.mult, None, ["P%d" % (4 + b)], ["ta%d" % b])
-        else:
-            act(out, bank(4 + b, 0, 128), Fn.Copy, ["P%d" % (4 + b)], ["ta%d" % b], scale=0.015625)
+        copy_out(q, T.tp[:, 4 * UP + b:4 * GAP:4], 4 + b, 128, "ta%d" % b)
 
-    def gather_z(b, q, lo, hi):
-        src = T.tp[:, W * b:W * b + W].indirect(T.su[:, lo // 16:hi // 16])
-        r, w = ["tz%d" % b, "ta%d" % b, "to%d" % b, "su"], ["z%d%d" % (b, h) for h in range(lo // 192, hi // 192)]
+    t_all = ["tz", "tg"] + ["ta%d" % b for b in range(4)] + ["to%d" % b for b in range(4)]
+
+    def gather_z(q, lo, hi, key):
+        move(q, T.z[:, 4 * lo:4 * hi], T.tp[:].indirect(T.su[:, lo // 4:hi // 4]), t_all + ["su"], [key])
+
+    def name_weights():
+        for b, o, x in ((2, Op.is_equal, -2.0 ** -15), (3, Op.not_equal, 2.0 ** -12)):
+            ts(T.wts[:, 512 + b:1026:4], T.comp[:, 256:384], col("q16"), x, o, Op.mult, ["compz", "pf"], ["wk%d" % b])
+
+    def weights():
+        whole(T.tp[:, 0:4 * UP], 4 * UP, 0, [], ["tz"])
+        whole(T.tp[:, 4 * GAP:4 * OWN], 4 * (OWN - GAP), 0, [], ["tg"])
+        whole(T.fw[:, 0:1], 1, 0, [], ["fwz"])
+        op("g", lambda: g.affine_select(T.tri[:], T.ones[:, 0:128], [[1, 128]], Op.is_gt, 0.0, 0, -1), ["ones"], ["tri"])
+        for b in range(4):
+            whole(T.wts[:, b:512:4], 128, int(b < 3), [], ["wv%d" % b])
+        for b in range(2):
+            whole(T.wts[:, 512 + b:1026:4], 129, 0, [], ["wk%d" % b])
+
+    def penalty(q):
         if q == "v":
-            cp(T.z[:, 4 * lo + b:4 * hi:4], src, r, w)
+            ts(T.pen[:], T.sees[:], (0.5 - OWN) * EPS, col("pens"), Op.is_gt, Op.mult, ["sees", "pens"], ["pen"])
         else:
-            act(T.z[:, 4 * lo + b:4 * hi:4], src, Fn.Copy, r, w)
+            act(T.far[:], T.sees[:], Fn.Relu, ["sees"], ["far"], bias=OWN - 0.5, scale=1 / EPS)
+            act(T.pen[:], T.far[:], Fn.Identity, ["far", "pens"], ["pen"], scale=col("pens"))
+
+    def backward(d, dk, i, parts=4):
+        hi = LS - 1 - i * LS // parts
+        src = d[:, hi:hi - LS // parts:-1] if i < parts - 1 else d[:, hi::-1]
+        start = T.bw[:, hi + 8:hi + 9] if i else 0.0
+        op("v", lambda: V.tensor_tensor_scan(T.bw[:, hi + 7:hi + 7 - LS // parts:-1], src, src, start, Op.mult, Op.min),
+           [dk] + ["bw%d" % (i - 1)] * (i > 0), ["bw%d" % i])
+
+    def hold_lines(i):
+        lo, hi = 128 * i, min(LL, 128 * i + 128)
+        hold(T.ext3[:, lo:hi], T.idl[:, lo:hi], hi - lo, ["idl"], "ext3%d" % i)
+
+    def seen_by():
+        act(T.back[:], T.bw[:, 8:LS + 7].indirect(T.pu[:]), Fn.Copy, ["bw3", "bw2", "bw1", "bw0", "pu"], ["back"], scale=-1 / EPS)
+
+    def hold_back():
+        hold(T.ext2[:], T.back[:], C, ["back"], "ext2")
+
+    def take_back():
+        ts(T.bu[:], T.ext2[:, 15:C:16], col("offb"), None, Op.subtract, None, ["ext2", "offb"], ["bu"])
+
+    def dead_along_partitions():
+        dma([("y", T.lt[:, k:k + 1], T.dead[0:1, OWN + 128 * k:OWN + 128 * k + 128]) for k in range(3)], dead_all, ["lt"])
 
     for t in range(R):
         first, last = t == 0, t == R - 1
-        tt(T.lb[:], T.life[:].indirect(lines), T.idl[:], Op.mult, ["life0", "life", "lu", "idl"], ["lb"])
-        act(T.la[:], T.life[:].indirect(lines), Fn.Identity, ["life0", "life", "lu"], ["la"], bias=1.0, scale=-1.0)
-        if first:
-            later_constants()
-        dma([("y", T.lt[:, k:k + 1], T.life[0:1, OWN + 128 * k:OWN + 128 * k + 128]) for k in range(3)], ["life"], ["lt"])
-        scan(T.fw[:, 1:LL + 1], T.la[:], T.lb[:], Op.mult, Op.add, ["la", "lb"], ["fw"])
-        scan(T.c64[:], T.m4[:], T.fw[:, 7:455:7], Op.add, Op.max, ["fw", "m4"], ["c64"])
-        ts(T.cu[:], T.c64[:, 3:64:4], 4.0, col("c4"), Op.mult, Op.add, ["c64", "c4"], ["cu"])
-        cp(T.comp[:, 0:256], T.xb[:].indirect(T.cu[:]), ["cu", "xz"] + xall, ["comp"])
+        d, dk = (T.d0, "d0") if first else (T.d1, "d1")
+        if not first:
+            tt(d[:], T.dead[:].indirect(T.lu[:, 0:31]), T.d0[:], Op.add, dead_all + ["lu", "d0"], [dk])
+            dead_along_partitions()
+            for b in range(3):
+                copy_t(b)
+                if b == 1:
+                    act(T.life[:], T.dead[:, OWN:W], Fn.Identity, dead_all, ["life"], bias=1.0, scale=-1.0)
+        else:
+            act(T.m16[:], T.blk[:, 0:16].indirect(T.q16u[:]), Fn.Identity, ["blk", "q16u"], ["m16"], bias=K)
+
+        def between(i):
+            if first:
+                unpacker(i)
+            else:
+                backward(d, dk, i)
+
+        scan(T.fw[:, 1:LS + 1], d[:, 0:LS], d[:, 0:LS], Op.mult, Op.min, [dk], ["fw"])
+        between(0)
+        hold4(T.c64, T.fw[:, 7:455:7], 64, ["fw"], "c64")
+        between(1)
+        ts(T.cu[:], T.c64[:, 3:64:4], -4 / EPS, col("c4c"), Op.mult, Op.add, ["c64", "c4c"], ["cu"])
+        between(2)
+        for h, q in enumerate("vs"):
+            move(q, T.comp[:, 128 * h:128 * h + 128], T.xb[:].indirect(T.cu[:, 8 * h:8 * h + 8]), ["cu", "xz"] + xall,
+                 ["comp%d" % h])
+        between(3)
         sq, sp, lq, lp = T["sq%d" % t], T["sp%d" % t], T["lq%d" % t], T["lp%d" % t]
-        quant(sq[:], sp[:], T.comp[:], ["comp", "compz"], ["sq%d" % t])
+        quant(sq[:], sp[:], T.comp[:], ["comp0", "comp1", "compz"], ["sq%d" % t])
         order("g", ["sq%d" % t], [], ())
         for src, dst, codes in ((sq, lq, True), (sp, lp, False)):
             moves = []
             for i, to in enumerate((below, above)):
-                eng = topo.engines(core, to)
-                half = eng[i * len(eng) // 2:(i + 1) * len(eng) // 2]
+                half = topo.engines(core, to)[i::2]
                 rid, pid = topo.addr(to)[:2]
                 a, b = src[:, 0:64], dst[:, 64 * i:64 * i + 64]
                 if codes:
@@ -310,123 +372,205 @@ def rank_program(g, core, T, topo):
         writer["land"] = [("arr%d" % t, landed, {}, "far")]
         readers["land"] = []
 
+        def unpack_arrived():
+            for b in range(4):
+                mm(4 + b, 128, *part(T.eq, T.es, b), lq[:], lp[:], ["e%d" % b, "land"])
+
         if first:
+            weights()
+            whole(T.win[:, 0:16], 16, 0, [], ["winz"])
+            act(T.dead[:, OWN:W], T.ni[:], Fn.Relu, ["ni"], ["deadA", "deadB"], scale=-EPS)
+            dead_along_partitions()
             quant_x()
             unpack_own(True)
-        for b in range(4):
-            act(T.tp[:, W * b + OWN:W * b + W], bank(b, 0, C), Fn.Copy, ["P%d" % b], ["to%d" % b], scale=0.015625)
-        for b in range(4):
-            mm(4 + b, 128, *part(T.eq, T.es, b), lq[:], lp[:], ["e%d" % b, "land"])
-        unpack_own(False)
-        if first:
-            cp(T.pc[:].indirect(seatu), T.posf[:], ["posf", "seatu"], ["pc"])
-            hold(T.ext, T.pc[:], C, ["pc"], "ext")
+            act(T.idl[:], T.d0[:], Fn.Relu, ["d0"], ["idl"], scale=-1 / EPS)
+            small("pens", "sg", Fn.Identity, 0.0, BIG / 256)
+            for b in range(4):
+                copy_t(b)
+            small("sg32", "sg", Fn.Identity, 0.0, 32.0)
+            cp(T.pc[:].indirect(T.seatu[:]), T.posf[:], ["posf", "seatu"], ["pc"])
             quant(T.uq[:], T.up[:], T.ub[:], ["ub"], ["uq"])
-            take(T.pu[:], T.ext, C, "ext", ["pu"])
+            hold(T.ext[:, 0:C], T.pc[:], C, ["pc"], "ext")
             ts(T.uu[:, 8:16], T.cnt[:, 0:8], col("q7"), 16.0, Op.max, Op.mult, ["cnt0", "pf"], ["uu1"])
+            tt(T.jw[:], T.ext[:, 15:C:16], alive, Op.mult, ["ext", "alive"], ["jw"])
             ts(T.uu[:, 16:24], T.cnt[:, 0:8], col("q7"), 16.0, Op.min, Op.mult, ["cnt0", "pf"], ["uu2"])
+            ts(T.pu[:], T.jw[:], col("offk"), None, Op.subtract, None, ["jw", "offk"], ["pu"])
             fill(T.uu[:, 0:8], 1, ["uu0"])
-            act(T.up2[:], T.up[:].indirect(T.uu[:]), Fn.Copy, ["uq", "uu0", "uu1", "uu2"], ["u2b"])
-        if last:
-            backward()
-            seen_by()
-        tt(T.sees[:], T.fw[:, 0:LL + 1].indirect(T.pu[:]), T.life[:, OWN:W], Op.mult, ["fw", "fwz", "pu", "life"], ["sees"])
-        if t == 1:
-            backward()
-        hold(T.ext, T.sees[:], C, ["sees"], "ext")
-        if t == 1:
-            quant(T.vq[:], T.vp[:], T.vb[:], ["vb"], ["vq"])
-        if last:
-            hold(T.ext2, T.back[:], C, ["back"], "ext2")
-        take(T.su[:], T.ext, C, "ext", ["su"])
-        if first:
+            unpack_arrived()
+            act(T.sees[:], T.fw[:, 0:LS + 1].indirect(T.pu[:]), Fn.Copy, ["fw", "fwz", "pu"], ["sees"])
+            ts(col("zp"), col("q16"), 0.0, col("p"), Op.is_equal, Op.mult, ["pf"], ["zp"])
             cp(T.uq2[:].bitcast(u32), T.uq[:].bitcast(u32).indirect(T.uu[:]), ["uq", "uu0", "uu1", "uu2"], ["u2a"])
+            hold4(T.ext, T.sees[:], C, ["sees"], "ext")
+            name_weights()
+        else:
+            copy_t(3)
+            unpack_own(False)
+            seen_by()
+            tt(T.sees[:], T.fw[:, 0:LS + 1].indirect(T.pu[:]), T.life[:], Op.mult, ["fw", "fwz", "pu", "life"], ["sees"])
+            if t == 1:
+                quant(T.vq[:], T.vp[:], T.vb[:], ["vb"], ["vq"])
+            hold4(T.ext, T.sees[:], C, ["sees"], "ext")
+            penalty("v")
+        ts(T.su[:], T.ext[:, 3:C:4], -4 / EPS, col("c4s"), Op.mult, Op.add, ["ext", "c4s"], ["su"])
+        act(T.pt[:, 0:3], T.lt[:, 0:3], Fn.Identity, ["lt"], ["pt"], scale=-BIG)
+        if first:
             for b in range(4):
                 arrived(b, "s")
-            for b, q, lo, hi in ((1, "s", 0, C), (0, "v", 0, C), (3, "s", 0, C), (2, "v", 0, C // 2), (2, "s", C // 2, C)):
-                gather_z(b, q, lo, hi)
-            act(T.pt[:, 0:3], T.lt[:, 0:3], Fn.Identity, ["lt"], ["pt"], bias=-BIG, scale=BIG)
-            act(T.far[:], T.sees[:], Fn.Relu, ["sees"], ["far"], bias=float(OWN), scale=-1.0)
+            unpack_own(False)
+            penalty("v")
         else:
-            act(T.pt[:, 0:3], T.lt[:, 0:3], Fn.Identity, ["lt"], ["pt"], bias=-BIG, scale=BIG)
+            hold_back()
+            unpack_arrived()
             for b in range(4):
-                arrived(b, "vs"[b % 2])
-            for b in range(4):
-                gather_z(b, "vs"[b % 2], 0, C)
-            if not last:
-                seen_by()
-        quant(T.zq[:], T.zp[:], T.z[:], ["z%d%d" % (b, h) for b in range(4) for h in range(2)], ["zq"])
-        if first:
-            backward()
-        else:
-            ts(T.pen[:], T.sees[:], OWN - 0.5, col("pens"), Op.is_lt, Op.mult, ["sees", "pens"], ["pen"])
-        uk = ["u2a", "u2b", "zq"]
-        for k in range(3):
-            mm(4 + k, 128, *part(T.zq, T.zp, k), *part(T.uq2, T.up2, 0), uk)
-        mm(7, C, *part(T.uq2, T.up2, 0), T.zq[:], T.zp[:], uk)
-        tt(T.sc[:, 0:3], T.ps[:, 2048:3584:512], T.pt[:, 0:3], Op.add, ["P4", "P5", "P6", "pt"], ["sc"])
+                arrived(b, "vssv"[b])
+        uk = ["u2a", "u2b"]
+        zk = ["zq0", "zq1", "zq2"]
+
+        def quant_z(k, r):
+            quant(*part(T.zq, T.zp, k), T.z[:, 512 * k:512 * k + 512], r, [zk[k]])
+
+        def along_partitions(k, b):
+            mm(b, 128, *part(T.zq, T.zp, k), *part(T.uq2, T.up2, 0), uk + [zk[k]])
+
+        def score(k, b):
+            act(T.sc[:, k:k + 1], bank(b, 0, 1), Fn.Identity, ["P%d" % b, "pt"], ["sc%d" % k], bias=T.pt[:, k:k + 1])
+
+        def step_up(lo, hi):
+            act(T.dl[:, lo:hi], T.ps[:, 2048:2048 + 512 * (hi - lo):512], Fn.Abs, ["P4", "P5"][:hi - lo],
+                ["dl%d" % k for k in range(lo, hi)], bias=2.0 ** -122, scale=1.25 * 2.0 ** -24)
+
+        def threshold(k):
+            act(T.thr[:, 128 * k:128 * k + 128], T.tri[:], Fn.Identity, ["tri", "sc%d" % k, "dl%d" % k], ["thr%d" % k],
+                bias=T.sc[:, k:k + 1], scale=T.dl[:, k:k + 1])
+
+        def pairs(lo, hi, r):
+            for i in (1, 2):
+                mm(5 + i, hi - lo, *part(T.uq2, T.up2, i), T.zq[:, lo:hi], T.zp[:, lo:hi], uk + r)
+
+        def lowered(lo, hi, key):
+            tt(T.xs[:, lo:hi], bank(6, 0, hi - lo), T.pen[:, lo:hi], Op.add, ["P6", "pen"], ["xs" + key])
+
+        def ahead(lo, hi, key):
+            tt(T.cm[:, 4 * lo + 3:4 * hi:4], bank(7, 0, hi - lo), T.xs[:, lo:hi], Op.is_gt, ["P7", "xs" + key], ["cma" + key])
 
         def layer(b):
-            mm(b, C, *part(T.wq, T.wp, b), T.zq[:], T.zp[:], ["w", "zq"], False, True)
+            mm(b, C, *part(T.wq, T.wp, b), T.zq[:], T.zp[:], ["w"] + zk, False, True)
 
-        layer(0)
-        mm(4, C, *part(T.uq2, T.up2, 1), T.zq[:], T.zp[:], uk)
-        mm(5, C, *part(T.uq2, T.up2, 2), T.zq[:], T.zp[:], uk)
-        for b in (1, 2, 3):
-            layer(b)
+        def beats(k, lo, hi, slot, o, key):
+            ts(T.cm[:, 4 * lo + slot:4 * hi:4], bank(5, lo, hi), T.sc[:, k:k + 1], None, o, None, ["P5", "sc%d" % k], [key])
+
+        def beats_near(lo, hi, thr, key):
+            tt(T.cm[:, 4 * lo + 2:4 * hi:4], bank(5, lo, hi), T.thr[:, lo:hi], Op.is_lt, ["P5"] + thr, ["cmd" + key])
+
+        def count_part(lo, hi, b, keys, key):
+            quant(T.cmq[:, lo:hi], T.cmp[:, lo:hi], T.cm[:, 4 * lo:4 * hi], keys + ["cmd" + key, "cma" + key], ["cmq" + key])
+            mm(b, hi - lo, *part(T.kq, T.ks, 0), T.cmq[:, lo:hi], T.cmp[:, lo:hi], ["kq", "cmq" + key])
+
+        gather_z("v", 0, 128, "za")
+        gather_z("s", 128, 256, "zb")
         if first:
-            act(T.pen[:], T.far[:], Fn.Identity, ["far", "pens"], ["pen"], scale=col("pens"))
-        act(T.dl[:, 0:3], T.sc[:, 0:3], Fn.Abs, ["sc"], ["dl"], bias=2.0 ** -122, scale=1.25 * 2.0 ** -24)
-        for k in range(3):
-            act(T.thr[:, 128 * k:128 * k + 128], T.tri[:], Fn.Identity, ["tri", "sc", "dl"], ["thr%d" % k],
-                bias=T.sc[:, k:k + 1], scale=T.dl[:, k:k + 1])
+            act(T.up2[:], T.up[:].indirect(T.uu[:]), Fn.Copy, ["uq", "uu0", "uu1", "uu2"], ["u2b"])
+        cut = 272 if first else 304
+        gather_z("s", cut, C, "zd")
+        if first:
+            hold_lines(0)
+        quant_z(0, ["za"])
+        along_partitions(0, 4)
+        quant_z(1, ["zb"])
+        along_partitions(1, 5)
+        pairs(0, 256, zk[:2])
+        gather_z("v", 256, cut, "zc")
+        if first:
+            backward(d, dk, 0, 1)
+            hold_lines(1)
+        step_up(0, 2)
+        score(1, 5)
+        score(0, 4)
+        threshold(1)
+        quant_z(2, ["zc", "zd"])
+        mm(5, C, *part(T.uq2, T.up2, 0), T.zq[:], T.zp[:], uk + zk)
+        along_partitions(2, 4)
+        threshold(0)
         if first:
             seen_by()
-            for b in range(4):
-                act(T.wts[:, 512 + b:1026:4], T.cnt[:, 0:129 if b < 2 else 128], Fn.Identity, ["cnt0", "w0", "w1"],
-                    ["wk%d" % b], bias=col("w%d" % (b - 2)) if b >= 2 else 0.0, scale=0.0)
-        for k, lo, hi, slot, o in ((0, 128, 384, 0, Op.is_le), (2, 0, 256, 1, Op.is_lt), (1, 0, 128, 0, Op.is_lt),
-                                   (1, 256, 384, 1, Op.is_le)):
-            ts(T.cm[:, 4 * lo + slot:4 * hi:4], bank(7, lo, hi), T.sc[:, k:k + 1], None, o, None, ["P7", "sc"],
-               ["cm%d%d" % (k, slot)])
-        tt(T.xs[:], bank(4, 0, C), T.pen[:], Op.add, ["P4", "pen"], ["xs"])
-        tt(T.cm[:, 2:4 * C:4], bank(7, 0, C), T.thr[:], Op.is_lt, ["P7", "thr0", "thr1", "thr2"], ["cmd"])
-        tt(T.cm[:, 3:4 * C:4], bank(5, 0, C), T.xs[:], Op.is_gt, ["P5", "xs"], ["cma"])
+        score(2, 4)
+        step_up(2, 3)
+        layer(0)
+        copy_x(0)
+        threshold(2)
+        lowered(0, 256, "A")
         if first:
             ts(T.wts[:, 3:512:64], T.cnt[:, 0:8], col("q16"), col("sg32"), Op.is_equal, Op.mult, ["cnt0", "pf", "sg32"], ["wv3"])
+        else:
+            take_back()
+        ahead(0, 256, "A")
+        layer(1)
+        pairs(256, C, zk[2:])
+        layer(2)
+        if not first:
+            layer(3)
+        if first:
             quant(*part(T.kq, T.ks, 0), T.wts[:, 0:512], ["wv0", "wv1", "wv2", "wv3"], ["kq"])
-        quant(T.cmq[:], T.cmp[:], T.cm[:], ["cm00", "cm21", "cm10", "cm11", "cmd", "cma"], ["cmq"])
-        mm(6, C, *part(T.kq, T.ks, 0), T.cmq[:], T.cmp[:], ["kq", "cmq"])
-        if not last:
-            hold(T.ext2, T.back[:], C, ["back"], "ext2")
-        for b in range(4):
-            act(T.xb[:, 4 * OWN + b:4 * W:4], bank(b, 0, C), Fn.Copy, ["P%d" % b], ["x%d" % b], scale=0.015625)
+            small("thv", "zp", Fn.Identity, 31.5, -2.0)
+            small("offb", "offk", Fn.Identity, OWN - 16.0, 1.0)
+        beats(0, 128, 256, 0, Op.is_le, "cm1")
+        beats(1, 0, 128, 0, Op.is_lt, "cm2")
+        beats(2, 0, 256, 1, Op.is_lt, "cm0")
+        beats_near(0, 256, ["thr0", "thr1"], "A")
+        lowered(256, C, "B")
+        count_part(0, 256, 4, ["cm0", "cm1", "cm2"], "A")
+        if first:
+            layer(3)
+        beats(0, 256, C, 0, Op.is_le, "cm3")
+        ahead(256, C, "B")
+        beats(1, 256, C, 1, Op.is_le, "cm4")
+        beats_near(256, C, ["thr2"], "B")
+        if first:
+            hold_lines(2)
+        count_part(256, C, 6, ["cm3", "cm4"], "B")
+        for b in (1, 2):
+            copy_x(b)
+        if first:
+            hold_back()
+        else:
+            copy_x(3, "s" if last else "v")
+        act(T.win[:, 16:16 + 256], bank(4, 0, 256), Fn.Relu, ["P4", "thv"], ["winA"], bias=col("thv"), scale=-1.0)
+        act(T.kt[:, 1:512:2], bank(4, 0, 256), Fn.Relu, ["P4", "thv"], ["ktA"], bias=col("thv"), scale=-1.0)
         if last:
             quant_x()
             mm(0, C, T.vq[:], T.vp[:], T.xq[:], T.xp[:], ["vq", "xq"])
             dma([("y", T.oc[:], T.xq[:].bitcast(dt.uint8))]
                 + [("y", T.osc[4 * k:4 * k + 4, :], T.xp[32 * k:32 * k + 4, :]) for k in range(4)], ["xq"], [])
-        ts(T.win[:, OWN:W], bank(6, 0, C), col("thv"), None, Op.is_lt, None, ["P6", "thv"], ["win"])
-        take(T.bu[:], T.ext2, C, "ext2", ["bu"])
+        ts(T.win[:, 16 + 256:16 + C], bank(6, 0, 128), col("thv"), None, Op.is_lt, None, ["P6", "thv"], ["winB"])
+        if first:
+            take_back()
+        ts(T.kt[:, 513:2 * C:2], bank(6, 0, 128), col("thv"), None, Op.is_lt, None, ["P6", "thv"], ["ktB"])
+        for q, lo, hi, key in (("s", 224, C, "kt1"), ("v", 0, 224, "kt0")):
+            move(q, T.kt[:, 2 * lo:2 * hi:2], T.win[:].indirect(T.bu[:, lo // 16:hi // 16]), ["winz", "winA", "winB", "bu"], [key])
         if last:
             act(T.yb[:], bank(0, 0, C), Fn.Copy, ["P0"], ["yb"])
-            dma([("y", T.y[:], T.yb[:])], ["yb"], [])
-        act(T.kt[:, 1:2 * C:2], T.win[:, OWN:W], Fn.Identity, ["win"], ["kt1"], bias=1.0, scale=-1.0)
-        cp(T.kt[:, 0:2 * C:2], T.win[:].indirect(T.bu[:]), ["win", "winz", "bu"], ["kt0"])
+            dma([("s", T.y[:], T.yb[:])], ["yb"], [])
         if first:
+            copy_x(3)
             for h in range(2):
                 quant(*part(T.kq, T.ks, 1 + h), T.wts[:, 514 - 2 * h:1026 - 2 * h], ["wk0", "wk1", "wk2", "wk3"], ["kq%d" % h])
-        quant(T.ktq[:], T.ktp[:], T.kt[:], ["kt0", "kt1"], ["ktq"])
+        quant(T.ktq[:], T.ktp[:], T.kt[:], ["kt0", "kt1", "ktA", "ktB"], ["ktq"])
         for h in range(2):
-            mm(7 - h, C // 2, *part(T.kq, T.ks, 1 + h), T.ktq[:], T.ktp[:], ["kq%d" % h, "ktq"])
+            mm(6 + h, C // 2, *part(T.kq, T.ks, 1 + h), T.ktq[:], T.ktp[:], ["kq%d" % h, "ktq"])
         if not last:
             quant_x()
             unpack_own(True)
-        order("v", ["life"], ["life"], ())
-        for h in range(2):
-            tt(T.life[:, OWN + h:W:2], bank(7 - h, 0, C // 2), T.life[:, OWN + h:W:2], Op.is_lt, ["P%d" % (7 - h)], ["lh%d" % h])
-        writer["life"] = writer["lh0"] + writer["lh1"]
-        readers["life"] = []
-    dma([("y", T.ol[:], T.life[0:1, OWN:W])], ["life"], [])
+        if first:
+            hold_lines(3)
+        for h, key in enumerate(("deadA", "deadB")):
+            was = T.dead[:, OWN + h:W:2]
+            if last:
+                tt(T.life[:, h:C:2], bank(6 + h, 0, C // 2), was, Op.is_ge, ["P%d" % (6 + h), key], ["life%d" % h, "life"][:2 - h])
+            else:
+                tt(was, bank(6 + h, 0, C // 2), was, Op.is_lt, ["P%d" % (6 + h), key], [key])
+            if first and h == 0:
+                ts(T.lu[:, 0:31], T.ext3[:, 15:LL:16], col("offk"), None, Op.subtract, None,
+                   ["ext30", "ext31", "ext32", "ext33", "offk"], ["lu"])
+    dma([("y", T.ol[:], T.life[0:1, :])], ["life0", "life1"], [])
     for sem in count:
         need("g", (sem, count[sem], {}))

@@ -3,9 +3,12 @@ from concourse.mybir import dt, AluOpType, ActivationFunctionType
 
 H, A, C, M, R = 6, 64, 384, 32, 3
 WAY = [(-1, -1), (-1, 0), (-1, 1), (0, -1), (0, 1), (1, -1), (1, 0), (1, 1)]
-UP, DOWN, GAP, OWN, W = 16, 80, 144, 160, 544
+UP, DOWN, GAP, OWN, W = 16, 88, 152, 160, 544
+LAND = GAP - UP
 XO = 4
 LL, LS = 496, 484
+SENT = 7 * A
+BACK = (LS, 420, 356, 228, 0)
 K, BIG, EPS = 1024.0, 1e29, 2.0 ** -36
 X4, U8 = "float8_e4m3fn_x4", "uint8"
 
@@ -16,20 +19,19 @@ def _sb(n, d):
 
 SCRATCH = {
     "ps": ("psum", [128, 4096], "float32"),
-    "cnt": _sb(W, "float32"), "pint": _sb(8, "int32"), "pf": _sb(32, "float32"), "ones": _sb(LL, "float32"),
-    "two": _sb(8, "float32"),
-    "tmp": _sb(256, "float32"), "blk": _sb(32, "float32"), "m16": _sb(C, "float32"), "m4": _sb(C, "float32"),
-    "q16u": _sb(24, "uint16"), "posi": _sb(48, "float32"), "posu": _sb(24, "uint16"), "posf": _sb(C, "float32"),
-    "tri": _sb(128, "float32"), "strip": _sb(528, "bfloat16"), "wts": _sb(1032, "bfloat16"),
+    "cnt": _sb(W, "float32"), "pint": _sb(8, "int32"), "pf": _sb(32, "float32"), "ones": _sb(W // 2, "bfloat16"),
+    "two": _sb(8, "float32"), "tmp": _sb(72, "float32"), "mm": _sb(768, "float32"), "turn": _sb(160, "float32"),
+    "turnu": _sb(32, "uint16"), "posi": _sb(48, "float32"), "posu": _sb(24, "uint16"), "posf": _sb(C, "float32"),
+    "tri": _sb(128, "bfloat16"), "strip": _sb(528, "bfloat16"), "wts": _sb(1032, "bfloat16"),
     "eq": _sb(512, X4), "es": _sb(512, U8), "kq": _sb(384, X4), "ks": _sb(384, U8),
     "lin": _sb(48, "int32"), "seatu": _sb(24, "uint16"), "aliveu": _sb(24, "uint16"), "jw": _sb(24, "float32"),
     "ni": _sb(C, "float32"), "nis": _sb(C, "float32"),
-    "d0": _sb(LL, "float32"), "d1": _sb(LL, "float32"), "idl": _sb(LL, "float32"),
-    "ext": _sb(C, "float32"), "ext3": _sb(LL, "float32"), "lu": _sb(32, "uint16"), "pc": _sb(C, "float32"), "pu": _sb(24, "uint16"),
-    "dead": _sb(W, "float32"), "life": _sb(C, "float32"),
+    "d0": _sb(512, "float32"), "d1": _sb(LL, "float32"), "idl": _sb(512, "float32"), "lw": _sb(32, "float32"),
+    "ext": _sb(C, "float32"), "lu": _sb(32, "uint16"), "pc": _sb(512, "float32"), "pu": _sb(24, "uint16"),
+    "pw": _sb(32, "float32"), "pv": _sb(32, "uint16"), "dead": _sb(W, "float32"), "life": _sb(C, "float32"),
     "fw": _sb(512, "float32"), "bw": _sb(512, "float32"), "c64": _sb(64, "float32"), "cu": _sb(16, "uint16"),
-    "sees": _sb(C, "float32"), "su": _sb(96, "uint16"), "back": _sb(C, "float32"), "bu": _sb(24, "uint16"),
-    "ext2": _sb(C, "float32"), "far": _sb(C, "float32"), "pen": _sb(C, "float32"), "lt": _sb(4, "float32"),
+    "sees": _sb(C, "float32"), "su": _sb(96, "uint16"), "back": _sb(512, "float32"), "bu": _sb(24, "uint16"),
+    "backw": _sb(32, "float32"), "far": _sb(C, "float32"), "pen": _sb(C, "float32"), "lt": _sb(4, "float32"),
     "pt": _sb(4, "float32"), "sc": _sb(4, "float32"), "dl": _sb(4, "float32"), "thr": _sb(C, "float32"),
     "xs": _sb(C, "float32"),
     "xb": _sb(4 * (XO + C), "bfloat16"), "xq": _sb(C, X4), "xp": _sb(C, U8), "tp": _sb(4 * W, "bfloat16"),
@@ -43,10 +45,10 @@ SCRATCH = {
 for _t in range(R):
     SCRATCH["sq%d" % _t] = _sb(128, X4)
     SCRATCH["sp%d" % _t] = _sb(128, U8)
-    SCRATCH["lq%d" % _t] = _sb(128, X4)
-    SCRATCH["lp%d" % _t] = _sb(128, U8)
+    SCRATCH["lq%d" % _t] = _sb(LAND, X4)
+    SCRATCH["lp%d" % _t] = _sb(LAND, U8)
 
-SEMAPHORES = ["v", "s", "t", "g", "sent", "arr0", "arr1", "arr2"] + ["d%d" % i for i in range(16)]
+SEMAPHORES = ["v", "s", "t", "g", "sent", "arr0", "arr1", "arr2"] + ["d%d" % i for i in range(30)]
 
 Op, Fn = AluOpType, ActivationFunctionType
 
@@ -157,8 +159,7 @@ def rank_program(g, core, T, topo):
     def part(q, p, b):
         return q[:, 128 * b:128 * b + 128], p[:, 128 * b:128 * b + 128]
 
-    names = ["p", "q16", "q12", "q3", "q7", "offk", "offb", "c4a", "c4s", "c4c", "z0", "zp", "thv", "g16", "ca", "cb", "cc",
-             "c3", "eb", "sg", "sg32", "pens", "w0", "w1"]
+    names = ["p", "q16", "q12", "q3", "q7", "offk", "c4a", "c4s", "c4c", "zp", "thv", "sg", "sg32", "pens", "q256", "offb"]
 
     def col(name):
         i = names.index(name)
@@ -169,17 +170,17 @@ def rank_program(g, core, T, topo):
         act(col(name), col(src), f, r, [name], bias=col(bias) if isinstance(bias, str) else bias,
             scale=col(scale) if isinstance(scale, str) else scale)
 
-    def const(out, cols, value, r, w):
-        act(out, T.cnt[:, 0:cols], Fn.Identity, ["cnt0"] + r, w, bias=value, scale=0.0)
-
     def hold(out, src, cols, r, key):
-        scan(out, T.m16[:, 0:cols], src, Op.add, Op.max, r + ["m16"], [key])
+        scan(out, T.mm[:, 0:2 * cols:2], src, Op.add, Op.max, r + ["mm0", "mm2"], [key])
 
     def hold4(buf, src, cols, r, key):
-        scan(buf[:, 0:cols], T.m4[:, 0:cols], src, Op.add, Op.max, r + ["m40", "m41", "m42", "m43"], [key])
+        scan(buf[:, 0:cols], T.mm[:, 1:2 * cols:2], src, Op.add, Op.max, r + ["mm1"] + ["mm2"] * (cols > 64), [key])
+
+    def deal(out, src, r, key):
+        dma([("y", out[:, 16 * b:16 * b + 16], src[0:128:16, 256 * b:256 * b + 256]) for b in range(2)], r, [key])
 
     u32 = dt.uint32
-    xall = ["x0", "x1", "x2", "x3"]
+    xall = ["x0", "x1", "x2", "x3", "x4"]
     X = T.xb[:, 4 * XO:4 * (XO + C)]
 
     def quant_x():
@@ -192,14 +193,14 @@ def rank_program(g, core, T, topo):
     def copy_t(b):
         act(T.tp[:, 4 * OWN + b:4 * W:4], bank(b, 0, C), Fn.Copy, ["P%d" % b], ["to%d" % b], scale=0.015625)
 
-    def copy_out(q, out, b, cols, key):
+    def copy_out(q, out, b, lo, hi, key):
         if q == "v":
-            ts(out, bank(b, 0, cols), 0.015625, None, Op.mult, None, ["P%d" % b], [key])
+            ts(out, bank(b, lo, hi), 0.015625, None, Op.mult, None, ["P%d" % b], [key])
         else:
-            act(out, bank(b, 0, cols), Fn.Copy, ["P%d" % b], [key], scale=0.015625)
+            act(out, bank(b, lo, hi), Fn.Copy, ["P%d" % b], [key], scale=0.015625)
 
-    def copy_x(b, q="s"):
-        copy_out(q, T.xb[:, 4 * XO + b:4 * (XO + C):4], b, C, "x%d" % b)
+    def copy_x(b, q="s", lo=0, hi=C):
+        copy_out(q, T.xb[:, 4 * (XO + lo) + b:4 * (XO + hi):4], b, lo, hi, "x4" if lo else "x%d" % b)
 
     dma([("s", T.lin[:, 0:24], T.seat[:])], [], ["seat"])
     dma([("y" if i < 5 else "s", T.lin[16 * i:16 * i + 16, 24:48], T.alive[:]) for i in range(8)], [], ["alive"])
@@ -210,7 +211,7 @@ def rank_program(g, core, T, topo):
     alive = T.lin[:, 24:48]
 
     iota(T.pint[:, 0:1], [[0, 1]], 0, 1, [], ["pi"])
-    iota(T.cnt[:, 0:OWN], [[1, OWN]], 0, 0, [], ["cnt0"], True)
+    iota(T.turn[:, 96:160], [[0, 16], [4, 4]], 0, 0, [], ["four"], True)
     for odd in (1, 0):
         for a in range(4):
             di, dj = WAY[2 * a + odd]
@@ -222,104 +223,116 @@ def rank_program(g, core, T, topo):
                 be, ga = (bi, ga) if di < 0 else (-bi, ga + 5 * bi)
             entry = -1000 if di == 0 else (UP if di < 0 else DOWN) - (6 if dj else 0)
             iota(T.posi[32 * a:32 * a + 16 + 16 * odd, :], [[entry, 2], [be, 6], [16 * al, 4]], ga - 16 * al * odd, al,
-                 ["pi", "cnt0"], ["posi%d" % a], True)
+                 ["pi", "four"], ["posi%d" % a], True)
     posi_all = ["posi0", "posi1", "posi2", "posi3"]
-    whole(T.strip[:], 528, 0, posi_all, ["strip"])
-    diagonal = T.strip[:, 3:515:4]
-    op("g", lambda: g.affine_select(diagonal, diagonal, [[1, 128]], Op.not_equal, 64.0, 0, -1), ["strip"], ["strip"])
-    whole(T.xb[:, 0:4 * XO], 4 * XO, 0, [], ["xz"])
-    whole(T.comp[:, 256:512], 256, 0, [], ["compz"])
-    whole(T.dead[:, 0:OWN], OWN, 0, [], ["dead0"])
+    iota(T.turn[:, 32:96], [[0, 4], [1, 16]], 0, 0, posi_all, ["sixteen"], True)
 
     fill(T.ones[:], 1.0, ["ones"])
     for i, m in enumerate((15, 12, 3, 7)):
         ts(T.pint[:, 1 + i:2 + i], T.pint[:, 0:1], m, None, Op.bitwise_and, None, ["pi"], ["pi%d" % i])
-    op("v", lambda: V.tensor_tensor_scan(T.cnt[:, OWN:W], T.ones[:, 0:C], T.ones[:, 0:C], OWN - 1.0, Op.mult, Op.add),
-       ["ones"], ["cnt1"])
+    op("v", lambda: V.tensor_tensor_scan(T.cnt[:, 0:W // 2], T.ones[:], T.ones[:], -1.0, Op.mult, Op.add), ["ones"], ["cnt0"])
     act(T.two[:, 0:1], T.ones[:, 0:1], Fn.Copy, ["ones"], ["two0"], scale=-1 / EPS)
     act(T.two[:, 1:2], T.ones[:, 0:1], Fn.Copy, ["ones"], ["two1"], scale=BIG)
-    act(T.d0[:], T.ones[:], Fn.Copy, ["ones"], ["d0"], scale=-EPS)
-    cp(T.aliveu[:], alive, ["alive"], ["aliveu"])
-    cp(T.pf[:, 0:5], T.pint[:, 0:5], ["pi", "pi0", "pi1", "pi2", "pi3"], ["pf"])
-    tt(T.ni[:], T.two[:, 0:2].indirect(T.aliveu[:]), T.cnt[:, OWN:W], Op.min, ["two0", "two1", "aliveu", "cnt1"], ["ni"])
-    cp(T.seatu[:], T.lin[:, 0:24], ["seat"], ["seatu"])
-    small("c4a", "q3", Fn.Identity, 12 * K, 1.0)
-    small("offk", "q16", Fn.Identity, 15 * K, -K)
-    small("c4s", "q12", Fn.Identity, "c4a", -K)
-    small("sg", "q16", Fn.Sign, "p", -17.0)
-    ts(T.blk[:, 16:32], T.cnt[:, 0:16], col("q12"), -BIG, Op.is_equal, Op.mult, ["cnt0", "pf"], ["blk4"])
-    act(T.nis[:, 0:224], T.ni[:].indirect(T.seatu[:, 0:14]), Fn.Copy, ["ni", "seatu"], ["nis0"], scale=-EPS)
-    ts(T.nis[:, 224:C], T.ni[:].indirect(T.seatu[:, 14:24]), -EPS, None, Op.mult, None, ["ni", "seatu"], ["nis1"])
-    cp(T.posu[:], T.posi[:, 0:24], posi_all, ["posu"])
-    ts(T.tmp[:, 0:69], T.cnt[:, 0:69], T.posi[:, 24:25], T.posi[:, 0:1], Op.add, Op.subtract, ["cnt0"] + posi_all, ["tmp0"])
-    cp(T.d0[:].indirect(T.posu[:]), T.nis[:], ["nis0", "nis1", "posu"], ["d0"])
-    cnt_all = ["cnt0", "cnt1"]
-    act(T.blk[:, 16:32], T.blk[:, 16:32], Fn.Identity, ["blk4"], ["blk4"], bias=K * EPS)
-    act(T.tmp[:, 72:141], T.tmp[:, 0:69], Fn.Copy, ["tmp0"], ["tmp1"], scale=-EPS)
-    for h, least in enumerate((1, DOWN)):
-        act(T.tmp[64 * h:64 * h + 64, 144:213], T.tmp[64 * h:64 * h + 64, 0:69], Fn.Relu, ["tmp0"], ["tmp2%d" % h],
-            bias=least - 0.5, scale=-1.0)
-    for b in range(4):
-        const(T.m4[:, b:C:4], C // 4, T.blk[:, 16 + 4 * b:17 + 4 * b], ["blk4"], ["m4%d" % b])
-    small("c4c", "c4s", Fn.Identity, -4.0 * (OWN - XO), 1.0)
-    act(T.posf[:], T.cnt[:, 0:W].indirect(T.posu[:]), Fn.Copy, cnt_all + ["posu"], ["posf"])
-    tt(T.tmp[:, 72:141], T.tmp[:, 72:141], T.tmp[:, 144:213], Op.add, ["tmp1", "tmp20", "tmp21"], ["tmp1"])
-    ts(T.q16u[:], T.cnt[:, 0:24], 0.0, col("q16"), Op.mult, Op.add, ["cnt0", "pf"], ["q16u"])
-    tt(T.d0[:, 0:483:7], T.d0[:, 0:483:7], T.tmp[:, 72:141], Op.min, ["tmp1", "d0"], ["d0"])
-    ts(T.blk[:, 0:16], T.cnt[:, 0:16], col("q16"), -BIG, Op.is_equal, Op.mult, ["cnt0", "pf"], ["blk"])
-    dead_all = ["dead0", "deadA", "deadB"]
+    for h in range(2):
+        act(T.d0[:, 256 * h:256 * h + 256], T.ones[:, 0:256], Fn.Copy, ["ones"], ["d0%d" % h], scale=-EPS)
+        if h == 0:
+            act(T.strip[:, 0:264], T.ones[:, 0:264], Fn.Copy, ["ones"], ["strip0"], scale=0.0)
+            act(T.cnt[:, W // 2:W], T.cnt[:, 0:W // 2], Fn.Identity, ["cnt0"], ["cnt1"], bias=float(W // 2))
+    whole(T.xb[:, 0:4 * XO], 4 * XO, 0, posi_all, ["xz"])
+    whole(T.comp[:, 256:512], 256, 0, [], ["compz"])
+    iota(T.turn[:, 0:32], [[256, 2], [1, 16]], 0, 0, [], ["turn"], True)
 
     def unpacker(b):
         quant(*part(T.eq, T.es, b), T.strip[:, 3 - b:515 - b], ["strip"], ["e%d" % b])
 
+    cp(T.pf[:, 0:5], T.pint[:, 0:5], ["pi", "pi0", "pi1", "pi2", "pi3"], ["pf"])
+    fill(T.uu[:, 0:8], 1, ["uu0"])
+    ts(T.mm[:, 1:128:2], T.turn[:, 96:160], col("q12"), -BIG, Op.is_equal, Op.mult, ["four", "pf"], ["mm1"])
+    act(T.mm[:, 1:128:2], T.mm[:, 1:128:2], Fn.Identity, ["mm1"], ["mm1"], bias=K * EPS)
+    ts(T.uu[:, 8:16], T.cnt[:, 0:8], col("q7"), 16.0, Op.max, Op.mult, ["cnt0", "pf"], ["uu1"])
+    ts(T.uu[:, 16:24], T.cnt[:, 0:8], col("q7"), 16.0, Op.min, Op.mult, ["cnt0", "pf"], ["uu2"])
+    cp(T.aliveu[:], alive, ["alive"], ["aliveu"])
+    cp(T.seatu[:], T.lin[:, 0:24], ["seat"], ["seatu"])
+    tt(T.ni[:], T.two[:, 0:2].indirect(T.aliveu[:]), T.cnt[:, OWN:W], Op.min, ["two0", "two1", "aliveu", "cnt0", "cnt1"], ["ni"])
+    act(T.strip[:, 264:528], T.ones[:, 0:264], Fn.Copy, ["ones"], ["strip1"], scale=0.0)
+    act(T.nis[:, 0:256], T.ni[:].indirect(T.seatu[:, 0:16]), Fn.Copy, ["ni", "seatu"], ["nis0"], scale=-EPS)
+    ts(T.tmp[:, 0:69], T.cnt[:, 0:69], T.posi[:, 24:25], T.posi[:, 0:1], Op.add, Op.subtract, ["cnt0"] + posi_all, ["tmp0"])
+    cp(T.posu[:], T.posi[:, 0:24], posi_all, ["posu"])
+    ts(T.nis[:, 256:C], T.ni[:].indirect(T.seatu[:, 16:24]), -EPS, None, Op.mult, None, ["ni", "seatu"], ["nis1"])
+    ts(T.d0[:, 0:483:7], T.tmp[:, 0:69], -EPS, -EPS, Op.mult, Op.min, ["tmp0", "d00", "d01"], ["d0"])
+    ts(T.mm[:, 0:128:2], T.turn[:, 32:96], col("q16"), -BIG, Op.is_equal, Op.mult, ["sixteen", "pf"], ["mm0"])
+    cp(T.d0[:].indirect(T.posu[:]), T.nis[:], ["nis0", "nis1", "posu"], ["d0"])
+    small("c4a", "q3", Fn.Identity, 12 * K, 1.0)
+    act(T.mm[:, 0:128:2], T.mm[:, 0:128:2], Fn.Identity, ["mm0"], ["mm0"], bias=K)
+    small("c4s", "q12", Fn.Identity, "c4a", -K)
+    small("q256", "q16", Fn.Identity, 0.0, 16.0)
+    dma([("y", T.mm[:, 128 * i:128 * i + 128], T.mm[:, 0:128]) for i in range(1, 6)], ["mm0", "mm1"], ["mm2"])
+    diagonal = T.strip[:, 3:515:4]
+    op("g", lambda: g.affine_select(diagonal, diagonal, [[1, 128]], Op.not_equal, 64.0, 0, -1), ["strip0", "strip1"], ["strip"])
+    whole(T.dead[:, 0:OWN], OWN, 0, [], ["dead0"])
+    whole(T.pc[:, C:512], 512 - C, 0, [], ["pcz"])
+    whole(T.wts[:, 3:512:4], 128, 0, [], ["wv3"])
+    whole(T.fw[:, 0:1], 1, 0, [], ["fwz"])
+    whole(T.tp[:, 0:4 * UP], 4 * UP, 0, [], ["tz"])
+    whole(T.tp[:, 4 * GAP:4 * OWN], 4 * (OWN - GAP), 0, [], ["tg"])
+    act(T.posf[:], T.cnt[:, 0:W].indirect(T.posu[:]), Fn.Copy, ["cnt0", "cnt1", "posu"], ["posf"])
+    small("c4c", "c4s", Fn.Identity, -4.0 * (OWN - XO), 1.0)
+    small("sg", "q16", Fn.Sign, "p", -17.0)
+    small("offk", "q16", Fn.Identity, 15 * K, -K)
+    small("sg32", "sg", Fn.Identity, 0.0, 32.0)
+    small("pens", "sg", Fn.Identity, 0.0, BIG / 256)
+    small("offb", "offk", Fn.Identity, OWN - 16.0, 1.0)
+    quant(T.uq[:], T.up[:], T.ub[:], ["ub"], ["uq"])
+    act(T.up2[:], T.up[:].indirect(T.uu[:]), Fn.Copy, ["uq", "uu0", "uu1", "uu2"], ["u2b"])
+    dead_all = ["dead0", "deadA", "deadB"]
+
+    def later_constants():
+        for b in range(3):
+            whole(T.wts[:, b:512:4], 128, 1, [], ["wv%d" % b])
+        op("g", lambda: g.affine_select(T.tri[:], T.ones[:, 0:128], [[1, 128]], Op.is_gt, 0.0, 0, -1), ["ones"], ["tri"])
+        for b in range(2):
+            whole(T.wts[:, 512 + b:1026:4], 129, 0, [], ["wk%d" % b])
+        whole(T.win[:, 0:16], 16, 0, [], ["winz"])
+
     def arrived(b, q):
-        copy_out(q, T.tp[:, 4 * UP + b:4 * GAP:4], 4 + b, 128, "ta%d" % b)
+        copy_out(q, T.tp[:, 4 * UP + b:4 * GAP:4], 4 + b, 0, LAND, "ta%d" % b)
 
     t_all = ["tz", "tg"] + ["ta%d" % b for b in range(4)] + ["to%d" % b for b in range(4)]
 
     def gather_z(q, lo, hi, key):
         move(q, T.z[:, 4 * lo:4 * hi], T.tp[:].indirect(T.su[:, lo // 4:hi // 4]), t_all + ["su"], [key])
 
-    def name_weights():
-        for b, o, x in ((2, Op.is_equal, -2.0 ** -15), (3, Op.not_equal, 2.0 ** -12)):
-            ts(T.wts[:, 512 + b:1026:4], T.comp[:, 256:384], col("q16"), x, o, Op.mult, ["compz", "pf"], ["wk%d" % b])
+    def name_weights(b):
+        o, x = (Op.is_equal, -2.0 ** -15) if b == 2 else (Op.not_equal, 2.0 ** -12)
+        ts(T.wts[:, 512 + b:1026:4], T.comp[:, 256:384], col("q16"), x, o, Op.mult, ["compz", "pf"], ["wk%d" % b])
 
-    def weights():
-        whole(T.tp[:, 0:4 * UP], 4 * UP, 0, [], ["tz"])
-        whole(T.tp[:, 4 * GAP:4 * OWN], 4 * (OWN - GAP), 0, [], ["tg"])
-        whole(T.fw[:, 0:1], 1, 0, [], ["fwz"])
-        op("g", lambda: g.affine_select(T.tri[:], T.ones[:, 0:128], [[1, 128]], Op.is_gt, 0.0, 0, -1), ["ones"], ["tri"])
-        for b in range(4):
-            whole(T.wts[:, b:512:4], 128, int(b < 3), [], ["wv%d" % b])
-        for b in range(2):
-            whole(T.wts[:, 512 + b:1026:4], 129, 0, [], ["wk%d" % b])
+    def name_tile(h):
+        quant(*part(T.kq, T.ks, 1 + h), T.wts[:, 514 - 2 * h:1026 - 2 * h], ["wk0", "wk1", "wk2", "wk3"], ["kq%d" % h])
 
-    def penalty(q):
-        if q == "v":
-            ts(T.pen[:], T.sees[:], (0.5 - OWN) * EPS, col("pens"), Op.is_gt, Op.mult, ["sees", "pens"], ["pen"])
-        else:
-            act(T.far[:], T.sees[:], Fn.Relu, ["sees"], ["far"], bias=OWN - 0.5, scale=1 / EPS)
-            act(T.pen[:], T.far[:], Fn.Identity, ["far", "pens"], ["pen"], scale=col("pens"))
+    def penalty(lo, hi):
+        ts(T.pen[:, 128 * lo:128 * hi], T.sees[:, 128 * lo:128 * hi], (0.5 - OWN) * EPS, col("pens"), Op.is_gt, Op.mult,
+           ["sees", "pens"], ["pen%d" % k for k in range(lo, hi)])
 
-    def backward(d, dk, i, parts=4):
-        hi = LS - 1 - i * LS // parts
-        src = d[:, hi:hi - LS // parts:-1] if i < parts - 1 else d[:, hi::-1]
+    def backward(d, dk, i, cuts):
+        hi, lo = cuts[i] - 1, cuts[i + 1] - 1
+        src = d[:, hi:lo:-1] if lo >= 0 else d[:, hi::-1]
         start = T.bw[:, hi + 8:hi + 9] if i else 0.0
-        op("v", lambda: V.tensor_tensor_scan(T.bw[:, hi + 7:hi + 7 - LS // parts:-1], src, src, start, Op.mult, Op.min),
-           [dk] + ["bw%d" % (i - 1)] * (i > 0), ["bw%d" % i])
-
-    def hold_lines(i):
-        lo, hi = 128 * i, min(LL, 128 * i + 128)
-        hold(T.ext3[:, lo:hi], T.idl[:, lo:hi], hi - lo, ["idl"], "ext3%d" % i)
+        op("v", lambda: V.tensor_tensor_scan(T.bw[:, hi + 7:lo + 7:-1], src, src, start, Op.mult, Op.min),
+           [dk, "d2"] + ["bw%d" % (i - 1)] * (i > 0), ["bw%d" % i])
 
     def seen_by():
-        act(T.back[:], T.bw[:, 8:LS + 7].indirect(T.pu[:]), Fn.Copy, ["bw3", "bw2", "bw1", "bw0", "pu"], ["back"], scale=-1 / EPS)
-
-    def hold_back():
-        hold(T.ext2[:], T.back[:], C, ["back"], "ext2")
+        act(T.back[:], T.bw[:, 8:LS + 7].indirect(T.pv[:]), Fn.Copy, ["bw3", "bw2", "bw1", "bw0", "pv"], ["back"], scale=-1 / EPS)
+        deal(T.backw, T.back, ["back"], "backw")
 
     def take_back():
-        ts(T.bu[:], T.ext2[:, 15:C:16], col("offb"), None, Op.subtract, None, ["ext2", "offb"], ["bu"])
+        ts(T.bu[:], T.backw[:, 0:24], OWN - 16.0, None, Op.subtract, None, ["backw"], ["bu"])
+
+    def slots(lo, hi, key):
+        tt(T.d1[:, lo:hi], T.dead[:].indirect(T.lu[:, lo // 16:hi // 16]), T.d0[:, lo:hi], Op.add, dead_all + ["lu", "d0"], [key])
+
+    def forward_rest(d):
+        op("v", lambda: V.tensor_tensor_scan(T.fw[:, SENT + 1:LS + 1], d[:, SENT:LS], d[:, SENT:LS],
+                                             T.fw[:, SENT:SENT + 1], Op.mult, Op.min), ["d2", "fw"], ["fw2"])
 
     def dead_along_partitions():
         dma([("y", T.lt[:, k:k + 1], T.dead[0:1, OWN + 128 * k:OWN + 128 * k + 128]) for k in range(3)], dead_all, ["lt"])
@@ -328,22 +341,28 @@ def rank_program(g, core, T, topo):
         first, last = t == 0, t == R - 1
         d, dk = (T.d0, "d0") if first else (T.d1, "d1")
         if not first:
-            tt(d[:], T.dead[:].indirect(T.lu[:, 0:31]), T.d0[:], Op.add, dead_all + ["lu", "d0"], [dk])
+            if t == 1:
+                cp(T.pv[:], T.pw[:], ["pw"], ["pv"])
+            slots(0, SENT, dk)
+            slots(SENT, LL, "d2")
             dead_along_partitions()
-            for b in range(3):
-                copy_t(b)
-                if b == 1:
-                    act(T.life[:], T.dead[:, OWN:W], Fn.Identity, dead_all, ["life"], bias=1.0, scale=-1.0)
-        else:
-            act(T.m16[:], T.blk[:, 0:16].indirect(T.q16u[:]), Fn.Identity, ["blk", "q16u"], ["m16"], bias=K)
+            copy_t(0)
+            copy_t(1)
+            act(T.life[:], T.dead[:, OWN:W], Fn.Identity, dead_all, ["life"], bias=1.0, scale=-1.0)
 
         def between(i):
-            if first:
+            if first and i < 3:
                 unpacker(i)
+            elif first:
+                unpacker(3)
+                ts(T.turnu[:], T.turn[:, 0:32], col("q256"), None, Op.add, None, ["turn", "q256"], ["turnu"])
+            elif i == 1:
+                forward_rest(d)
             else:
-                backward(d, dk, i)
+                backward(d, dk, max(i - 1, 0), BACK)
 
-        scan(T.fw[:, 1:LS + 1], d[:, 0:LS], d[:, 0:LS], Op.mult, Op.min, [dk], ["fw"])
+        now = LS if first else SENT
+        scan(T.fw[:, 1:now + 1], d[:, 0:now], d[:, 0:now], Op.mult, Op.min, [dk], ["fw"])
         between(0)
         hold4(T.c64, T.fw[:, 7:455:7], 64, ["fw"], "c64")
         between(1)
@@ -361,7 +380,7 @@ def rank_program(g, core, T, topo):
             for i, to in enumerate((below, above)):
                 half = topo.engines(core, to)[i::2]
                 rid, pid = topo.addr(to)[:2]
-                a, b = src[:, 0:64], dst[:, 64 * i:64 * i + 64]
+                a, b = src[:, 0:64], dst[:, (DOWN - UP) * i:(DOWN - UP) * i + 64]
                 if codes:
                     a, b = a.bitcast(dt.uint8), b.bitcast(dt.uint8)
                 moves.append(RemoteDMATransfer(dst_ids=[DstId(rid=rid, pnc=pid)], dma_engine_mask=sum(1 << e for e in half),
@@ -374,55 +393,54 @@ def rank_program(g, core, T, topo):
 
         def unpack_arrived():
             for b in range(4):
-                mm(4 + b, 128, *part(T.eq, T.es, b), lq[:], lp[:], ["e%d" % b, "land"])
+                mm(4 + b, LAND, *part(T.eq, T.es, b), lq[:], lp[:], ["e%d" % b, "land", "landz%d" % t])
 
         if first:
-            weights()
-            whole(T.win[:, 0:16], 16, 0, [], ["winz"])
             act(T.dead[:, OWN:W], T.ni[:], Fn.Relu, ["ni"], ["deadA", "deadB"], scale=-EPS)
+            act(T.idl[:], T.d0[:].indirect(T.turnu[:]), Fn.Relu, ["d0", "turnu"], ["idl"], scale=-1 / EPS)
+            for i in range(R):
+                dma([("y", T["lq%d" % i][:, 64:DOWN - UP].bitcast(dt.uint8), sq[:, 64:DOWN - UP].bitcast(dt.uint8)),
+                     ("y", T["lp%d" % i][:, 64:DOWN - UP], sp[:, 64:DOWN - UP])], ["sq0"], ["landz%d" % i])
             dead_along_partitions()
+            deal(T.lw, T.idl, ["idl"], "lw")
+            later_constants()
             quant_x()
             unpack_own(True)
-            act(T.idl[:], T.d0[:], Fn.Relu, ["d0"], ["idl"], scale=-1 / EPS)
-            small("pens", "sg", Fn.Identity, 0.0, BIG / 256)
             for b in range(4):
                 copy_t(b)
-            small("sg32", "sg", Fn.Identity, 0.0, 32.0)
-            cp(T.pc[:].indirect(T.seatu[:]), T.posf[:], ["posf", "seatu"], ["pc"])
-            quant(T.uq[:], T.up[:], T.ub[:], ["ub"], ["uq"])
-            hold(T.ext[:, 0:C], T.pc[:], C, ["pc"], "ext")
-            ts(T.uu[:, 8:16], T.cnt[:, 0:8], col("q7"), 16.0, Op.max, Op.mult, ["cnt0", "pf"], ["uu1"])
+            cp(T.pc[:, 0:C].indirect(T.seatu[:]), T.posf[:], ["posf", "seatu"], ["pc"])
+            deal(T.pw, T.pc, ["pc", "pcz"], "pw")
+            name_weights(3)
+            hold(T.ext[:, 0:C], T.pc[:, 0:C], C, ["pc"], "ext")
+            ts(T.wts[:, 3:512:64], T.cnt[:, 0:8], col("q16"), col("sg32"), Op.is_equal, Op.mult, ["cnt0", "pf", "sg32"], ["wv3"])
             tt(T.jw[:], T.ext[:, 15:C:16], alive, Op.mult, ["ext", "alive"], ["jw"])
-            ts(T.uu[:, 16:24], T.cnt[:, 0:8], col("q7"), 16.0, Op.min, Op.mult, ["cnt0", "pf"], ["uu2"])
+            name_weights(2)
             ts(T.pu[:], T.jw[:], col("offk"), None, Op.subtract, None, ["jw", "offk"], ["pu"])
-            fill(T.uu[:, 0:8], 1, ["uu0"])
             unpack_arrived()
-            act(T.sees[:], T.fw[:, 0:LS + 1].indirect(T.pu[:]), Fn.Copy, ["fw", "fwz", "pu"], ["sees"])
-            ts(col("zp"), col("q16"), 0.0, col("p"), Op.is_equal, Op.mult, ["pf"], ["zp"])
+            unpack_own(False)
+            act(T.sees[:], T.fw[:, 0:LS + 1].indirect(T.pu[:]), Fn.Copy, ["fw", "fw2", "fwz", "pu"], ["sees"])
             cp(T.uq2[:].bitcast(u32), T.uq[:].bitcast(u32).indirect(T.uu[:]), ["uq", "uu0", "uu1", "uu2"], ["u2a"])
-            hold4(T.ext, T.sees[:], C, ["sees"], "ext")
-            name_weights()
+            ts(col("zp"), col("q16"), 0.0, col("p"), Op.is_equal, Op.mult, ["pf"], ["zp"])
         else:
+            copy_t(2)
             copy_t(3)
             unpack_own(False)
+            backward(d, dk, 3, BACK)
             seen_by()
-            tt(T.sees[:], T.fw[:, 0:LS + 1].indirect(T.pu[:]), T.life[:], Op.mult, ["fw", "fwz", "pu", "life"], ["sees"])
-            if t == 1:
-                quant(T.vq[:], T.vp[:], T.vb[:], ["vb"], ["vq"])
-            hold4(T.ext, T.sees[:], C, ["sees"], "ext")
-            penalty("v")
+            tt(T.sees[:], T.fw[:, 0:LS + 1].indirect(T.pu[:]), T.life[:], Op.mult, ["fw", "fw2", "fwz", "pu", "life"], ["sees"])
+        if t == 1:
+            quant(T.vq[:], T.vp[:], T.vb[:], ["vb"], ["vq"])
+        hold4(T.ext, T.sees[:], C, ["sees"], "ext")
+        penalty(0, 1 if first else 3)
         ts(T.su[:], T.ext[:, 3:C:4], -4 / EPS, col("c4s"), Op.mult, Op.add, ["ext", "c4s"], ["su"])
         act(T.pt[:, 0:3], T.lt[:, 0:3], Fn.Identity, ["lt"], ["pt"], scale=-BIG)
         if first:
-            for b in range(4):
-                arrived(b, "s")
-            unpack_own(False)
-            penalty("v")
+            ts(col("thv"), col("zp"), -2.0, 31.5, Op.mult, Op.add, ["zp"], ["thv"])
+            quant(*part(T.kq, T.ks, 0), T.wts[:, 0:512], ["wv0", "wv1", "wv2", "wv3"], ["kq"])
         else:
-            hold_back()
             unpack_arrived()
-            for b in range(4):
-                arrived(b, "vssv"[b])
+        for b in range(4):
+            arrived(b, "s" if first else "vssv"[b])
         uk = ["u2a", "u2b"]
         zk = ["zq0", "zq1", "zq2"]
 
@@ -435,20 +453,19 @@ def rank_program(g, core, T, topo):
         def score(k, b):
             act(T.sc[:, k:k + 1], bank(b, 0, 1), Fn.Identity, ["P%d" % b, "pt"], ["sc%d" % k], bias=T.pt[:, k:k + 1])
 
-        def step_up(lo, hi):
-            act(T.dl[:, lo:hi], T.ps[:, 2048:2048 + 512 * (hi - lo):512], Fn.Abs, ["P4", "P5"][:hi - lo],
-                ["dl%d" % k for k in range(lo, hi)], bias=2.0 ** -122, scale=1.25 * 2.0 ** -24)
+        def step_up(k, b):
+            act(T.dl[:, k:k + 1], bank(b, 0, 1), Fn.Abs, ["P%d" % b], ["dl%d" % k], bias=2.0 ** -122, scale=1.25 * 2.0 ** -24)
 
         def threshold(k):
             act(T.thr[:, 128 * k:128 * k + 128], T.tri[:], Fn.Identity, ["tri", "sc%d" % k, "dl%d" % k], ["thr%d" % k],
                 bias=T.sc[:, k:k + 1], scale=T.dl[:, k:k + 1])
 
-        def pairs(lo, hi, r):
-            for i in (1, 2):
-                mm(5 + i, hi - lo, *part(T.uq2, T.up2, i), T.zq[:, lo:hi], T.zp[:, lo:hi], uk + r)
+        def pair(i, lo, hi, r):
+            mm(5 + i, hi - lo, *part(T.uq2, T.up2, i), T.zq[:, lo:hi], T.zp[:, lo:hi], uk + r)
 
         def lowered(lo, hi, key):
-            tt(T.xs[:, lo:hi], bank(6, 0, hi - lo), T.pen[:, lo:hi], Op.add, ["P6", "pen"], ["xs" + key])
+            tt(T.xs[:, lo:hi], bank(6, 0, hi - lo), T.pen[:, lo:hi], Op.add,
+               ["P6"] + ["pen%d" % k for k in range(lo // 128, hi // 128)], ["xs" + key])
 
         def ahead(lo, hi, key):
             tt(T.cm[:, 4 * lo + 3:4 * hi:4], bank(7, 0, hi - lo), T.xs[:, lo:hi], Op.is_gt, ["P7", "xs" + key], ["cma" + key])
@@ -468,109 +485,114 @@ def rank_program(g, core, T, topo):
 
         gather_z("v", 0, 128, "za")
         gather_z("s", 128, 256, "zb")
+        gather_z("s", 256 if first else 296, C, "zd")
         if first:
-            act(T.up2[:], T.up[:].indirect(T.uu[:]), Fn.Copy, ["uq", "uu0", "uu1", "uu2"], ["u2b"])
-        cut = 272 if first else 304
-        gather_z("s", cut, C, "zd")
-        if first:
-            hold_lines(0)
+            penalty(1, 2)
         quant_z(0, ["za"])
-        along_partitions(0, 4)
+        along_partitions(0, 5)
         quant_z(1, ["zb"])
-        along_partitions(1, 5)
-        pairs(0, 256, zk[:2])
-        gather_z("v", 256, cut, "zc")
+        pair(1, 0, 256, zk[:2])
+        along_partitions(1, 4)
+        pair(2, 0, 256, zk[:2])
         if first:
-            backward(d, dk, 0, 1)
-            hold_lines(1)
-        step_up(0, 2)
-        score(1, 5)
-        score(0, 4)
-        threshold(1)
+            backward(d, dk, 0, (LS, 0))
+        else:
+            gather_z("v", 256, 296, "zc")
+        score(0, 5)
+        step_up(0, 5)
+        score(1, 4)
+        step_up(1, 4)
         quant_z(2, ["zc", "zd"])
         mm(5, C, *part(T.uq2, T.up2, 0), T.zq[:], T.zp[:], uk + zk)
         along_partitions(2, 4)
         threshold(0)
-        if first:
-            seen_by()
+        threshold(1)
         score(2, 4)
-        step_up(2, 3)
+        step_up(2, 4)
+        if first:
+            act(T.back[:, 0:C], T.bw[:, 8:LS + 7].indirect(T.pu[:]), Fn.Copy, ["bw0", "pu"], ["back"], scale=-1 / EPS)
         layer(0)
         copy_x(0)
         threshold(2)
         lowered(0, 256, "A")
         if first:
-            ts(T.wts[:, 3:512:64], T.cnt[:, 0:8], col("q16"), col("sg32"), Op.is_equal, Op.mult, ["cnt0", "pf", "sg32"], ["wv3"])
+            penalty(2, 3)
         else:
             take_back()
         ahead(0, 256, "A")
+        pair(2, 256, C, zk[2:])
+        pair(1, 256, C, zk[2:])
         layer(1)
-        pairs(256, C, zk[2:])
         layer(2)
-        if not first:
+        if last:
             layer(3)
-        if first:
-            quant(*part(T.kq, T.ks, 0), T.wts[:, 0:512], ["wv0", "wv1", "wv2", "wv3"], ["kq"])
-            small("thv", "zp", Fn.Identity, 31.5, -2.0)
-            small("offb", "offk", Fn.Identity, OWN - 16.0, 1.0)
-        beats(0, 128, 256, 0, Op.is_le, "cm1")
         beats(1, 0, 128, 0, Op.is_lt, "cm2")
-        beats(2, 0, 256, 1, Op.is_lt, "cm0")
+        beats(0, 128, C, 0, Op.is_le, "cm1")
         beats_near(0, 256, ["thr0", "thr1"], "A")
+        beats(2, 0, 256, 1, Op.is_lt, "cm0")
         lowered(256, C, "B")
         count_part(0, 256, 4, ["cm0", "cm1", "cm2"], "A")
-        if first:
+        if not last:
             layer(3)
-        beats(0, 256, C, 0, Op.is_le, "cm3")
         ahead(256, C, "B")
         beats(1, 256, C, 1, Op.is_le, "cm4")
         beats_near(256, C, ["thr2"], "B")
         if first:
-            hold_lines(2)
-        count_part(256, C, 6, ["cm3", "cm4"], "B")
+            name_tile(0)
+        count_part(256, C, 6, ["cm1", "cm4"], "B")
         for b in (1, 2):
             copy_x(b)
         if first:
-            hold_back()
+            hold(T.ext[:], T.back[:, 0:C], C, ["back"], "ext")
+        elif last:
+            copy_x(3)
         else:
-            copy_x(3, "s" if last else "v")
+            copy_x(3, "v", 0, 256)
         act(T.win[:, 16:16 + 256], bank(4, 0, 256), Fn.Relu, ["P4", "thv"], ["winA"], bias=col("thv"), scale=-1.0)
         act(T.kt[:, 1:512:2], bank(4, 0, 256), Fn.Relu, ["P4", "thv"], ["ktA"], bias=col("thv"), scale=-1.0)
+        if not first and not last:
+            copy_x(3, "s", 256, C)
+
+        def last_codes(h, lo, hi):
+            quant(T.xq[:, lo:hi], T.xp[:, lo:hi], T.xb[:, 4 * (XO + lo):4 * (XO + hi)], xall, ["xq%d" % h] + ["xq"] * (1 - h))
+            mm(h, hi - lo, T.vq[:], T.vp[:], T.xq[:, lo:hi], T.xp[:, lo:hi], ["vq", "xq%d" % h])
+            dma([("y", T.oc[:, 4 * lo:4 * hi], T.xq[:, lo:hi].bitcast(dt.uint8))], ["xq%d" % h], [])
+
+        def last_product(q, h, lo, hi):
+            move(q, T.yb[:, lo:hi], bank(h, 0, hi - lo), ["P%d" % h], ["yb%d" % h])
+            dma([("y", T.y[:, lo:hi], T.yb[:, lo:hi])], ["yb%d" % h], [])
+
         if last:
-            quant_x()
-            mm(0, C, T.vq[:], T.vp[:], T.xq[:], T.xp[:], ["vq", "xq"])
-            dma([("y", T.oc[:], T.xq[:].bitcast(dt.uint8))]
-                + [("y", T.osc[4 * k:4 * k + 4, :], T.xp[32 * k:32 * k + 4, :]) for k in range(4)], ["xq"], [])
+            last_codes(0, 0, 256)
         ts(T.win[:, 16 + 256:16 + C], bank(6, 0, 128), col("thv"), None, Op.is_lt, None, ["P6", "thv"], ["winB"])
         if first:
-            take_back()
+            ts(T.bu[:], T.ext[:, 15:C:16], col("offb"), None, Op.subtract, None, ["ext", "offb"], ["bu"])
         ts(T.kt[:, 513:2 * C:2], bank(6, 0, 128), col("thv"), None, Op.is_lt, None, ["P6", "thv"], ["ktB"])
-        for q, lo, hi, key in (("s", 224, C, "kt1"), ("v", 0, 224, "kt0")):
+        for q, lo, hi, key in (("s", 192, C, "kt1"), ("v", 0, 192, "kt0")):
             move(q, T.kt[:, 2 * lo:2 * hi:2], T.win[:].indirect(T.bu[:, lo // 16:hi // 16]), ["winz", "winA", "winB", "bu"], [key])
         if last:
-            act(T.yb[:], bank(0, 0, C), Fn.Copy, ["P0"], ["yb"])
-            dma([("s", T.y[:], T.yb[:])], ["yb"], [])
+            last_codes(1, 256, C)
+            last_product("s", 0, 0, 256)
         if first:
             copy_x(3)
-            for h in range(2):
-                quant(*part(T.kq, T.ks, 1 + h), T.wts[:, 514 - 2 * h:1026 - 2 * h], ["wk0", "wk1", "wk2", "wk3"], ["kq%d" % h])
+            name_tile(1)
         quant(T.ktq[:], T.ktp[:], T.kt[:], ["kt0", "kt1", "ktA", "ktB"], ["ktq"])
         for h in range(2):
             mm(6 + h, C // 2, *part(T.kq, T.ks, 1 + h), T.ktq[:], T.ktp[:], ["kq%d" % h, "ktq"])
-        if not last:
+        if first:
+            cp(T.lu[:], T.lw[:], ["lw"], ["lu"])
+        if last:
+            last_product("v", 1, 256, C)
+            dma([("s", T.osc[4 * k:4 * k + 4, :], T.xp[32 * k:32 * k + 4, :]) for k in range(4)], ["xq0", "xq1"], [])
+        else:
             quant_x()
             unpack_own(True)
-        if first:
-            hold_lines(3)
         for h, key in enumerate(("deadA", "deadB")):
             was = T.dead[:, OWN + h:W:2]
             if last:
                 tt(T.life[:, h:C:2], bank(6 + h, 0, C // 2), was, Op.is_ge, ["P%d" % (6 + h), key], ["life%d" % h, "life"][:2 - h])
             else:
                 tt(was, bank(6 + h, 0, C // 2), was, Op.is_lt, ["P%d" % (6 + h), key], [key])
-            if first and h == 0:
-                ts(T.lu[:, 0:31], T.ext3[:, 15:LL:16], col("offk"), None, Op.subtract, None,
-                   ["ext30", "ext31", "ext32", "ext33", "offk"], ["lu"])
     dma([("y", T.ol[:], T.life[0:1, :])], ["life0", "life1"], [])
     for sem in count:
         need("g", (sem, count[sem], {}))

@@ -8,8 +8,9 @@ LAND = GAP - UP
 XO = 4
 LL, LS = 496, 484
 SENT = 7 * A
-BACK = (LS, 420, 356, 228, 0)
-K, BIG, EPS = 1024.0, 1e29, 2.0 ** -36
+CUT = 280
+TRIO = 40
+K, BIG, EPS = 2048.0, 1e29, 2.0 ** -36
 X4, U8 = "float8_e4m3fn_x4", "uint8"
 
 
@@ -19,27 +20,29 @@ def _sb(n, d):
 
 SCRATCH = {
     "ps": ("psum", [128, 4096], "float32"),
-    "cnt": _sb(W, "float32"), "pint": _sb(8, "int32"), "pf": _sb(32, "float32"), "ones": _sb(W // 2, "bfloat16"),
-    "two": _sb(8, "float32"), "tmp": _sb(72, "float32"), "mm": _sb(768, "float32"), "turn": _sb(160, "float32"),
+    "cnt": _sb(W, "float32"), "pint": _sb(8, "int32"), "pf": _sb(16, "float32"), "ones": _sb(W // 2, "bfloat16"),
+    "two": _sb(8, "float32"), "tmp": _sb(72, "float32"), "mm": _sb(256, "float32"), "turn": _sb(160, "float32"),
     "turnu": _sb(32, "uint16"), "posi": _sb(48, "float32"), "posu": _sb(24, "uint16"), "posf": _sb(C, "float32"),
-    "tri": _sb(128, "bfloat16"), "strip": _sb(528, "bfloat16"), "wts": _sb(1032, "bfloat16"),
-    "eq": _sb(512, X4), "es": _sb(512, U8), "kq": _sb(384, X4), "ks": _sb(384, U8),
+    "strip": _sb(528, "bfloat16"), "wts": _sb(1024, "bfloat16"), "cells": _sb(C, "bfloat16"),
+    "eq": _sb(512, X4), "es": _sb(512, U8), "kq": _sb(256, X4), "ks": _sb(256, U8),
     "lin": _sb(48, "int32"), "seatu": _sb(24, "uint16"), "aliveu": _sb(24, "uint16"), "jw": _sb(24, "float32"),
     "ni": _sb(C, "float32"), "nis": _sb(C, "float32"),
     "d0": _sb(512, "float32"), "d1": _sb(LL, "float32"), "idl": _sb(512, "float32"), "lw": _sb(32, "float32"),
-    "ext": _sb(C, "float32"), "lu": _sb(32, "uint16"), "pc": _sb(512, "float32"), "pu": _sb(24, "uint16"),
-    "pw": _sb(32, "float32"), "pv": _sb(32, "uint16"), "dead": _sb(W, "float32"), "life": _sb(C, "float32"),
-    "fw": _sb(512, "float32"), "bw": _sb(512, "float32"), "c64": _sb(64, "float32"), "cu": _sb(16, "uint16"),
-    "sees": _sb(C, "float32"), "su": _sb(96, "uint16"), "back": _sb(512, "float32"), "bu": _sb(24, "uint16"),
-    "backw": _sb(32, "float32"), "far": _sb(C, "float32"), "pen": _sb(C, "float32"), "lt": _sb(4, "float32"),
-    "pt": _sb(4, "float32"), "sc": _sb(4, "float32"), "dl": _sb(4, "float32"), "thr": _sb(C, "float32"),
-    "xs": _sb(C, "float32"),
+    "ext": _sb(C, "float32"), "ex4": _sb(C, "float32"), "lu": _sb(32, "uint16"), "pc": _sb(C, "float32"), "pu": _sb(24, "uint16"),
+    "sg": _sb(W, "float32"), "was": _sb(C, "float32"), "life": _sb(C, "float32"),
+    "fw": _sb(512, "float32"), "c64": _sb(64, "float32"), "cu": _sb(16, "uint16"),
+    "sees": ("sbuf", [128, 3, 128], "float32"), "su": _sb(96, "uint16"), "rows": _sb(96, "float32"), "st": _sb(96, "float32"),
+    "pen": _sb(48, "float32"), "av": _sb(48, "float32"), "run": _sb(48, "float32"), "anew": _sb(TRIO, "float32"),
+    "sc": _sb(48, "float32"), "close": _sb(4, "uint16"),
+    "old": _sb(TRIO, "float32"), "pick": _sb(TRIO, "float32"), "best": _sb(TRIO, "float32"),
+    "lives": _sb(4, "float32"), "dl": _sb(4, "float32"), "rs": _sb(4, "float32"), "named": _sb(4, "bfloat16"),
+    "wins": _sb(4, "bfloat16"), "step": _sb(C, "bfloat16"), "thr": _sb(2 * C, "float32"), "sums": _sb(C, "float32"),
     "xb": _sb(4 * (XO + C), "bfloat16"), "xq": _sb(C, X4), "xp": _sb(C, U8), "tp": _sb(4 * W, "bfloat16"),
     "comp": _sb(512, "bfloat16"), "z": _sb(4 * C, "bfloat16"), "zq": _sb(C, X4), "zp": _sb(C, U8),
-    "cm": _sb(4 * C, "bfloat16"), "cmq": _sb(C, X4), "cmp": _sb(C, U8),
-    "win": _sb(16 + C, "bfloat16"), "kt": _sb(2 * C, "bfloat16"), "ktq": _sb(C // 2, X4), "ktp": _sb(C // 2, U8),
-    "ub": _sb(512, "bfloat16"), "uq": _sb(128, X4), "up": _sb(128, U8), "uu": _sb(24, "uint16"),
-    "uq2": _sb(C, X4), "up2": _sb(C, U8), "vb": _sb(512, "bfloat16"), "vq": _sb(128, X4), "vp": _sb(128, U8),
+    "cm": _sb(1024, "bfloat16"), "cmq": _sb(256, X4), "cmp": _sb(256, U8),
+    "kt": _sb(4 * C, "bfloat16"), "ktq": _sb(C, X4), "ktp": _sb(C, U8),
+    "ub": _sb(512, "bfloat16"), "uq": _sb(128, X4), "up": _sb(128, U8), "uu": _sb(8, "uint16"),
+    "uq2": _sb(256, X4), "up2": _sb(256, U8), "vb": _sb(512, "bfloat16"), "vq": _sb(128, X4), "vp": _sb(128, U8),
     "wq": _sb(512, X4), "wp": _sb(512, U8), "yb": _sb(C, "float32"),
 }
 for _t in range(R):
@@ -48,7 +51,7 @@ for _t in range(R):
     SCRATCH["lq%d" % _t] = _sb(LAND, X4)
     SCRATCH["lp%d" % _t] = _sb(LAND, U8)
 
-SEMAPHORES = ["v", "s", "t", "g", "sent", "arr0", "arr1", "arr2"] + ["d%d" % i for i in range(30)]
+SEMAPHORES = ["v", "s", "t", "g", "sent", "arr0", "arr1", "arr2"] + ["d%d" % i for i in range(32)]
 
 Op, Fn = AluOpType, ActivationFunctionType
 
@@ -124,15 +127,18 @@ def rank_program(g, core, T, topo):
     def fill(out, c, w):
         op("v", lambda: V.memset(out, c), [], w)
 
-    def scan(out, a, b, o0, o1, r, w):
-        op("v", lambda: V.tensor_tensor_scan(out, a, b, 0.0, o0, o1), r, w)
+    def scan(out, a, b, o0, o1, r, w, start=0.0):
+        op("v", lambda: V.tensor_tensor_scan(out, a, b, start, o0, o1), r, w)
 
     def quant(q, p, a, r, w):
         op("v", lambda: V.quantize_mx(q, p, a), r, w)
 
-    def act(out, a, f, r, w, bias=None, scale=None):
-        more = {k: x for k, x in (("bias", bias), ("scale", scale)) if x is not None}
+    def act(out, a, f, r, w, bias=None, scale=None, total=None):
+        more = {k: x for k, x in (("bias", bias), ("scale", scale), ("accum_out", total)) if x is not None}
         op("s", lambda: S.activation(out, a, f, **more), r, w)
+
+    def level(out, cols, value, w):
+        act(out, T.ones[:, 0:cols], Fn.Copy, ["ones"], w, scale=value)
 
     def move(q, out, a, r, w):
         if q == "v":
@@ -140,17 +146,20 @@ def rank_program(g, core, T, topo):
         else:
             act(out, a, Fn.Copy, r, w)
 
-    def iota(out, pattern, base, cm, r, w, small=False):
-        if small:
-            op("g", lambda: g.iota(out, pattern, base, cm, allow_small_or_imprecise_dtypes=True), r, w)
+    def times(q, out, a, c, r, w):
+        if q == "v":
+            ts(out, a, c, None, Op.mult, None, r, w)
         else:
-            op("g", lambda: g.iota(out, pattern, base, cm), r, w)
+            act(out, a, Fn.Copy, r, w, scale=c)
 
-    def whole(out, cols, value, r, w):
-        iota(out, [[0, cols]], value, 0, r, w, True)
+    def iota(out, pattern, base, cm, r, w):
+        op("g", lambda: g.iota(out, pattern, base, cm, allow_small_or_imprecise_dtypes=True), r, w)
 
-    def bank(b, lo, hi):
-        return T.ps[:, 512 * b + lo:512 * b + hi]
+    def whole(out, cols, value, w):
+        iota(out, [[0, cols]], value, 0, [], w)
+
+    def bank(b, lo, hi, step=1):
+        return T.ps[:, 512 * b + lo:512 * b + hi:step]
 
     def mm(b, cols, lq, lp, rq, rp, r, start=True, stop=True):
         k = "P%d" % b
@@ -159,59 +168,46 @@ def rank_program(g, core, T, topo):
     def part(q, p, b):
         return q[:, 128 * b:128 * b + 128], p[:, 128 * b:128 * b + 128]
 
-    names = ["p", "q16", "q12", "q3", "q7", "offk", "c4a", "c4s", "c4c", "zp", "thv", "sg", "sg32", "pens", "q256", "offb"]
+    names = ["p", "q16", "q12", "q3", "offk", "c4a", "c4b", "c4s", "c4c", "q256"]
 
     def col(name):
         i = names.index(name)
         return T.pf[:, i:i + 1]
 
-    def small(name, src, f, bias, scale):
-        r = [k if k not in names[:5] else "pf" for k in (src, bias, scale) if isinstance(k, str)]
-        act(col(name), col(src), f, r, [name], bias=col(bias) if isinstance(bias, str) else bias,
-            scale=col(scale) if isinstance(scale, str) else scale)
-
-    def hold(out, src, cols, r, key):
-        scan(out, T.mm[:, 0:2 * cols:2], src, Op.add, Op.max, r + ["mm0", "mm2"], [key])
-
-    def hold4(buf, src, cols, r, key):
-        scan(buf[:, 0:cols], T.mm[:, 1:2 * cols:2], src, Op.add, Op.max, r + ["mm1"] + ["mm2"] * (cols > 64), [key])
-
-    def deal(out, src, r, key):
-        dma([("y", out[:, 16 * b:16 * b + 16], src[0:128:16, 256 * b:256 * b + 256]) for b in range(2)], r, [key])
+    def small(name, src, bias, scale):
+        r = [k if k not in names[:4] else "pf" for k in (src, bias) if isinstance(k, str)]
+        act(col(name), col(src), Fn.Identity, r, [name], bias=col(bias) if isinstance(bias, str) else bias, scale=scale)
 
     u32 = dt.uint32
     xall = ["x0", "x1", "x2", "x3", "x4"]
     X = T.xb[:, 4 * XO:4 * (XO + C)]
+    diagonal = T.strip[:, 3:515:4]
 
     def quant_x():
         quant(T.xq[:], T.xp[:], X, xall, ["xq"])
 
-    def unpack_own(stop):
-        for b in range(4):
+    def unpacker(b):
+        quant(*part(T.eq, T.es, b), T.strip[:, 3 - b:515 - b], ["strip"], ["e%d" % b])
+
+    def unpack_own(stop, banks=range(4)):
+        for b in banks:
             mm(b, C, *part(T.eq, T.es, b), T.xq[:], T.xp[:], ["e%d" % b, "xq"], True, stop)
 
     def copy_t(b):
-        act(T.tp[:, 4 * OWN + b:4 * W:4], bank(b, 0, C), Fn.Copy, ["P%d" % b], ["to%d" % b], scale=0.015625)
-
-    def copy_out(q, out, b, lo, hi, key):
-        if q == "v":
-            ts(out, bank(b, lo, hi), 0.015625, None, Op.mult, None, ["P%d" % b], [key])
-        else:
-            act(out, bank(b, lo, hi), Fn.Copy, ["P%d" % b], [key], scale=0.015625)
+        times("s", T.tp[:, 4 * OWN + b:4 * W:4], bank(b, 0, C), 0.015625, ["P%d" % b], ["to%d" % b])
 
     def copy_x(b, q="s", lo=0, hi=C):
-        copy_out(q, T.xb[:, 4 * (XO + lo) + b:4 * (XO + hi):4], b, lo, hi, "x4" if lo else "x%d" % b)
+        times(q, T.xb[:, 4 * (XO + lo) + b:4 * (XO + hi):4], bank(b, lo, hi), 0.015625, ["P%d" % b], ["x4" if lo else "x%d" % b])
 
-    dma([("s", T.lin[:, 0:24], T.seat[:])], [], ["seat"])
     dma([("y" if i < 5 else "s", T.lin[16 * i:16 * i + 16, 24:48], T.alive[:]) for i in range(8)], [], ["alive"])
+    dma([("s", T.lin[:, 0:24], T.seat[:])], [], ["seat"])
     dma([("y", X, T.x[:])], [], xall)
     dma([("y", T.ub[:], T.u[:])], [], ["ub"])
     dma([("y", T.wq[:].bitcast(dt.uint8), T.wc[:]), ("y", T.wp[:], T.ws[:])], [], ["w"])
     dma([("y", T.vb[:], T.v[:])], [], ["vb"])
-    alive = T.lin[:, 24:48]
 
-    iota(T.pint[:, 0:1], [[0, 1]], 0, 1, [], ["pi"])
-    iota(T.turn[:, 96:160], [[0, 16], [4, 4]], 0, 0, [], ["four"], True)
+    op("g", lambda: g.iota(T.pint[:, 0:1], [[0, 1]], 0, 1), [], ["pi"])
+    posi_all = ["posi0", "posi1", "posi2", "posi3"]
     for odd in (1, 0):
         for a in range(4):
             di, dj = WAY[2 * a + odd]
@@ -223,148 +219,209 @@ def rank_program(g, core, T, topo):
                 be, ga = (bi, ga) if di < 0 else (-bi, ga + 5 * bi)
             entry = -1000 if di == 0 else (UP if di < 0 else DOWN) - (6 if dj else 0)
             iota(T.posi[32 * a:32 * a + 16 + 16 * odd, :], [[entry, 2], [be, 6], [16 * al, 4]], ga - 16 * al * odd, al,
-                 ["pi", "four"], ["posi%d" % a], True)
-    posi_all = ["posi0", "posi1", "posi2", "posi3"]
-    iota(T.turn[:, 32:96], [[0, 4], [1, 16]], 0, 0, posi_all, ["sixteen"], True)
+                 ["pi"], [posi_all[a]])
+    iota(T.turn[:, 96:160], [[0, 16], [4, 4]], 0, 0, posi_all, ["four"])
+    iota(T.turn[:, 32:96], [[0, 4], [1, 16]], 0, 0, [], ["sixteen"])
+    whole(T.xb[:, 0:4 * XO], 4 * XO, 0, ["xz"])
+    iota(T.turn[:, 0:32], [[256, 2], [1, 16]], 0, 0, [], ["turn"])
+    whole(T.comp[:, 256:512], 256, 0, ["compz"])
+    whole(T.fw[:, 0:1], 1, 0, ["fwz"])
+    whole(T.rows[:], 96, 1, ["rows"])
+    whole(T.tp[:, 0:4 * UP], 4 * UP, 0, ["tz"])
+    whole(T.tp[:, 4 * GAP:4 * OWN], 4 * (OWN - GAP), 0, ["tg"])
 
     fill(T.ones[:], 1.0, ["ones"])
-    for i, m in enumerate((15, 12, 3, 7)):
+    fill(T.two[:, 0:1], -1 / EPS, ["two0"])
+    fill(T.two[:, 1:2], BIG, ["two1"])
+    fill(T.uu[:], 1, ["uu"])
+    scan(T.cnt[:, 0:W // 2], T.ones[:], T.ones[:], Op.mult, Op.add, ["ones"], ["cnt0"], -1.0)
+    for i, m in enumerate((15, 12, 3)):
         ts(T.pint[:, 1 + i:2 + i], T.pint[:, 0:1], m, None, Op.bitwise_and, None, ["pi"], ["pi%d" % i])
-    op("v", lambda: V.tensor_tensor_scan(T.cnt[:, 0:W // 2], T.ones[:], T.ones[:], -1.0, Op.mult, Op.add), ["ones"], ["cnt0"])
-    act(T.two[:, 0:1], T.ones[:, 0:1], Fn.Copy, ["ones"], ["two0"], scale=-1 / EPS)
-    act(T.two[:, 1:2], T.ones[:, 0:1], Fn.Copy, ["ones"], ["two1"], scale=BIG)
+    act(T.cnt[:, W // 2:W], T.cnt[:, 0:W // 2], Fn.Identity, ["cnt0"], ["cnt1"], bias=float(W // 2))
     for h in range(2):
-        act(T.d0[:, 256 * h:256 * h + 256], T.ones[:, 0:256], Fn.Copy, ["ones"], ["d0%d" % h], scale=-EPS)
-        if h == 0:
-            act(T.strip[:, 0:264], T.ones[:, 0:264], Fn.Copy, ["ones"], ["strip0"], scale=0.0)
-            act(T.cnt[:, W // 2:W], T.cnt[:, 0:W // 2], Fn.Identity, ["cnt0"], ["cnt1"], bias=float(W // 2))
-    whole(T.xb[:, 0:4 * XO], 4 * XO, 0, posi_all, ["xz"])
-    whole(T.comp[:, 256:512], 256, 0, [], ["compz"])
-    iota(T.turn[:, 0:32], [[256, 2], [1, 16]], 0, 0, [], ["turn"], True)
-
-    def unpacker(b):
-        quant(*part(T.eq, T.es, b), T.strip[:, 3 - b:515 - b], ["strip"], ["e%d" % b])
-
-    cp(T.pf[:, 0:5], T.pint[:, 0:5], ["pi", "pi0", "pi1", "pi2", "pi3"], ["pf"])
-    fill(T.uu[:, 0:8], 1, ["uu0"])
-    ts(T.mm[:, 1:128:2], T.turn[:, 96:160], col("q12"), -BIG, Op.is_equal, Op.mult, ["four", "pf"], ["mm1"])
-    act(T.mm[:, 1:128:2], T.mm[:, 1:128:2], Fn.Identity, ["mm1"], ["mm1"], bias=K * EPS)
-    ts(T.uu[:, 8:16], T.cnt[:, 0:8], col("q7"), 16.0, Op.max, Op.mult, ["cnt0", "pf"], ["uu1"])
-    ts(T.uu[:, 16:24], T.cnt[:, 0:8], col("q7"), 16.0, Op.min, Op.mult, ["cnt0", "pf"], ["uu2"])
-    cp(T.aliveu[:], alive, ["alive"], ["aliveu"])
+        level(T.strip[:, 264 * h:264 * h + 264], 264, 0.0, ["strip%d" % h])
+    for h in range(2):
+        level(T.d0[:, 256 * h:256 * h + 256], 256, -EPS, ["d0%d" % h])
+    cp(T.pf[:, 0:4], T.pint[:, 0:4], ["pi", "pi0", "pi1", "pi2"], ["pf"])
+    cp(T.aliveu[:], T.lin[:, 24:48], ["alive"], ["aliveu"])
     cp(T.seatu[:], T.lin[:, 0:24], ["seat"], ["seatu"])
+    ts(T.close[:], T.cnt[:, 0:128:32], col("q16"), None, Op.add, None, ["cnt0", "pf"], ["close"])
     tt(T.ni[:], T.two[:, 0:2].indirect(T.aliveu[:]), T.cnt[:, OWN:W], Op.min, ["two0", "two1", "aliveu", "cnt0", "cnt1"], ["ni"])
-    act(T.strip[:, 264:528], T.ones[:, 0:264], Fn.Copy, ["ones"], ["strip1"], scale=0.0)
-    act(T.nis[:, 0:256], T.ni[:].indirect(T.seatu[:, 0:16]), Fn.Copy, ["ni", "seatu"], ["nis0"], scale=-EPS)
+    ts(diagonal, T.cnt[:, 0:128], col("p"), 64.0, Op.is_equal, Op.mult, ["cnt0", "pf", "strip0", "strip1"], ["strip"])
     ts(T.tmp[:, 0:69], T.cnt[:, 0:69], T.posi[:, 24:25], T.posi[:, 0:1], Op.add, Op.subtract, ["cnt0"] + posi_all, ["tmp0"])
     cp(T.posu[:], T.posi[:, 0:24], posi_all, ["posu"])
-    ts(T.nis[:, 256:C], T.ni[:].indirect(T.seatu[:, 16:24]), -EPS, None, Op.mult, None, ["ni", "seatu"], ["nis1"])
+    small("c4a", "q3", 12 * K - 4.0 * (OWN - XO), 1.0)
+    small("q256", "q16", 0.0, 16.0)
+    for h, q in enumerate("sv"):
+        times(q, T.nis[:, 192 * h:192 * h + 192], T.ni[:].indirect(T.seatu[:, 12 * h:12 * h + 12]), -EPS, ["ni", "seatu"], ["nis%d" % h])
     ts(T.d0[:, 0:483:7], T.tmp[:, 0:69], -EPS, -EPS, Op.mult, Op.min, ["tmp0", "d00", "d01"], ["d0"])
+    ts(T.mm[:, 1:128:2], T.turn[:, 96:160], col("q12"), -BIG, Op.is_equal, Op.mult, ["four", "pf"], ["mm1"])
     ts(T.mm[:, 0:128:2], T.turn[:, 32:96], col("q16"), -BIG, Op.is_equal, Op.mult, ["sixteen", "pf"], ["mm0"])
     cp(T.d0[:].indirect(T.posu[:]), T.nis[:], ["nis0", "nis1", "posu"], ["d0"])
-    small("c4a", "q3", Fn.Identity, 12 * K, 1.0)
+    small("c4c", "q12", "c4a", -K)
+    act(T.posf[:], T.cnt[:].indirect(T.posu[:]), Fn.Copy, ["cnt0", "cnt1", "posu"], ["posf"])
+    act(T.mm[:, 1:128:2], T.mm[:, 1:128:2], Fn.Identity, ["mm1"], ["mm1"], bias=K * EPS)
     act(T.mm[:, 0:128:2], T.mm[:, 0:128:2], Fn.Identity, ["mm0"], ["mm0"], bias=K)
-    small("c4s", "q12", Fn.Identity, "c4a", -K)
-    small("q256", "q16", Fn.Identity, 0.0, 16.0)
-    dma([("y", T.mm[:, 128 * i:128 * i + 128], T.mm[:, 0:128]) for i in range(1, 6)], ["mm0", "mm1"], ["mm2"])
-    diagonal = T.strip[:, 3:515:4]
-    op("g", lambda: g.affine_select(diagonal, diagonal, [[1, 128]], Op.not_equal, 64.0, 0, -1), ["strip0", "strip1"], ["strip"])
-    whole(T.dead[:, 0:OWN], OWN, 0, [], ["dead0"])
-    whole(T.pc[:, C:512], 512 - C, 0, [], ["pcz"])
-    whole(T.wts[:, 3:512:4], 128, 0, [], ["wv3"])
-    whole(T.fw[:, 0:1], 1, 0, [], ["fwz"])
-    whole(T.tp[:, 0:4 * UP], 4 * UP, 0, [], ["tz"])
-    whole(T.tp[:, 4 * GAP:4 * OWN], 4 * (OWN - GAP), 0, [], ["tg"])
-    act(T.posf[:], T.cnt[:, 0:W].indirect(T.posu[:]), Fn.Copy, ["cnt0", "cnt1", "posu"], ["posf"])
-    small("c4c", "c4s", Fn.Identity, -4.0 * (OWN - XO), 1.0)
-    small("sg", "q16", Fn.Sign, "p", -17.0)
-    small("offk", "q16", Fn.Identity, 15 * K, -K)
-    small("sg32", "sg", Fn.Identity, 0.0, 32.0)
-    small("pens", "sg", Fn.Identity, 0.0, BIG / 256)
-    small("offb", "offk", Fn.Identity, OWN - 16.0, 1.0)
-    quant(T.uq[:], T.up[:], T.ub[:], ["ub"], ["uq"])
-    act(T.up2[:], T.up[:].indirect(T.uu[:]), Fn.Copy, ["uq", "uu0", "uu1", "uu2"], ["u2b"])
-    dead_all = ["dead0", "deadA", "deadB"]
+    dma([("y", T.mm[:, 128:256], T.mm[:, 0:128])], ["mm0", "mm1"], ["mm2"])
+    small("c4b", "q3", -12 * K, 1.0)
+    small("offk", "q16", 15 * K, -K)
+    small("c4s", "q12", "c4b", K)
+    for b in range(4):
+        level(T.wts[:, 512 + b:1024:4], 128, 1.0 if b == 3 else -1.0, ["w1%d" % b])
+    level(T.wts[:, 0:16], 16, 0.0, ["w0a"])
+    level(T.av[:], 48, BIG, ["av0", "av1", "av2"])
+    level(T.anew[:], TRIO, -BIG, ["anew"])
+    level(T.run[:, 0:1], 1, BIG, ["runz"])
+    level(T.anew[:, 15:TRIO:16], 2, BIG, ["anew"])
+    for lo, hi in ((0, 2), (6, 7), (8, 11)):
+        level(T.wts[:, lo:hi], hi - lo, 1.0, ["w0%d" % lo] + ["w0a"] * (lo == 0))
+    unpacker(0)
+    sg_all = ["sg0", "sgA", "sgB", "sgC"]
+    sees_all = ["sees0", "sees1", "sees2"]
 
     def later_constants():
-        for b in range(3):
-            whole(T.wts[:, b:512:4], 128, 1, [], ["wv%d" % b])
-        op("g", lambda: g.affine_select(T.tri[:], T.ones[:, 0:128], [[1, 128]], Op.is_gt, 0.0, 0, -1), ["ones"], ["tri"])
-        for b in range(2):
-            whole(T.wts[:, 512 + b:1026:4], 129, 0, [], ["wk%d" % b])
-        whole(T.win[:, 0:16], 16, 0, [], ["winz"])
+        op("g", lambda: g.affine_select(T.step[:, 0:128], T.comp[:, 256:384], [[1, 128]], Op.is_ge, -1.25 * 2.0 ** -25, 0, -1),
+           ["compz"], ["tri"])
+        whole(T.wts[:, 16:512], 496, 0, ["w0b"])
+        whole(T.cm[:, 3:1024:4], 256, 0, ["cmz"])
+        iota(T.cells[:], [[1, C]], -C // 2, 0, [], ["cells"])
+        whole(T.sg[:, 0:OWN], OWN, -1, ["sg0"])
 
     def arrived(b, q):
-        copy_out(q, T.tp[:, 4 * UP + b:4 * GAP:4], 4 + b, 0, LAND, "ta%d" % b)
+        times(q, T.tp[:, 4 * UP + b:4 * GAP:4], bank(4 + b, 0, LAND), 0.015625, ["P%d" % (4 + b)], ["ta%d" % b])
 
     t_all = ["tz", "tg"] + ["ta%d" % b for b in range(4)] + ["to%d" % b for b in range(4)]
 
     def gather_z(q, lo, hi, key):
         move(q, T.z[:, 4 * lo:4 * hi], T.tp[:].indirect(T.su[:, lo // 4:hi // 4]), t_all + ["su"], [key])
 
-    def name_weights(b):
-        o, x = (Op.is_equal, -2.0 ** -15) if b == 2 else (Op.not_equal, 2.0 ** -12)
-        ts(T.wts[:, 512 + b:1026:4], T.comp[:, 256:384], col("q16"), x, o, Op.mult, ["compz", "pf"], ["wk%d" % b])
+    def hold(k):
+        scan(T.ext[:, 128 * k:128 * k + 128], T.mm[:, 0:256:2], T.pc[:, 128 * k:128 * k + 128], Op.add, Op.max,
+             ["pc", "mm0", "mm2"], ["ext%d" % k])
 
-    def name_tile(h):
-        quant(*part(T.kq, T.ks, 1 + h), T.wts[:, 514 - 2 * h:1026 - 2 * h], ["wk0", "wk1", "wk2", "wk3"], ["kq%d" % h])
+    def hold4(k):
+        scan(T.ex4[:, 128 * k:128 * k + 128], T.mm[:, 1:256:2], T.sees[:, k, :], Op.add, Op.max, [sees_all[k], "mm1", "mm2"], ["ex%d" % k])
 
-    def penalty(lo, hi):
-        ts(T.pen[:, 128 * lo:128 * hi], T.sees[:, 128 * lo:128 * hi], (0.5 - OWN) * EPS, col("pens"), Op.is_gt, Op.mult,
-           ["sees", "pens"], ["pen%d" % k for k in range(lo, hi)])
+    def offsets_z():
+        ts(T.su[:], T.ex4[:, 3:C:4], 4 / EPS, col("c4s"), Op.mult, Op.add, ["ex0", "ex1", "ex2", "c4s"], ["su"])
 
-    def backward(d, dk, i, cuts):
-        hi, lo = cuts[i] - 1, cuts[i + 1] - 1
-        src = d[:, hi:lo:-1] if lo >= 0 else d[:, hi::-1]
-        start = T.bw[:, hi + 8:hi + 9] if i else 0.0
-        op("v", lambda: V.tensor_tensor_scan(T.bw[:, hi + 7:lo + 7:-1], src, src, start, Op.mult, Op.min),
-           [dk, "d2"] + ["bw%d" % (i - 1)] * (i > 0), ["bw%d" % i])
+    def look(k, q):
+        src = T.fw[:, 0:LS + 1].indirect(T.pu[:, 8 * k:8 * k + 8])
+        if q:
+            times(q, T.sees[:, k, :], src, -1.0, ["fw", "fwz", "pu"], [sees_all[k]])
+        else:
+            tt(T.sees[:, k, :], src, T.sg[:, OWN + 128 * k:OWN + 128 * k + 128], Op.mult, ["fw", "fw2", "fwz", "pu"] + sg_all, [sees_all[k]])
 
-    def seen_by():
-        act(T.back[:], T.bw[:, 8:LS + 7].indirect(T.pv[:]), Fn.Copy, ["bw3", "bw2", "bw1", "bw0", "pv"], ["back"], scale=-1 / EPS)
-        deal(T.backw, T.back, ["back"], "backw")
+    def turn_sees():
+        dma([("ys"[a % 2], T.rows[32 * a:32 * a + 8, :], T.sees[0:128:16, :, 32 * a:32 * a + 32]) for a in range(4)], sees_all, ["rows"])
 
-    def take_back():
-        ts(T.bu[:], T.backw[:, 0:24], OWN - 16.0, None, Op.subtract, None, ["backw"], ["bu"])
+    def turned(i):
+        if i == 0:
+            op("v", lambda: V.transpose(T.st[:], T.rows[:]), ["rows"], ["st"])
+        elif i == 1:
+            ts(T.pen[:], T.st[:].indirect(T.close[:, 0:3]), (OWN - 0.5) * EPS, BIG, Op.is_lt, Op.mult, ["st", "close"], ["pen"])
+        elif i == 2:
+            ts(T.pen[:, 8:48:16], T.st[:, 0:96:32], 0.0, -BIG, Op.is_le, Op.mult, ["st", "pen"], ["pen"])
+        else:
+            act(T.lives[:, 0:3], T.st[:, 0:96:32], Fn.Sign, ["st"], ["lives"])
+            act(T.sc[:], T.st[:].indirect(T.close[:, 0:3]), Fn.Copy, ["st", "close"], ["sc"])
+
+    def harmless(k):
+        ts(T.step[:, 128 * k:128 * k + 128], T.sees[:, k, :], 0.0, None, Op.is_le, None, [sees_all[k]], ["dead%d" % k])
 
     def slots(lo, hi, key):
-        tt(T.d1[:, lo:hi], T.dead[:].indirect(T.lu[:, lo // 16:hi // 16]), T.d0[:, lo:hi], Op.add, dead_all + ["lu", "d0"], [key])
+        tt(T.d1[:, lo:hi], T.sg[:].indirect(T.lu[:, lo // 16:hi // 16]), T.d0[:, lo:hi], Op.max, sg_all + ["lu", "d0"], [key])
 
-    def forward_rest(d):
-        op("v", lambda: V.tensor_tensor_scan(T.fw[:, SENT + 1:LS + 1], d[:, SENT:LS], d[:, SENT:LS],
-                                             T.fw[:, SENT:SENT + 1], Op.mult, Op.min), ["d2", "fw"], ["fw2"])
+    def zero_columns(i):
+        dma([("y", T["lq%d" % i][:, 64:DOWN - UP].bitcast(dt.uint8), T.sq0[:, 64:DOWN - UP].bitcast(dt.uint8)),
+             ("y", T["lp%d" % i][:, 64:DOWN - UP], T.sp0[:, 64:DOWN - UP])], ["sq0"], ["landz%d" % i])
 
-    def dead_along_partitions():
-        dma([("y", T.lt[:, k:k + 1], T.dead[0:1, OWN + 128 * k:OWN + 128 * k + 128]) for k in range(3)], dead_all, ["lt"])
+    uk = ["u2a", "u2b", "u2c"]
+    zk = ["zq0", "zq1", "zq2"]
+    av_all = ["av0", "av1", "av2"]
+
+    def quant_z(k, r):
+        quant(*part(T.zq, T.zp, k), T.z[:, 512 * k:512 * k + 512], r, [zk[k]])
+
+    def along_partitions(k):
+        mm(4 + k, 130, *part(T.zq, T.zp, k), T.uq2[:, 0:130], T.up2[:, 0:130], uk + [zk[k]])
+
+    def scores(k):
+        tt(T.av[:, 16 * k:16 * k + 9], bank(4 + k, 0, 129, 16), T.pen[:, 16 * k:16 * k + 9], Op.add, ["P%d" % (4 + k), "pen"], [av_all[k]])
+
+    def size(k):
+        act(T.dl[:, k:k + 1], T.av[:, 16 * k + 8:16 * k + 9], Fn.Abs, [av_all[k]], ["dl%d" % k], bias=2.0 ** -100, scale=2.0)
+
+    def near(k):
+        act(T.thr[:, 128 * k:128 * k + 128], T.step[:, 0:128], Fn.Identity, ["tri", av_all[k], "dl%d" % k], ["near%d" % k],
+            bias=T.av[:, 16 * k + 8:16 * k + 9], scale=T.dl[:, k:k + 1])
+
+    def far(k):
+        act(T.thr[:, C + 256 * k:C + 256 + 128 * k], T.step[:, 128 * k + 128:C], Fn.Identity, ["dead1", "dead2"][k:] + [av_all[k]],
+            ["far%d" % k], bias=T.av[:, 16 * k + 8:16 * k + 9], scale=2 * BIG)
+
+    def beats(r, lo, hi, at, to, slot, key):
+        tt(T.cm[:, 4 * to + slot:4 * (to + hi - lo):4], bank(7, lo, hi), T.thr[:, at:at + hi - lo], Op.is_gt, ["P7", r], [key])
+
+    def beaten(k, to, cols, slot, least, key):
+        act(T.sums[:, 128 * (1 - k):128 * (1 - k) + cols], T.cm[:, 4 * to + slot:4 * (to + cols):4], Fn.Identity, [key], ["rs%d" % k],
+            bias=least / cols, total=T.rs[:, k:k + 1])
+
+    def count_down(h, r):
+        quant(*part(T.cmq, T.cmp, h), T.cm[:, 512 * h:512 * h + 512], r + ["cmz"], ["cmq%d" % h])
+        mm(4 + h, 128, *part(T.cmq, T.cmp, h), *part(T.kq, T.ks, 0), ["kq0", "cmq%d" % h])
+
+    def layer(b):
+        mm(b, C, *part(T.wq, T.wp, b), T.zq[:], T.zp[:], ["w"] + zk, False, True)
+
+    def contested(k, b, at, least, r):
+        ts(T.wins[:, k:k + 1], bank(b, at, at + 1), least, T.lives[:, k:k + 1], Op.is_gt, Op.min, ["P%d" % b, "lives"] + r, ["wins%d" % k])
+
+    def names_of(k):
+        ts(T.kt[:, k:4 * C:4], T.cells[:], T.named[:, k:k + 1], T.wins[:, k:k + 1], Op.is_equal, Op.mult,
+           ["cells", "named", "wins%d" % k], ["kt%d" % k])
+
+    def spared(k):
+        ts(T.kt[:, 512 * k + 3:512 * k + 512:4], diagonal, T.wins[:, k:k + 1], None, Op.mult, None, ["strip", "wins%d" % k], ["kd%d" % k])
+
+    def last_codes(h, lo, hi):
+        quant(T.xq[:, lo:hi], T.xp[:, lo:hi], T.xb[:, 4 * (XO + lo):4 * (XO + hi)], xall, ["xq%d" % h] + ["xq"] * (1 - h))
+        mm(h, hi - lo, T.vq[:], T.vp[:], T.xq[:, lo:hi], T.xp[:, lo:hi], ["vq", "xq%d" % h])
+        dma([("y", T.oc[:, 4 * lo:4 * hi], T.xq[:, lo:hi].bitcast(dt.uint8))], ["xq%d" % h], [])
+
+    def last_product(q, h, lo, hi):
+        move(q, T.yb[:, lo:hi], bank(h, 0, hi - lo), ["P%d" % h], ["yb%d" % h])
+        dma([("y", T.y[:, lo:hi], T.yb[:, lo:hi])], ["yb%d" % h], [])
 
     for t in range(R):
         first, last = t == 0, t == R - 1
-        d, dk = (T.d0, "d0") if first else (T.d1, "d1")
+        d, dk = (T.d0, ["d0"]) if first else (T.d1, ["d1", "d2"])
         if not first:
-            if t == 1:
-                cp(T.pv[:], T.pw[:], ["pw"], ["pv"])
-            slots(0, SENT, dk)
-            slots(SENT, LL, "d2")
-            dead_along_partitions()
+            slots(0, SENT, dk[0])
+            slots(SENT, LL, dk[1])
+            if last:
+                act(T.was[:], T.ni[:], Fn.Relu, ["ni"], ["was"], scale=-EPS)
             copy_t(0)
             copy_t(1)
-            act(T.life[:], T.dead[:, OWN:W], Fn.Identity, dead_all, ["life"], bias=1.0, scale=-1.0)
 
         def between(i):
             if first and i < 3:
-                unpacker(i)
+                unpacker(i + 1)
+                if i == 1:
+                    ts(T.turnu[:], T.turn[:, 0:32], col("q256"), None, Op.add, None, ["turn", "q256"], ["turnu"])
             elif first:
-                unpacker(3)
-                ts(T.turnu[:], T.turn[:, 0:32], col("q256"), None, Op.add, None, ["turn", "q256"], ["turnu"])
+                quant_x()
+            elif i == 0 and t == 1:
+                quant(T.vq[:], T.vp[:], T.vb[:], ["vb"], ["vq"])
             elif i == 1:
-                forward_rest(d)
-            else:
-                backward(d, dk, max(i - 1, 0), BACK)
+                scan(T.fw[:, SENT + 1:LS + 1], d[:, SENT:LS], d[:, SENT:LS], Op.mult, Op.min, [dk[1], "fw"], ["fw2"], T.fw[:, SENT:SENT + 1])
+            elif i > 1:
+                look(i - 2, None)
 
         now = LS if first else SENT
-        scan(T.fw[:, 1:now + 1], d[:, 0:now], d[:, 0:now], Op.mult, Op.min, [dk], ["fw"])
+        scan(T.fw[:, 1:now + 1], d[:, 0:now], d[:, 0:now], Op.mult, Op.min, dk[:1], ["fw"])
         between(0)
-        hold4(T.c64, T.fw[:, 7:455:7], 64, ["fw"], "c64")
+        scan(T.c64[:], T.mm[:, 1:128:2], T.fw[:, 7:455:7], Op.add, Op.max, ["fw", "mm1"], ["c64"])
         between(1)
         ts(T.cu[:], T.c64[:, 3:64:4], -4 / EPS, col("c4c"), Op.mult, Op.add, ["c64", "c4c"], ["cu"])
         between(2)
@@ -396,203 +453,130 @@ def rank_program(g, core, T, topo):
                 mm(4 + b, LAND, *part(T.eq, T.es, b), lq[:], lp[:], ["e%d" % b, "land", "landz%d" % t])
 
         if first:
-            act(T.dead[:, OWN:W], T.ni[:], Fn.Relu, ["ni"], ["deadA", "deadB"], scale=-EPS)
-            act(T.idl[:], T.d0[:].indirect(T.turnu[:]), Fn.Relu, ["d0", "turnu"], ["idl"], scale=-1 / EPS)
-            for i in range(R):
-                dma([("y", T["lq%d" % i][:, 64:DOWN - UP].bitcast(dt.uint8), sq[:, 64:DOWN - UP].bitcast(dt.uint8)),
-                     ("y", T["lp%d" % i][:, 64:DOWN - UP], sp[:, 64:DOWN - UP])], ["sq0"], ["landz%d" % i])
-            dead_along_partitions()
-            deal(T.lw, T.idl, ["idl"], "lw")
+            zero_columns(0)
             later_constants()
-            quant_x()
+            cp(T.pc[:].indirect(T.seatu[:]), T.posf[:], ["posf", "seatu"], ["pc"])
             unpack_own(True)
+            act(T.idl[:], T.d0[:].indirect(T.turnu[:]), Fn.Relu, ["d0", "turnu"], ["idl"], scale=-1 / EPS)
+            dma([("y", T.lw[:, 16 * b:16 * b + 16], T.idl[0:128:16, 256 * b:256 * b + 256]) for b in range(2)], ["idl"], ["lw"])
             for b in range(4):
                 copy_t(b)
-            cp(T.pc[:, 0:C].indirect(T.seatu[:]), T.posf[:], ["posf", "seatu"], ["pc"])
-            deal(T.pw, T.pc, ["pc", "pcz"], "pw")
-            name_weights(3)
-            hold(T.ext[:, 0:C], T.pc[:, 0:C], C, ["pc"], "ext")
-            ts(T.wts[:, 3:512:64], T.cnt[:, 0:8], col("q16"), col("sg32"), Op.is_equal, Op.mult, ["cnt0", "pf", "sg32"], ["wv3"])
-            tt(T.jw[:], T.ext[:, 15:C:16], alive, Op.mult, ["ext", "alive"], ["jw"])
-            name_weights(2)
+            quant(T.uq[:], T.up[:], T.ub[:], ["ub"], ["uq"])
+            dma([("y", T.uq2[:, 0:128].bitcast(dt.uint8), T.uq[:].bitcast(dt.uint8)), ("y", T.up2[:, 0:128], T.up[:])], ["uq"], ["u2c"])
+            for k in range(3):
+                hold(k)
+            act(T.up2[:, 128:256], T.up[:].indirect(T.uu[:]), Fn.Copy, ["uq", "uu"], ["u2b"])
+            tt(T.jw[:], T.ext[:, 15:C:16], T.lin[:, 24:48], Op.mult, ["ext0", "ext1", "ext2", "alive"], ["jw"])
+            cp(T.uq2[:, 128:256].bitcast(u32), T.uq[:].bitcast(u32).indirect(T.uu[:]), ["uq", "uu"], ["u2a"])
             ts(T.pu[:], T.jw[:], col("offk"), None, Op.subtract, None, ["jw", "offk"], ["pu"])
+            quant(*part(T.kq, T.ks, 1), T.wts[:, 512:1024], ["w10", "w11", "w12", "w13"], ["kq1"])
+            unpack_own(False, (0, 1))
             unpack_arrived()
-            unpack_own(False)
-            act(T.sees[:], T.fw[:, 0:LS + 1].indirect(T.pu[:]), Fn.Copy, ["fw", "fw2", "fwz", "pu"], ["sees"])
-            cp(T.uq2[:].bitcast(u32), T.uq[:].bitcast(u32).indirect(T.uu[:]), ["uq", "uu0", "uu1", "uu2"], ["u2a"])
-            ts(col("zp"), col("q16"), 0.0, col("p"), Op.is_equal, Op.mult, ["pf"], ["zp"])
+            unpack_own(False, (2, 3))
+            for k in range(3):
+                look(k, "vsv"[k])
+            turn_sees()
+            for k in range(3):
+                hold4(k)
+            harmless(2)
+            for b in range(4):
+                arrived(b, "sssv"[b])
+            offsets_z()
+            harmless(1)
         else:
+            look(2, None)
             copy_t(2)
+            turn_sees()
             copy_t(3)
             unpack_own(False)
-            backward(d, dk, 3, BACK)
-            seen_by()
-            tt(T.sees[:], T.fw[:, 0:LS + 1].indirect(T.pu[:]), T.life[:], Op.mult, ["fw", "fw2", "fwz", "pu", "life"], ["sees"])
-        if t == 1:
-            quant(T.vq[:], T.vp[:], T.vb[:], ["vb"], ["vq"])
-        hold4(T.ext, T.sees[:], C, ["sees"], "ext")
-        penalty(0, 1 if first else 3)
-        ts(T.su[:], T.ext[:, 3:C:4], -4 / EPS, col("c4s"), Op.mult, Op.add, ["ext", "c4s"], ["su"])
-        act(T.pt[:, 0:3], T.lt[:, 0:3], Fn.Identity, ["lt"], ["pt"], scale=-BIG)
-        if first:
-            ts(col("thv"), col("zp"), -2.0, 31.5, Op.mult, Op.add, ["zp"], ["thv"])
-            quant(*part(T.kq, T.ks, 0), T.wts[:, 0:512], ["wv0", "wv1", "wv2", "wv3"], ["kq"])
-        else:
+            for k in range(3):
+                hold4(k)
+            harmless(1)
+            harmless(2)
+            offsets_z()
             unpack_arrived()
-        for b in range(4):
-            arrived(b, "s" if first else "vssv"[b])
-        uk = ["u2a", "u2b"]
-        zk = ["zq0", "zq1", "zq2"]
-
-        def quant_z(k, r):
-            quant(*part(T.zq, T.zp, k), T.z[:, 512 * k:512 * k + 512], r, [zk[k]])
-
-        def along_partitions(k, b):
-            mm(b, 128, *part(T.zq, T.zp, k), *part(T.uq2, T.up2, 0), uk + [zk[k]])
-
-        def score(k, b):
-            act(T.sc[:, k:k + 1], bank(b, 0, 1), Fn.Identity, ["P%d" % b, "pt"], ["sc%d" % k], bias=T.pt[:, k:k + 1])
-
-        def step_up(k, b):
-            act(T.dl[:, k:k + 1], bank(b, 0, 1), Fn.Abs, ["P%d" % b], ["dl%d" % k], bias=2.0 ** -122, scale=1.25 * 2.0 ** -24)
-
-        def threshold(k):
-            act(T.thr[:, 128 * k:128 * k + 128], T.tri[:], Fn.Identity, ["tri", "sc%d" % k, "dl%d" % k], ["thr%d" % k],
-                bias=T.sc[:, k:k + 1], scale=T.dl[:, k:k + 1])
-
-        def pair(i, lo, hi, r):
-            mm(5 + i, hi - lo, *part(T.uq2, T.up2, i), T.zq[:, lo:hi], T.zp[:, lo:hi], uk + r)
-
-        def lowered(lo, hi, key):
-            tt(T.xs[:, lo:hi], bank(6, 0, hi - lo), T.pen[:, lo:hi], Op.add,
-               ["P6"] + ["pen%d" % k for k in range(lo // 128, hi // 128)], ["xs" + key])
-
-        def ahead(lo, hi, key):
-            tt(T.cm[:, 4 * lo + 3:4 * hi:4], bank(7, 0, hi - lo), T.xs[:, lo:hi], Op.is_gt, ["P7", "xs" + key], ["cma" + key])
-
-        def layer(b):
-            mm(b, C, *part(T.wq, T.wp, b), T.zq[:], T.zp[:], ["w"] + zk, False, True)
-
-        def beats(k, lo, hi, slot, o, key):
-            ts(T.cm[:, 4 * lo + slot:4 * hi:4], bank(5, lo, hi), T.sc[:, k:k + 1], None, o, None, ["P5", "sc%d" % k], [key])
-
-        def beats_near(lo, hi, thr, key):
-            tt(T.cm[:, 4 * lo + 2:4 * hi:4], bank(5, lo, hi), T.thr[:, lo:hi], Op.is_lt, ["P5"] + thr, ["cmd" + key])
-
-        def count_part(lo, hi, b, keys, key):
-            quant(T.cmq[:, lo:hi], T.cmp[:, lo:hi], T.cm[:, 4 * lo:4 * hi], keys + ["cmd" + key, "cma" + key], ["cmq" + key])
-            mm(b, hi - lo, *part(T.kq, T.ks, 0), T.cmq[:, lo:hi], T.cmp[:, lo:hi], ["kq", "cmq" + key])
-
+            for b in range(4):
+                arrived(b, "vssv"[b])
+            turned(0)
         gather_z("v", 0, 128, "za")
         gather_z("s", 128, 256, "zb")
-        gather_z("s", 256 if first else 296, C, "zd")
+        gather_z("s", CUT, C, "zd")
+        if not first:
+            turned(1)
+        gather_z("v", 256, CUT, "zc")
         if first:
-            penalty(1, 2)
+            turned(0)
         quant_z(0, ["za"])
-        along_partitions(0, 5)
+        along_partitions(0)
+        turned(1 if first else 2)
         quant_z(1, ["zb"])
-        pair(1, 0, 256, zk[:2])
-        along_partitions(1, 4)
-        pair(2, 0, 256, zk[:2])
+        along_partitions(1)
         if first:
-            backward(d, dk, 0, (LS, 0))
-        else:
-            gather_z("v", 256, 296, "zc")
-        score(0, 5)
-        step_up(0, 5)
-        score(1, 4)
-        step_up(1, 4)
+            turned(2)
         quant_z(2, ["zc", "zd"])
-        mm(5, C, *part(T.uq2, T.up2, 0), T.zq[:], T.zp[:], uk + zk)
-        along_partitions(2, 4)
-        threshold(0)
-        threshold(1)
-        score(2, 4)
-        step_up(2, 4)
-        if first:
-            act(T.back[:, 0:C], T.bw[:, 8:LS + 7].indirect(T.pu[:]), Fn.Copy, ["bw0", "pu"], ["back"], scale=-1 / EPS)
-        layer(0)
-        copy_x(0)
-        threshold(2)
-        lowered(0, 256, "A")
-        if first:
-            penalty(2, 3)
-        else:
-            take_back()
-        ahead(0, 256, "A")
-        pair(2, 256, C, zk[2:])
-        pair(1, 256, C, zk[2:])
-        layer(1)
-        layer(2)
-        if last:
-            layer(3)
-        beats(1, 0, 128, 0, Op.is_lt, "cm2")
-        beats(0, 128, C, 0, Op.is_le, "cm1")
-        beats_near(0, 256, ["thr0", "thr1"], "A")
-        beats(2, 0, 256, 1, Op.is_lt, "cm0")
-        lowered(256, C, "B")
-        count_part(0, 256, 4, ["cm0", "cm1", "cm2"], "A")
-        if not last:
-            layer(3)
-        ahead(256, C, "B")
-        beats(1, 256, C, 1, Op.is_le, "cm4")
-        beats_near(256, C, ["thr2"], "B")
-        if first:
-            name_tile(0)
-        count_part(256, C, 6, ["cm1", "cm4"], "B")
-        for b in (1, 2):
-            copy_x(b)
-        if first:
-            hold(T.ext[:], T.back[:, 0:C], C, ["back"], "ext")
-        elif last:
-            copy_x(3)
-        else:
-            copy_x(3, "v", 0, 256)
-        act(T.win[:, 16:16 + 256], bank(4, 0, 256), Fn.Relu, ["P4", "thv"], ["winA"], bias=col("thv"), scale=-1.0)
-        act(T.kt[:, 1:512:2], bank(4, 0, 256), Fn.Relu, ["P4", "thv"], ["ktA"], bias=col("thv"), scale=-1.0)
-        if not first and not last:
-            copy_x(3, "s", 256, C)
-
-        def last_codes(h, lo, hi):
-            quant(T.xq[:, lo:hi], T.xp[:, lo:hi], T.xb[:, 4 * (XO + lo):4 * (XO + hi)], xall, ["xq%d" % h] + ["xq"] * (1 - h))
-            mm(h, hi - lo, T.vq[:], T.vp[:], T.xq[:, lo:hi], T.xp[:, lo:hi], ["vq", "xq%d" % h])
-            dma([("y", T.oc[:, 4 * lo:4 * hi], T.xq[:, lo:hi].bitcast(dt.uint8))], ["xq%d" % h], [])
-
-        def last_product(q, h, lo, hi):
-            move(q, T.yb[:, lo:hi], bank(h, 0, hi - lo), ["P%d" % h], ["yb%d" % h])
-            dma([("y", T.y[:, lo:hi], T.yb[:, lo:hi])], ["yb%d" % h], [])
-
-        if last:
-            last_codes(0, 0, 256)
-        ts(T.win[:, 16 + 256:16 + C], bank(6, 0, 128), col("thv"), None, Op.is_lt, None, ["P6", "thv"], ["winB"])
-        if first:
-            ts(T.bu[:], T.ext[:, 15:C:16], col("offb"), None, Op.subtract, None, ["ext", "offb"], ["bu"])
-        ts(T.kt[:, 513:2 * C:2], bank(6, 0, 128), col("thv"), None, Op.is_lt, None, ["P6", "thv"], ["ktB"])
-        for q, lo, hi, key in (("s", 192, C, "kt1"), ("v", 0, 192, "kt0")):
-            move(q, T.kt[:, 2 * lo:2 * hi:2], T.win[:].indirect(T.bu[:, lo // 16:hi // 16]), ["winz", "winA", "winB", "bu"], [key])
-        if last:
-            last_codes(1, 256, C)
-            last_product("s", 0, 0, 256)
-        if first:
-            copy_x(3)
-            name_tile(1)
-        quant(T.ktq[:], T.ktp[:], T.kt[:], ["kt0", "kt1", "ktA", "ktB"], ["ktq"])
-        for h in range(2):
-            mm(6 + h, C // 2, *part(T.kq, T.ks, 1 + h), T.ktq[:], T.ktp[:], ["kq%d" % h, "ktq"])
+        along_partitions(2)
+        mm(7, C, *part(T.uq2, T.up2, 1), T.zq[:], T.zp[:], uk + zk)
+        for b in (3, 1, 0, 2):
+            layer(b)
+        turned(3)
+        for k in range(3):
+            scores(k)
+            if first and k == 0:
+                quant(*part(T.kq, T.ks, 0), T.wts[:, 0:512], ["w0a", "w0b", "w00", "w06", "w08"], ["kq0"])
         if first:
             cp(T.lu[:], T.lw[:], ["lw"], ["lu"])
+        for step, k in ((far, 0), (size, 1), (far, 1), (size, 0), (near, 1), (size, 2), (near, 0), (near, 2)):
+            step(k)
+        copy_x(3, "s", C // 2, C)
+        scan(T.run[:, 1:TRIO + 1], T.anew[:], T.av[:, 0:TRIO], Op.max, Op.min, av_all + ["anew"], ["run"], BIG)
+        beats("far0", 128, C, C, 0, 0, "cm0")
+        tt(T.old[:], T.av[:, 0:TRIO], T.run[:, 0:TRIO], Op.is_ge, av_all + ["run", "runz"], ["old"])
+        beats("near1", 128, 256, 128, 0, 1, "cm4")
+        beats("far1", 256, C, C + 256, 128, 1, "cm2")
+        beats("near0", 0, 128, 0, 0, 2, "cm1")
+        tt(T.pick[:], T.old[:], T.sc[:, 0:TRIO], Op.subtract, ["old", "sc"], ["pick"])
+        beats("near2", 256, C, 256, 128, 2, "cm3")
+        beaten(1, 128, 128, 1, 255.5 - M, "cm2")
+        beaten(0, 0, 256, 0, 127.5 - M, "cm0")
+        count_down(0, ["cm0", "cm1", "cm4"])
+        scan(T.best[:], T.pick[:], T.pick[:], Op.mult, Op.min, ["pick"], ["best"])
+        count_down(1, ["cm0", "cm2", "cm3"])
+        for b in (1, 0, 2):
+            copy_x(b)
+        copy_x(3, "v", 0, C // 2)
+        contested(0, 4, 1, T.rs[:, 0:1], ["rs0"])
+        ts(T.named[:, 0:3], T.best[:, 7:TRIO:16], -1 / EPS, -OWN - C / 2, Op.mult, Op.add, ["best"], ["named"])
+        contested(1, 4, 0, T.rs[:, 1:2], ["rs1"])
+        contested(2, 5, 2, C - 0.5 - M, [])
+        spared(0)
+        for k in (0, 2, 1):
+            names_of(k)
+        spared(2)
         if last:
-            last_product("v", 1, 256, C)
+            last_codes(0, 0, 256)
+        spared(1)
+        if first:
+            zero_columns(1)
+            zero_columns(2)
+        for h in range(3):
+            quant(*part(T.ktq, T.ktp, h), T.kt[:, 512 * h:512 * h + 512], ["kt0", "kt1", "kt2", "kd%d" % h], ["ktq%d" % h])
+            mm(5 + h, 128, *part(T.kq, T.ks, 1), *part(T.ktq, T.ktp, h), ["kq1", "ktq%d" % h])
+            if last and h == 1:
+                last_codes(1, 256, C)
+        if last:
+            last_product("s", 0, 0, 256)
             dma([("s", T.osc[4 * k:4 * k + 4, :], T.xp[32 * k:32 * k + 4, :]) for k in range(4)], ["xq0", "xq1"], [])
         else:
             quant_x()
             unpack_own(True)
-        for h, key in enumerate(("deadA", "deadB")):
-            was = T.dead[:, OWN + h:W:2]
+        for h, key in enumerate(sg_all[1:]):
+            lo, hi = 128 * h, 128 * h + 128
             if last:
-                tt(T.life[:, h:C:2], bank(6 + h, 0, C // 2), was, Op.is_ge, ["P%d" % (6 + h), key], ["life%d" % h, "life"][:2 - h])
+                tt(T.life[:, lo:hi], bank(5 + h, 0, 128), T.was[:, lo:hi], Op.is_ge, ["P%d" % (5 + h), "was"], ["life%d" % h])
+                if h == 1:
+                    last_product("v", 1, 256, C)
             else:
-                tt(was, bank(6 + h, 0, C // 2), was, Op.is_lt, ["P%d" % (6 + h), key], [key])
-    dma([("y", T.ol[:], T.life[0:1, :])], ["life0", "life1"], [])
+                act(T.sg[:, OWN + lo:OWN + hi], bank(5 + h, 0, 128), Fn.Sign, ["P%d" % (5 + h)], [key], bias=-0.5, scale=-1.0)
+    dma([("y", T.ol[:], T.life[0:1, :])], ["life0", "life1", "life2"], [])
     for sem in count:
         need("g", (sem, count[sem], {}))

from concourse.bass import DstId, RemoteDMATransfer
from concourse.mybir import dt, AluOpType, ActivationFunctionType

H, A, C, M, R = 6, 64, 384, 32, 3
WAY = [(-1, -1), (-1, 0), (-1, 1), (0, -1), (0, 1), (1, -1), (1, 0), (1, 1)]
UP, DOWN, GAP, OWN, W = 16, 88, 152, 160, 544
LAND = GAP - UP
XO = 4
LL, LS = 496, 484
SENT = 7 * A
CUT = 280
TRIO = 40
K, BIG, EPS = 2048.0, 1e29, 2.0 ** -36
X4, U8 = "float8_e4m3fn_x4", "uint8"


def _sb(n, d):
    return ("sbuf", [128, n], d)


SCRATCH = {
    "ps": ("psum", [128, 4096], "float32"),
    "cnt": _sb(W, "float32"), "pint": _sb(8, "int32"), "pf": _sb(16, "float32"), "ones": _sb(W // 2, "bfloat16"),
    "two": _sb(8, "float32"), "tmp": _sb(72, "float32"), "mm": _sb(256, "float32"), "turn": _sb(160, "float32"),
    "turnu": _sb(32, "uint16"), "posi": _sb(48, "float32"), "posu": _sb(24, "uint16"), "posf": _sb(C, "float32"),
    "strip": _sb(528, "bfloat16"), "wts": _sb(1024, "bfloat16"), "cells": _sb(C, "bfloat16"),
    "eq": _sb(512, X4), "es": _sb(512, U8), "kq": _sb(256, X4), "ks": _sb(256, U8),
    "lin": _sb(48, "int32"), "seatu": _sb(24, "uint16"), "aliveu": _sb(24, "uint16"), "jw": _sb(24, "float32"),
    "ni": _sb(C, "float32"), "nis": _sb(C, "float32"),
    "d0": _sb(512, "float32"), "d1": _sb(LL, "float32"), "idl": _sb(512, "float32"), "lw": _sb(32, "float32"),
    "ext": _sb(C, "float32"), "ex4": _sb(C, "float32"), "lu": _sb(32, "uint16"), "pc": _sb(C, "float32"), "pu": _sb(24, "uint16"),
    "sg": _sb(W, "float32"), "was": _sb(C, "float32"), "life": _sb(C, "float32"),
    "fw": _sb(512, "float32"), "c64": _sb(64, "float32"), "cu": _sb(16, "uint16"),
    "sees": ("sbuf", [128, 3, 128], "float32"), "su": _sb(96, "uint16"), "rows": _sb(96, "float32"), "st": _sb(96, "float32"),
    "pen": _sb(48, "float32"), "av": _sb(48, "float32"), "run": _sb(48, "float32"), "anew": _sb(TRIO, "float32"),
    "sc": _sb(48, "float32"), "close": _sb(4, "uint16"),
    "old": _sb(TRIO, "float32"), "pick": _sb(TRIO, "float32"), "best": _sb(TRIO, "float32"),
    "lives": _sb(4, "float32"), "dl": _sb(4, "float32"), "rs": _sb(4, "float32"), "named": _sb(4, "bfloat16"),
    "wins": _sb(4, "bfloat16"), "step": _sb(C, "bfloat16"), "thr": _sb(2 * C, "float32"), "sums": _sb(C, "float32"),
    "xb": _sb(4 * (XO + C), "bfloat16"), "xq": _sb(C, X4), "xp": _sb(C, U8), "tp": _sb(4 * W, "bfloat16"),
    "comp": _sb(512, "bfloat16"), "z": _sb(4 * C, "bfloat16"), "zq": _sb(C, X4), "zp": _sb(C, U8),
    "cm": _sb(1024, "bfloat16"), "cmq": _sb(256, X4), "cmp": _sb(256, U8),
    "kt": _sb(4 * C, "bfloat16"), "ktq": _sb(C, X4), "ktp": _sb(C, U8),
    "ub": _sb(512, "bfloat16"), "uq": _sb(128, X4), "up": _sb(128, U8), "uu": _sb(8, "uint16"),
    "uq2": _sb(256, X4), "up2": _sb(256, U8), "vb": _sb(512, "bfloat16"), "vq": _sb(128, X4), "vp": _sb(128, U8),
    "wq": _sb(512, X4), "wp": _sb(512, U8), "yb": _sb(C, "float32"),
}
for _t in range(R):
    SCRATCH["sq%d" % _t] = _sb(128, X4)
    SCRATCH["sp%d" % _t] = _sb(128, U8)
    SCRATCH["lq%d" % _t] = _sb(LAND, X4)
    SCRATCH["lp%d" % _t] = _sb(LAND, U8)

SEMAPHORES = ["v", "s", "t", "g", "sent", "arr0", "arr1", "arr2"] + ["d%d" % i for i in range(32)]

Op, Fn = AluOpType, ActivationFunctionType


def rank_program(g, core, T, topo):
    rank = T.rank_of(core)
    if rank is None:
        return
    n = len(T.cores)
    above, below = T.cores[(rank - 1) % n], T.cores[(rank + 1) % n]
    V, S, PE = g.vector, g.scalar, g.tensor
    queue = {"v": V, "s": S, "t": PE, "g": g, "y": g.sync}
    count = {}
    known = {q: {} for q in queue}
    writer, readers = {}, {}

    def need(q, tok):
        sem, val, seen = tok[0], tok[1], tok[2]
        if known[q].get(sem, 0) >= val:
            return
        queue[q].wait_ge(T.sem[sem], val)
        known[q][sem] = val
        for k in seen:
            known[q][k] = max(known[q].get(k, 0), seen[k])

    def order(q, r, w, add):
        toks = []
        for k in r:
            toks += writer.get(k, [])
            if k[0] == "P":
                toks += [t for t in readers.get(k, []) if t[3] != q]
        for k in w:
            if k not in add:
                toks += writer.get(k, [])
            toks += readers.get(k, [])
        for tok in sorted(toks, key=lambda t: -t[1]):
            need(q, tok)

    def note(tok, r, w):
        for k in r:
            readers.setdefault(k, []).append(tok)
        for k in w:
            writer[k] = [tok]
            readers[k] = []

    def op(q, call, r, w, add=()):
        order(q, r, w, add)
        count[q] = count.get(q, 0) + 1
        call().then_inc(T.sem[q], 1)
        note((q, count[q], dict(known[q]), q), r, w)

    def dma(parts, r, w):
        sem = "d%d" % len([k for k in count if k[0] == "d"])
        for q, out, src in parts:
            order(q, r, w, ())
        for q, out, src in parts:
            queue[q].dma_start(out, src).then_inc(T.sem[sem], 16)
        count[sem] = 16 * len(parts)
        note((sem, count[sem], dict(known[parts[0][0]]), "dma"), r, w)

    def ts(out, a, s1, s2, o1, o2, r, w):
        if o2 is None:
            op("v", lambda: V.tensor_scalar(out, a, s1, None, o1), r, w)
        else:
            op("v", lambda: V.tensor_scalar(out, a, s1, s2, o1, o2), r, w)

    def tt(out, a, b, o, r, w):
        op("v", lambda: V.tensor_tensor(out, a, b, o), r, w)

    def cp(out, a, r, w):
        op("v", lambda: V.tensor_copy(out, a), r, w)

    def fill(out, c, w):
        op("v", lambda: V.memset(out, c), [], w)

    def scan(out, a, b, o0, o1, r, w, start=0.0):
        op("v", lambda: V.tensor_tensor_scan(out, a, b, start, o0, o1), r, w)

    def quant(q, p, a, r, w):
        op("v", lambda: V.quantize_mx(q, p, a), r, w)

    def act(out, a, f, r, w, bias=None, scale=None, total=None):
        more = {k: x for k, x in (("bias", bias), ("scale", scale), ("accum_out", total)) if x is not None}
        op("s", lambda: S.activation(out, a, f, **more), r, w)

    def level(out, cols, value, w):
        act(out, T.ones[:, 0:cols], Fn.Copy, ["ones"], w, scale=value)

    def move(q, out, a, r, w):
        if q == "v":
            cp(out, a, r, w)
        else:
            act(out, a, Fn.Copy, r, w)

    def times(q, out, a, c, r, w):
        if q == "v":
            ts(out, a, c, None, Op.mult, None, r, w)
        else:
            act(out, a, Fn.Copy, r, w, scale=c)

    def iota(out, pattern, base, cm, r, w):
        op("g", lambda: g.iota(out, pattern, base, cm, allow_small_or_imprecise_dtypes=True), r, w)

    def whole(out, cols, value, w):
        iota(out, [[0, cols]], value, 0, [], w)

    def bank(b, lo, hi, step=1):
        return T.ps[:, 512 * b + lo:512 * b + hi:step]

    def mm(b, cols, lq, lp, rq, rp, r, start=True, stop=True):
        k = "P%d" % b
        op("t", lambda: PE.matmul_mx(bank(b, 0, cols), lq, lp, rq, rp, start, stop), r, [k], add=() if start else (k,))

    def part(q, p, b):
        return q[:, 128 * b:128 * b + 128], p[:, 128 * b:128 * b + 128]

    names = ["p", "q16", "q12", "q3", "offk", "c4a", "c4b", "c4s", "c4c", "q256"]

    def col(name):
        i = names.index(name)
        return T.pf[:, i:i + 1]

    def small(name, src, bias, scale):
        r = [k if k not in names[:4] else "pf" for k in (src, bias) if isinstance(k, str)]
        act(col(name), col(src), Fn.Identity, r, [name], bias=col(bias) if isinstance(bias, str) else bias, scale=scale)

    u32 = dt.uint32
    xall = ["x0", "x1", "x2", "x3", "x4"]
    X = T.xb[:, 4 * XO:4 * (XO + C)]
    diagonal = T.strip[:, 3:515:4]

    def quant_x():
        quant(T.xq[:], T.xp[:], X, xall, ["xq"])

    def unpacker(b):
        quant(*part(T.eq, T.es, b), T.strip[:, 3 - b:515 - b], ["strip"], ["e%d" % b])

    def unpack_own(stop, banks=range(4)):
        for b in banks:
            mm(b, C, *part(T.eq, T.es, b), T.xq[:], T.xp[:], ["e%d" % b, "xq"], True, stop)

    def copy_t(b):
        times("s", T.tp[:, 4 * OWN + b:4 * W:4], bank(b, 0, C), 0.015625, ["P%d" % b], ["to%d" % b])

    def copy_x(b, q="s", lo=0, hi=C):
        times(q, T.xb[:, 4 * (XO + lo) + b:4 * (XO + hi):4], bank(b, lo, hi), 0.015625, ["P%d" % b], ["x4" if lo else "x%d" % b])

    dma([("y" if i < 5 else "s", T.lin[16 * i:16 * i + 16, 24:48], T.alive[:]) for i in range(8)], [], ["alive"])
    dma([("s", T.lin[:, 0:24], T.seat[:])], [], ["seat"])
    dma([("y", X, T.x[:])], [], xall)
    dma([("y", T.ub[:], T.u[:])], [], ["ub"])
    dma([("y", T.wq[:].bitcast(dt.uint8), T.wc[:]), ("y", T.wp[:], T.ws[:])], [], ["w"])
    dma([("y", T.vb[:], T.v[:])], [], ["vb"])

    op("g", lambda: g.iota(T.pint[:, 0:1], [[0, 1]], 0, 1), [], ["pi"])
    posi_all = ["posi0", "posi1", "posi2", "posi3"]
    for odd in (1, 0):
        for a in range(4):
            di, dj = WAY[2 * a + odd]
            if di == 0:
                al, be, ga = -dj, 65, (1 if dj < 0 else 64)
            else:
                al = -7 if dj > 0 else 7
                bi, ga = (1, 1) if dj == 0 else (-6, 36 + (7 * 63 if dj > 0 else 0))
                be, ga = (bi, ga) if di < 0 else (-bi, ga + 5 * bi)
            entry = -1000 if di == 0 else (UP if di < 0 else DOWN) - (6 if dj else 0)
            iota(T.posi[32 * a:32 * a + 16 + 16 * odd, :], [[entry, 2], [be, 6], [16 * al, 4]], ga - 16 * al * odd, al,
                 ["pi"], [posi_all[a]])
    iota(T.turn[:, 96:160], [[0, 16], [4, 4]], 0, 0, posi_all, ["four"])
    iota(T.turn[:, 32:96], [[0, 4], [1, 16]], 0, 0, [], ["sixteen"])
    whole(T.xb[:, 0:4 * XO], 4 * XO, 0, ["xz"])
    iota(T.turn[:, 0:32], [[256, 2], [1, 16]], 0, 0, [], ["turn"])
    whole(T.comp[:, 256:512], 256, 0, ["compz"])
    whole(T.fw[:, 0:1], 1, 0, ["fwz"])
    whole(T.rows[:], 96, 1, ["rows"])
    whole(T.tp[:, 0:4 * UP], 4 * UP, 0, ["tz"])
    whole(T.tp[:, 4 * GAP:4 * OWN], 4 * (OWN - GAP), 0, ["tg"])

    fill(T.ones[:], 1.0, ["ones"])
    fill(T.two[:, 0:1], -1 / EPS, ["two0"])
    fill(T.two[:, 1:2], BIG, ["two1"])
    fill(T.uu[:], 1, ["uu"])
    scan(T.cnt[:, 0:W // 2], T.ones[:], T.ones[:], Op.mult, Op.add, ["ones"], ["cnt0"], -1.0)
    for i, m in enumerate((15, 12, 3)):
        ts(T.pint[:, 1 + i:2 + i], T.pint[:, 0:1], m, None, Op.bitwise_and, None, ["pi"], ["pi%d" % i])
    act(T.cnt[:, W // 2:W], T.cnt[:, 0:W // 2], Fn.Identity, ["cnt0"], ["cnt1"], bias=float(W // 2))
    for h in range(2):
        level(T.strip[:, 264 * h:264 * h + 264], 264, 0.0, ["strip%d" % h])
    for h in range(2):
        level(T.d0[:, 256 * h:256 * h + 256], 256, -EPS, ["d0%d" % h])
    cp(T.pf[:, 0:4], T.pint[:, 0:4], ["pi", "pi0", "pi1", "pi2"], ["pf"])
    cp(T.aliveu[:], T.lin[:, 24:48], ["alive"], ["aliveu"])
    cp(T.seatu[:], T.lin[:, 0:24], ["seat"], ["seatu"])
    ts(T.close[:], T.cnt[:, 0:128:32], col("q16"), None, Op.add, None, ["cnt0", "pf"], ["close"])
    tt(T.ni[:], T.two[:, 0:2].indirect(T.aliveu[:]), T.cnt[:, OWN:W], Op.min, ["two0", "two1", "aliveu", "cnt0", "cnt1"], ["ni"])
    ts(diagonal, T.cnt[:, 0:128], col("p"), 64.0, Op.is_equal, Op.mult, ["cnt0", "pf", "strip0", "strip1"], ["strip"])
    ts(T.tmp[:, 0:69], T.cnt[:, 0:69], T.posi[:, 24:25], T.posi[:, 0:1], Op.add, Op.subtract, ["cnt0"] + posi_all, ["tmp0"])
    cp(T.posu[:], T.posi[:, 0:24], posi_all, ["posu"])
    small("c4a", "q3", 12 * K - 4.0 * (OWN - XO), 1.0)
    small("q256", "q16", 0.0, 16.0)
    for h, q in enumerate("sv"):
        times(q, T.nis[:, 192 * h:192 * h + 192], T.ni[:].indirect(T.seatu[:, 12 * h:12 * h + 12]), -EPS, ["ni", "seatu"], ["nis%d" % h])
    ts(T.d0[:, 0:483:7], T.tmp[:, 0:69], -EPS, -EPS, Op.mult, Op.min, ["tmp0", "d00", "d01"], ["d0"])
    ts(T.mm[:, 1:128:2], T.turn[:, 96:160], col("q12"), -BIG, Op.is_equal, Op.mult, ["four", "pf"], ["mm1"])
    ts(T.mm[:, 0:128:2], T.turn[:, 32:96], col("q16"), -BIG, Op.is_equal, Op.mult, ["sixteen", "pf"], ["mm0"])
    cp(T.d0[:].indirect(T.posu[:]), T.nis[:], ["nis0", "nis1", "posu"], ["d0"])
    small("c4c", "q12", "c4a", -K)
    act(T.posf[:], T.cnt[:].indirect(T.posu[:]), Fn.Copy, ["cnt0", "cnt1", "posu"], ["posf"])
    act(T.mm[:, 1:128:2], T.mm[:, 1:128:2], Fn.Identity, ["mm1"], ["mm1"], bias=K * EPS)
    act(T.mm[:, 0:128:2], T.mm[:, 0:128:2], Fn.Identity, ["mm0"], ["mm0"], bias=K)
    dma([("y", T.mm[:, 128:256], T.mm[:, 0:128])], ["mm0", "mm1"], ["mm2"])
    small("c4b", "q3", -12 * K, 1.0)
    small("offk", "q16", 15 * K, -K)
    small("c4s", "q12", "c4b", K)
    for b in range(4):
        level(T.wts[:, 512 + b:1024:4], 128, 1.0 if b == 3 else -1.0, ["w1%d" % b])
    level(T.wts[:, 0:16], 16, 0.0, ["w0a"])
    level(T.av[:], 48, BIG, ["av0", "av1", "av2"])
    level(T.anew[:], TRIO, -BIG, ["anew"])
    level(T.run[:, 0:1], 1, BIG, ["runz"])
    level(T.anew[:, 15:TRIO:16], 2, BIG, ["anew"])
    for lo, hi in ((0, 2), (6, 7), (8, 11)):
        level(T.wts[:, lo:hi], hi - lo, 1.0, ["w0%d" % lo] + ["w0a"] * (lo == 0))
    unpacker(0)
    sg_all = ["sg0", "sgA", "sgB", "sgC"]
    sees_all = ["sees0", "sees1", "sees2"]

    def later_constants():
        op("g", lambda: g.affine_select(T.step[:, 0:128], T.comp[:, 256:384], [[1, 128]], Op.is_ge, -1.25 * 2.0 ** -25, 0, -1),
           ["compz"], ["tri"])
        whole(T.wts[:, 16:512], 496, 0, ["w0b"])
        whole(T.cm[:, 3:1024:4], 256, 0, ["cmz"])
        iota(T.cells[:], [[1, C]], -C // 2, 0, [], ["cells"])
        whole(T.sg[:, 0:OWN], OWN, -1, ["sg0"])

    def arrived(b, q):
        times(q, T.tp[:, 4 * UP + b:4 * GAP:4], bank(4 + b, 0, LAND), 0.015625, ["P%d" % (4 + b)], ["ta%d" % b])

    t_all = ["tz", "tg"] + ["ta%d" % b for b in range(4)] + ["to%d" % b for b in range(4)]

    def gather_z(q, lo, hi, key):
        move(q, T.z[:, 4 * lo:4 * hi], T.tp[:].indirect(T.su[:, lo // 4:hi // 4]), t_all + ["su"], [key])

    def hold(k):
        scan(T.ext[:, 128 * k:128 * k + 128], T.mm[:, 0:256:2], T.pc[:, 128 * k:128 * k + 128], Op.add, Op.max,
             ["pc", "mm0", "mm2"], ["ext%d" % k])

    def hold4(k):
        scan(T.ex4[:, 128 * k:128 * k + 128], T.mm[:, 1:256:2], T.sees[:, k, :], Op.add, Op.max, [sees_all[k], "mm1", "mm2"], ["ex%d" % k])

    def offsets_z():
        ts(T.su[:], T.ex4[:, 3:C:4], 4 / EPS, col("c4s"), Op.mult, Op.add, ["ex0", "ex1", "ex2", "c4s"], ["su"])

    def look(k, q):
        src = T.fw[:, 0:LS + 1].indirect(T.pu[:, 8 * k:8 * k + 8])
        if q:
            times(q, T.sees[:, k, :], src, -1.0, ["fw", "fwz", "pu"], [sees_all[k]])
        else:
            tt(T.sees[:, k, :], src, T.sg[:, OWN + 128 * k:OWN + 128 * k + 128], Op.mult, ["fw", "fw2", "fwz", "pu"] + sg_all, [sees_all[k]])

    def turn_sees():
        dma([("ys"[a % 2], T.rows[32 * a:32 * a + 8, :], T.sees[0:128:16, :, 32 * a:32 * a + 32]) for a in range(4)], sees_all, ["rows"])

    def turned(i):
        if i == 0:
            op("v", lambda: V.transpose(T.st[:], T.rows[:]), ["rows"], ["st"])
        elif i == 1:
            ts(T.pen[:], T.st[:].indirect(T.close[:, 0:3]), (OWN - 0.5) * EPS, BIG, Op.is_lt, Op.mult, ["st", "close"], ["pen"])
        elif i == 2:
            ts(T.pen[:, 8:48:16], T.st[:, 0:96:32], 0.0, -BIG, Op.is_le, Op.mult, ["st", "pen"], ["pen"])
        else:
            act(T.lives[:, 0:3], T.st[:, 0:96:32], Fn.Sign, ["st"], ["lives"])
            act(T.sc[:], T.st[:].indirect(T.close[:, 0:3]), Fn.Copy, ["st", "close"], ["sc"])

    def harmless(k):
        ts(T.step[:, 128 * k:128 * k + 128], T.sees[:, k, :], 0.0, None, Op.is_le, None, [sees_all[k]], ["dead%d" % k])

    def slots(lo, hi, key):
        tt(T.d1[:, lo:hi], T.sg[:].indirect(T.lu[:, lo // 16:hi // 16]), T.d0[:, lo:hi], Op.max, sg_all + ["lu", "d0"], [key])

    def zero_columns(i):
        dma([("y", T["lq%d" % i][:, 64:DOWN - UP].bitcast(dt.uint8), T.sq0[:, 64:DOWN - UP].bitcast(dt.uint8)),
             ("y", T["lp%d" % i][:, 64:DOWN - UP], T.sp0[:, 64:DOWN - UP])], ["sq0"], ["landz%d" % i])

    uk = ["u2a", "u2b", "u2c"]
    zk = ["zq0", "zq1", "zq2"]
    av_all = ["av0", "av1", "av2"]

    def quant_z(k, r):
        quant(*part(T.zq, T.zp, k), T.z[:, 512 * k:512 * k + 512], r, [zk[k]])

    def along_partitions(k):
        mm(4 + k, 130, *part(T.zq, T.zp, k), T.uq2[:, 0:130], T.up2[:, 0:130], uk + [zk[k]])

    def scores(k):
        tt(T.av[:, 16 * k:16 * k + 9], bank(4 + k, 0, 129, 16), T.pen[:, 16 * k:16 * k + 9], Op.add, ["P%d" % (4 + k), "pen"], [av_all[k]])

    def size(k):
        act(T.dl[:, k:k + 1], T.av[:, 16 * k + 8:16 * k + 9], Fn.Abs, [av_all[k]], ["dl%d" % k], bias=2.0 ** -100, scale=2.0)

    def near(k):
        act(T.thr[:, 128 * k:128 * k + 128], T.step[:, 0:128], Fn.Identity, ["tri", av_all[k], "dl%d" % k], ["near%d" % k],
            bias=T.av[:, 16 * k + 8:16 * k + 9], scale=T.dl[:, k:k + 1])

    def far(k):
        act(T.thr[:, C + 256 * k:C + 256 + 128 * k], T.step[:, 128 * k + 128:C], Fn.Identity, ["dead1", "dead2"][k:] + [av_all[k]],
            ["far%d" % k], bias=T.av[:, 16 * k + 8:16 * k + 9], scale=2 * BIG)

    def beats(r, lo, hi, at, to, slot, key):
        tt(T.cm[:, 4 * to + slot:4 * (to + hi - lo):4], bank(7, lo, hi), T.thr[:, at:at + hi - lo], Op.is_gt, ["P7", r], [key])

    def beaten(k, to, cols, slot, least, key):
        act(T.sums[:, 128 * (1 - k):128 * (1 - k) + cols], T.cm[:, 4 * to + slot:4 * (to + cols):4], Fn.Identity, [key], ["rs%d" % k],
            bias=least / cols, total=T.rs[:, k:k + 1])

    def count_down(h, r):
        quant(*part(T.cmq, T.cmp, h), T.cm[:, 512 * h:512 * h + 512], r + ["cmz"], ["cmq%d" % h])
        mm(4 + h, 128, *part(T.cmq, T.cmp, h), *part(T.kq, T.ks, 0), ["kq0", "cmq%d" % h])

    def layer(b):
        mm(b, C, *part(T.wq, T.wp, b), T.zq[:], T.zp[:], ["w"] + zk, False, True)

    def contested(k, b, at, least, r):
        ts(T.wins[:, k:k + 1], bank(b, at, at + 1), least, T.lives[:, k:k + 1], Op.is_gt, Op.min, ["P%d" % b, "lives"] + r, ["wins%d" % k])

    def names_of(k):
        ts(T.kt[:, k:4 * C:4], T.cells[:], T.named[:, k:k + 1], T.wins[:, k:k + 1], Op.is_equal, Op.mult,
           ["cells", "named", "wins%d" % k], ["kt%d" % k])

    def spared(k):
        ts(T.kt[:, 512 * k + 3:512 * k + 512:4], diagonal, T.wins[:, k:k + 1], None, Op.mult, None, ["strip", "wins%d" % k], ["kd%d" % k])

    def last_codes(h, lo, hi):
        quant(T.xq[:, lo:hi], T.xp[:, lo:hi], T.xb[:, 4 * (XO + lo):4 * (XO + hi)], xall, ["xq%d" % h] + ["xq"] * (1 - h))
        mm(h, hi - lo, T.vq[:], T.vp[:], T.xq[:, lo:hi], T.xp[:, lo:hi], ["vq", "xq%d" % h])
        dma([("y", T.oc[:, 4 * lo:4 * hi], T.xq[:, lo:hi].bitcast(dt.uint8))], ["xq%d" % h], [])

    def last_product(q, h, lo, hi):
        move(q, T.yb[:, lo:hi], bank(h, 0, hi - lo), ["P%d" % h], ["yb%d" % h])
        dma([("y", T.y[:, lo:hi], T.yb[:, lo:hi])], ["yb%d" % h], [])

    for t in range(R):
        first, last = t == 0, t == R - 1
        d, dk = (T.d0, ["d0"]) if first else (T.d1, ["d1", "d2"])
        if not first:
            slots(0, SENT, dk[0])
            slots(SENT, LL, dk[1])
            if last:
                act(T.was[:], T.ni[:], Fn.Relu, ["ni"], ["was"], scale=-EPS)
            copy_t(0)
            copy_t(1)

        def between(i):
            if first and i < 3:
                unpacker(i + 1)
                if i == 1:
                    ts(T.turnu[:], T.turn[:, 0:32], col("q256"), None, Op.add, None, ["turn", "q256"], ["turnu"])
            elif first:
                quant_x()
            elif i == 0 and t == 1:
                quant(T.vq[:], T.vp[:], T.vb[:], ["vb"], ["vq"])
            elif i == 1:
                scan(T.fw[:, SENT + 1:LS + 1], d[:, SENT:LS], d[:, SENT:LS], Op.mult, Op.min, [dk[1], "fw"], ["fw2"], T.fw[:, SENT:SENT + 1])
            elif i > 1:
                look(i - 2, None)

        now = LS if first else SENT
        scan(T.fw[:, 1:now + 1], d[:, 0:now], d[:, 0:now], Op.mult, Op.min, dk[:1], ["fw"])
        between(0)
        scan(T.c64[:], T.mm[:, 1:128:2], T.fw[:, 7:455:7], Op.add, Op.max, ["fw", "mm1"], ["c64"])
        between(1)
        ts(T.cu[:], T.c64[:, 3:64:4], -4 / EPS, col("c4c"), Op.mult, Op.add, ["c64", "c4c"], ["cu"])
        between(2)
        for h, q in enumerate("vs"):
            move(q, T.comp[:, 128 * h:128 * h + 128], T.xb[:].indirect(T.cu[:, 8 * h:8 * h + 8]), ["cu", "xz"] + xall,
                 ["comp%d" % h])
        between(3)
        sq, sp, lq, lp = T["sq%d" % t], T["sp%d" % t], T["lq%d" % t], T["lp%d" % t]
        quant(sq[:], sp[:], T.comp[:], ["comp0", "comp1", "compz"], ["sq%d" % t])
        order("g", ["sq%d" % t], [], ())
        for src, dst, codes in ((sq, lq, True), (sp, lp, False)):
            moves = []
            for i, to in enumerate((below, above)):
                half = topo.engines(core, to)[i::2]
                rid, pid = topo.addr(to)[:2]
                a, b = src[:, 0:64], dst[:, (DOWN - UP) * i:(DOWN - UP) * i + 64]
                if codes:
                    a, b = a.bitcast(dt.uint8), b.bitcast(dt.uint8)
                moves.append(RemoteDMATransfer(dst_ids=[DstId(rid=rid, pnc=pid)], dma_engine_mask=sum(1 << e for e in half),
                                               remote_sem=T.sem["arr%d" % t], src=a, dst=b))
                count["sent"] = count.get("sent", 0) + len(half)
            g.remote_dma_fused(moves, local_sem=T.sem.sent)
        landed = len(topo.engines(above, core)) + len(topo.engines(below, core))
        writer["land"] = [("arr%d" % t, landed, {}, "far")]
        readers["land"] = []

        def unpack_arrived():
            for b in range(4):
                mm(4 + b, LAND, *part(T.eq, T.es, b), lq[:], lp[:], ["e%d" % b, "land", "landz%d" % t])

        if first:
            zero_columns(0)
            later_constants()
            cp(T.pc[:].indirect(T.seatu[:]), T.posf[:], ["posf", "seatu"], ["pc"])
            unpack_own(True)
            act(T.idl[:], T.d0[:].indirect(T.turnu[:]), Fn.Relu, ["d0", "turnu"], ["idl"], scale=-1 / EPS)
            dma([("y", T.lw[:, 16 * b:16 * b + 16], T.idl[0:128:16, 256 * b:256 * b + 256]) for b in range(2)], ["idl"], ["lw"])
            for b in range(4):
                copy_t(b)
            quant(T.uq[:], T.up[:], T.ub[:], ["ub"], ["uq"])
            dma([("y", T.uq2[:, 0:128].bitcast(dt.uint8), T.uq[:].bitcast(dt.uint8)), ("y", T.up2[:, 0:128], T.up[:])], ["uq"], ["u2c"])
            for k in range(3):
                hold(k)
            act(T.up2[:, 128:256], T.up[:].indirect(T.uu[:]), Fn.Copy, ["uq", "uu"], ["u2b"])
            tt(T.jw[:], T.ext[:, 15:C:16], T.lin[:, 24:48], Op.mult, ["ext0", "ext1", "ext2", "alive"], ["jw"])
            cp(T.uq2[:, 128:256].bitcast(u32), T.uq[:].bitcast(u32).indirect(T.uu[:]), ["uq", "uu"], ["u2a"])
            ts(T.pu[:], T.jw[:], col("offk"), None, Op.subtract, None, ["jw", "offk"], ["pu"])
            quant(*part(T.kq, T.ks, 1), T.wts[:, 512:1024], ["w10", "w11", "w12", "w13"], ["kq1"])
            unpack_own(False, (0, 1))
            unpack_arrived()
            unpack_own(False, (2, 3))
            for k in range(3):
                look(k, "vsv"[k])
            turn_sees()
            for k in range(3):
                hold4(k)
            harmless(2)
            for b in range(4):
                arrived(b, "sssv"[b])
            offsets_z()
            harmless(1)
        else:
            look(2, None)
            copy_t(2)
            turn_sees()
            copy_t(3)
            unpack_own(False)
            for k in range(3):
                hold4(k)
            harmless(1)
            harmless(2)
            offsets_z()
            unpack_arrived()
            for b in range(4):
                arrived(b, "vssv"[b])
            turned(0)
        gather_z("v", 0, 128, "za")
        gather_z("s", 128, 256, "zb")
        gather_z("s", CUT, C, "zd")
        if not first:
            turned(1)
        gather_z("v", 256, CUT, "zc")
        if first:
            turned(0)
        quant_z(0, ["za"])
        along_partitions(0)
        turned(1 if first else 2)
        quant_z(1, ["zb"])
        along_partitions(1)
        if first:
            turned(2)
        quant_z(2, ["zc", "zd"])
        along_partitions(2)
        mm(7, C, *part(T.uq2, T.up2, 1), T.zq[:], T.zp[:], uk + zk)
        for b in (3, 1, 0, 2):
            layer(b)
        turned(3)
        for k in range(3):
            scores(k)
            if first and k == 0:
                quant(*part(T.kq, T.ks, 0), T.wts[:, 0:512], ["w0a", "w0b", "w00", "w06", "w08"], ["kq0"])
        if first:
            cp(T.lu[:], T.lw[:], ["lw"], ["lu"])
        for step, k in ((far, 0), (size, 1), (far, 1), (size, 0), (near, 1), (size, 2), (near, 0), (near, 2)):
            step(k)
        copy_x(3, "s", C // 2, C)
        scan(T.run[:, 1:TRIO + 1], T.anew[:], T.av[:, 0:TRIO], Op.max, Op.min, av_all + ["anew"], ["run"], BIG)
        beats("far0", 128, C, C, 0, 0, "cm0")
        tt(T.old[:], T.av[:, 0:TRIO], T.run[:, 0:TRIO], Op.is_ge, av_all + ["run", "runz"], ["old"])
        beats("near1", 128, 256, 128, 0, 1, "cm4")
        beats("far1", 256, C, C + 256, 128, 1, "cm2")
        beats("near0", 0, 128, 0, 0, 2, "cm1")
        tt(T.pick[:], T.old[:], T.sc[:, 0:TRIO], Op.subtract, ["old", "sc"], ["pick"])
        beats("near2", 256, C, 256, 128, 2, "cm3")
        beaten(1, 128, 128, 1, 255.5 - M, "cm2")
        beaten(0, 0, 256, 0, 127.5 - M, "cm0")
        count_down(0, ["cm0", "cm1", "cm4"])
        scan(T.best[:], T.pick[:], T.pick[:], Op.mult, Op.min, ["pick"], ["best"])
        count_down(1, ["cm0", "cm2", "cm3"])
        for b in (1, 0, 2):
            copy_x(b)
        copy_x(3, "v", 0, C // 2)
        contested(0, 4, 1, T.rs[:, 0:1], ["rs0"])
        ts(T.named[:, 0:3], T.best[:, 7:TRIO:16], -1 / EPS, -OWN - C / 2, Op.mult, Op.add, ["best"], ["named"])
        contested(1, 4, 0, T.rs[:, 1:2], ["rs1"])
        contested(2, 5, 2, C - 0.5 - M, [])
        spared(0)
        for k in (0, 2, 1):
            names_of(k)
        spared(2)
        if last:
            last_codes(0, 0, 256)
        spared(1)
        if first:
            zero_columns(1)
            zero_columns(2)
        for h in range(3):
            quant(*part(T.ktq, T.ktp, h), T.kt[:, 512 * h:512 * h + 512], ["kt0", "kt1", "kt2", "kd%d" % h], ["ktq%d" % h])
            mm(5 + h, 128, *part(T.kq, T.ks, 1), *part(T.ktq, T.ktp, h), ["kq1", "ktq%d" % h])
            if last and h == 1:
                last_codes(1, 256, C)
        if last:
            last_product("s", 0, 0, 256)
            dma([("s", T.osc[4 * k:4 * k + 4, :], T.xp[32 * k:32 * k + 4, :]) for k in range(4)], ["xq0", "xq1"], [])
        else:
            quant_x()
            unpack_own(True)
        for h, key in enumerate(sg_all[1:]):
            lo, hi = 128 * h, 128 * h + 128
            if last:
                tt(T.life[:, lo:hi], bank(5 + h, 0, 128), T.was[:, lo:hi], Op.is_ge, ["P%d" % (5 + h), "was"], ["life%d" % h])
                if h == 1:
                    last_product("v", 1, 256, C)
            else:
                act(T.sg[:, OWN + lo:OWN + hi], bank(5 + h, 0, 128), Fn.Sign, ["P%d" % (5 + h)], [key], bias=-0.5, scale=-1.0)
    dma([("y", T.ol[:], T.life[0:1, :])], ["life0", "life1", "life2"], [])
    for sem in count:
        need("g", (sem, count[sem], {}))
